import numpy as np
import ml_dtypes


def mxq(x, axis, fmt="e4m3"):
    dtype, down = {"e4m3": (ml_dtypes.float8_e4m3fn, 7), "e5m2": (ml_dtypes.float8_e5m2, 14)}[fmt]
    v = np.moveaxis(np.asarray(x, np.float32).astype(ml_dtypes.bfloat16).astype(np.float64), axis, -1)
    blocks = v.reshape(v.shape[:-1] + (-1, 32))
    amax = np.abs(blocks).max(-1, keepdims=True)
    byte = np.maximum(np.where(amax > 0, np.frexp(amax)[1] - 1 + 127, 0) - down, 1)
    scale = np.exp2(byte - 127.0)
    codes = (blocks / scale).astype(np.float32).astype(dtype).astype(np.float64)
    return np.moveaxis((codes * scale).reshape(v.shape), -1, axis)


WIDE = False


def mx_kscale(k):
    if not WIDE:
        return np.ones(k)
    levels = np.array([10, -10, 5, -5, 0])
    if k % 512:
        return np.exp2(np.random.permutation(np.resize(levels, k // 32))).repeat(32)
    a = np.empty((k // 512, 16))
    for p in range(k // 512):
        a[p, :8] = np.random.permutation(np.resize(levels, 8))
        for g in range(8):
            far = levels[np.abs(levels - a[p, g]) >= 10]
            a[p, g + 8] = far[np.random.randint(len(far))]
    return np.exp2(a.ravel()).repeat(32)


def f64(x):
    return np.asarray(x).astype(np.float64)


def striped(idx):
    return np.tile(idx.reshape(-1, 16).T, (8, 1)).astype(np.uint16)


def unstriped(offs):
    return offs[:16].T.reshape(-1).astype(np.int64)


E2M1 = np.array([0.0, 0.5, 1.0, 1.5, 2.0, 3.0, 4.0, 6.0, -0.0, -0.5, -1.0, -1.5, -2.0, -3.0, -4.0, -6.0])


def pack_weight(w, fmt):
    k, n = w.shape
    w = f64(np.asarray(w, np.float32).astype(ml_dtypes.bfloat16)).reshape(k // 32, 32, n)
    amax = np.abs(w).max(1)
    if fmt == "e4m3":
        byte = np.frexp(amax)[1] - 1 + 127 - 7
    else:
        mant, ex = np.frexp(amax / 6.0)
        byte = np.where(mant > 0.5, ex, ex - 1) + 127
    byte = np.clip(np.where(amax > 0, byte, 1), 1, 254)
    scaled = (w * np.exp2(127.0 - byte)[:, None, :]).reshape(k, n).astype(np.float32)
    by_word = np.ascontiguousarray(scaled.reshape(k // 512, 128, 4, n).transpose(0, 1, 3, 2))
    if fmt == "e4m3":
        words = by_word.astype(ml_dtypes.float8_e4m3fn).view(np.uint8)
    else:
        c = by_word.astype(ml_dtypes.float4_e2m1fn).view(np.uint8) & 0xF
        words = (c[..., 0::2] | (c[..., 1::2] << 4)).reshape(k // 512, 128, 2 * n)
    return np.ascontiguousarray(words), np.ascontiguousarray(byte.astype(np.uint8).reshape(k // 512, 16, n))


def unpack_weight(words, scales, fmt):
    g, _, n = scales.shape
    words = np.ascontiguousarray(words).reshape(g, 128, n, -1)
    if fmt == "e4m3":
        vals = words.view(ml_dtypes.float8_e4m3fn).astype(np.float64)
    else:
        nib = np.empty((g, 128, n, 4), np.uint8)
        nib[..., 0::2] = words & 0xF
        nib[..., 1::2] = words >> 4
        vals = E2M1[nib]
    vals = vals * np.repeat(np.exp2(scales.astype(np.float64) - 127.0), 8, axis=1)[..., None]
    return vals.transpose(0, 1, 3, 2).reshape(g * 512, n)


def gelu(v):
    return 0.5 * v * (1.0 + np.tanh(np.sqrt(2.0 / np.pi) * (v + 0.044715 * v**3)))


def striped8(idx):
    return np.concatenate([v.reshape(-1, 16).T for v in idx]).astype(np.uint16)


def unstriped8(offs):
    return np.stack([offs[16 * g:16 * g + 16].T.reshape(-1) for g in range(8)]).astype(np.int64)


def runs(v, idx8):
    k = np.arange(v.shape[0])
    return v[k[:, None], idx8[k % 512 // 64]]


def often(T, S):
    return np.random.permutation(T)[(T * np.random.uniform(0, 1, S) ** 4).astype(np.int64)]


K, T, S, H, N = 1024, 2048, 1024, 512, 384

def setup_inputs():
    n = np.random.standard_normal
    s = mx_kscale(K)[:, None]
    u = mx_kscale(H)[:, None]
    tab_words, tab_scales = pack_weight(n((K, T)) * s, "e4m3")
    w2_words, w2_scales = pack_weight(n((K, H)) / np.sqrt(K) / s * u.T, "e2m1")
    w3_words, w3_scales = pack_weight(n((K, H)) / np.sqrt(K) / s * u.T, "e4m3")
    return {
        "tab_words": tab_words, "tab_scales": tab_scales,
        "offs": striped8(np.stack([often(T, S) for _ in range(8)])),
        "w1": (n((K, H)) / np.sqrt(K) / s * u.T).astype(np.float32),
        "w2_words": w2_words, "w2_scales": w2_scales,
        "w3_words": w3_words, "w3_scales": w3_scales,
        "lam": (0.8 * np.exp(0.3 * n(H))).astype(np.float32),
        "w4": (n((H, N)) / np.sqrt(H) / u).astype(np.float32),
        "bo": (0.5 * n(N)).astype(np.float32),
    }

def reference(tab_words, tab_scales, offs, w1, w2_words, w2_scales,
              w3_words, w3_scales, lam, w4, bo):
    v = runs(unpack_weight(tab_words, tab_scales, "e4m3"), unstriped8(offs))
    w2 = unpack_weight(w2_words, w2_scales, "e2m1")
    w3 = unpack_weight(w3_words, w3_scales, "e4m3")
    goal = mxq(f64(w1), 0, "e4m3").T @ v
    infer = w2.T @ v
    length = w3.T @ v
    h = np.maximum(goal, infer) - f64(lam)[:, None] * length
    y = mxq(f64(w4), 0, "e4m3").T @ mxq(h, 0, "e4m3")
    return y + f64(bo)[:, None]

@@ -1,0 +1,224 @@
+from contextlib import ExitStack
+
+import concourse.mybir as mybir
+
+K, T, S, H, N = 1024, 2048, 1024, 512, 384
+FLOPS = 2 * K * H * S * 3 + 2 * H * N * S
+
+F32 = mybir.dt.float32
+BF16 = mybir.dt.bfloat16
+I32 = mybir.dt.int32
+U32 = mybir.dt.uint32
+U16 = mybir.dt.uint16
+U8 = mybir.dt.uint8
+FP8X4 = mybir.dt.float8_e4m3fn_x4
+FP4X4 = mybir.dt.float4_e2m1fn_x4
+ALU = mybir.AluOpType
+ACT = mybir.ActivationFunctionType
+
+P = 128
+PASSES = 2
+HALF = 512
+QUART = 256
+SROW = S + 2 * H
+
+
+def tile_list_clause_evaluator_kernel(
+    tc, tab_words, tab_scales, offs, w1, w2_words, w2_scales, w3_words, w3_scales, lam, w4, bo, out
+):
+    nc = tc.nc
+    with ExitStack() as ctx:
+        keep = ctx.enter_context(tc.tile_pool(name="keep", bufs=1))
+        ring = ctx.enter_context(tc.tile_pool(name="ring", bufs=2))
+        psum = ctx.enter_context(tc.psum_pool(name="psum", bufs=2))
+
+        offsets = keep.tile([P, S // 16], U16, name="offsets")
+        nc.sync.dma_start(offsets[:], offs)
+
+        ts_win = keep.tile([P, T], U8, name="ts_win", align_bytes=64)
+        ws_raw = keep.tile([P, 2 * H], U8, name="ws_raw", tag="ws_then_w2", align_bytes=64)
+        planes = keep.tile([P, PASSES * SROW], U8, name="planes", align_bytes=64)
+        nc.gpsimd.memset(ts_win[:].bitcast(I32), 0)
+        nc.vector.memset(ws_raw[:].bitcast(I32), 0)
+        nc.vector.memset(planes[:].bitcast(I32), 0)
+        nc.scalar.dma_start(ts_win[0:P:4, :].bitcast(I32), tab_scales.bitcast(I32).rearrange("a q c -> q a c"))
+        nc.gpsimd.dma_start(ws_raw[0:P:4, 0:H].bitcast(I32), w2_scales.bitcast(I32).rearrange("a q c -> q a c"))
+        nc.gpsimd.dma_start(ws_raw[0:P:4, H:2 * H].bitcast(I32), w3_scales.bitcast(I32).rearrange("a q c -> q a c"))
+
+        w2_raw = keep.tile([P, PASSES, H // 2], I32, name="w2_raw", align_bytes=64)
+        w3_raw = keep.tile([P, PASSES, H], I32, name="w3_raw", align_bytes=64)
+        nc.sync.dma_start(w2_raw[:], w2_words.bitcast(I32).rearrange("a p c -> p a c"))
+        tab = []
+        for a in range(PASSES):
+            t_a = keep.tile([P, T], I32, name="tab%d" % a, align_bytes=64)
+            nc.sync.dma_start(t_a[:], tab_words[a].rearrange("p t i -> p (t i)").bitcast(I32))
+            tab.append(t_a)
+        nc.sync.dma_start(
+            w3_raw[:], w3_words.rearrange("a p c i -> a p (c i)").bitcast(I32).rearrange("a p c -> p a c"))
+        w1_first = keep.tile([P, 4 * H], F32, name="w1_first", align_bytes=64)
+        nc.sync.dma_start(w1_first[:], w1[0:512, :].rearrange("(p j) c -> p (j c)", j=4))
+
+        ts_got = keep.tile([P, S], U8, name="ts_got", tag="v0_0", align_bytes=64)
+        nc.vector.tensor_copy(ts_got[:], ts_win[:].indirect(offsets[:]))
+        staged = keep.tile([P, SROW], U8, name="staged", tag="staged_then_late", align_bytes=64)
+        nc.vector.tensor_copy(staged[:, 0:S].bitcast(I32), ts_got[:].bitcast(I32))
+        nc.vector.tensor_copy(
+            staged[:, S:].rearrange("p (w t m) -> p w m t", w=2, t=4),
+            ws_raw[:].rearrange("p (w m t) -> p w m t", w=2, t=4))
+        for d in range(4):
+            nc.scalar.dma_start(
+                planes[32 * d:32 * d + 4, :].bitcast(I32).rearrange("p (a c) -> p a c", a=PASSES),
+                staged[32 * d:32 * d + 32:4, :].bitcast(I32))
+
+        late = keep.tile([P, 4 * H + 4 * N + 16], F32, name="late", tag="staged_then_late", align_bytes=64)
+        lam_t = late[:, 4 * H + 4 * N:4 * H + 4 * N + 4]
+        bo_t = late[:, 4 * H + 4 * N + 8:4 * H + 4 * N + 11]
+        nc.sync.dma_start(lam_t, lam.rearrange("(p t) -> p t", t=4))
+        w1_second = [late[:, u * 2 * H:(u + 1) * 2 * H].rearrange("p (j c) -> p j c", j=4) for u in range(2)]
+        for u in range(2):
+            nc.sync.dma_start(
+                w1_second[u], w1[512:1024, u * (H // 2):(u + 1) * (H // 2)].rearrange("(p j) c -> p j c", j=4))
+        w4_raw = late[:, 4 * H:4 * H + 4 * N]
+        nc.sync.dma_start(w4_raw, w4.rearrange("(p t) n -> p (t n)", t=4))
+        with nc.allow_non_contiguous_dma(reason="one value a partition"):
+            nc.sync.dma_start(bo_t, bo.rearrange("(m p) -> p m", p=P))
+
+        w2_c = keep.tile([P, PASSES * H], U16, name="w2_c", tag="ws_then_w2", align_bytes=64)
+        w3_c = keep.tile([P, PASSES * H], I32, name="w3_c", align_bytes=64)
+        nc.vector.tensor_copy(
+            w2_c[:].rearrange("p (a t m) -> p a m t", a=PASSES, t=4),
+            w2_raw[:].bitcast(U16).rearrange("p a (m t) -> p a m t", t=4))
+
+        v = {}
+
+        def look_up(a, hf):
+            got = keep.tile([P, HALF], U32, name="v%d_%d" % (a, hf), tag="v%d_%d" % (a, hf), align_bytes=64)
+            nc.vector.tensor_copy(got[:], tab[a][:].bitcast(U32).indirect(offsets[:, 32 * hf:32 * (hf + 1)]))
+            v[a, hf] = got
+
+        look_up(0, 0)
+        look_up(1, 0)
+        nc.vector.tensor_copy(
+            w3_c[:].rearrange("p (a t m) -> p a m t", a=PASSES, t=4),
+            w3_raw[:].rearrange("p a (m t) -> p a m t", t=4))
+        look_up(0, 1)
+        look_up(1, 1)
+
+        def plane(a, c0, n):
+            return planes[:, a * SROW + c0:a * SROW + c0 + n]
+
+        inf_sb = [keep.tile([P, 4, HALF], F32, name="inf%d" % hf, align_bytes=64) for hf in range(2)]
+        len_sb = [keep.tile([P, 4, HALF], F32, name="len%d" % hf, align_bytes=64) for hf in range(2)]
+
+        def side_product(hf, ts, codes, dtype, scale_col):
+            banks = {t: psum.tile([P, HALF], F32, name="side_bank", bufs=4) for t in ts}
+            for a in range(PASSES):
+                for t in ts:
+                    c = a * H + t * P
+                    nc.tensor.matmul_mx(
+                        banks[t][:], lhsT=codes[:, c:c + P].bitcast(dtype),
+                        lhsT_scale=plane(a, scale_col + t * P, P),
+                        rhs=v[a, hf][:].bitcast(FP8X4), rhs_scale=plane(a, hf * HALF, HALF),
+                        start=(a == 0), stop=(a == PASSES - 1))
+            return banks
+
+        def infer(hf, ts):
+            banks = side_product(hf, ts, w2_c, FP4X4, S)
+            for t in ts:
+                nc.scalar.copy(inf_sb[hf][:, t, :], banks[t][:])
+
+        def length(hf, ts):
+            banks = side_product(hf, ts, w3_c, FP8X4, S + H)
+            for t in ts:
+                nc.scalar.activation(len_sb[hf][:, t, :], banks[t][:], ACT.Copy, scale=lam_t[:, t:t + 1])
+
+        infer(0, (0, 1, 2, 3))
+        for t in range(4):
+            length(0, (t,))
+
+        w1_c = keep.tile([P, PASSES * H], U32, name="w1_c", align_bytes=64)
+        w1_s = keep.tile([P, PASSES * H], U8, name="w1_s", align_bytes=64)
+        w1_g = [keep.tile([P, 4 * H], BF16, name="w1_g%d" % a, align_bytes=64) for a in range(PASSES)]
+        nc.vector.tensor_copy(
+            w1_g[0][:].rearrange("p (t m j) -> p m j t", t=4, j=4),
+            w1_first[:].rearrange("p (j m t) -> p m j t", t=4, j=4))
+        nc.vector.quantize_mx(w1_c[:, 0:H].bitcast(FP8X4), w1_s[:, 0:H], w1_g[0][:])
+        for u in range(2):
+            nc.vector.tensor_copy(
+                w1_g[1][:].rearrange("p (t m j) -> p m j t", t=4, j=4)[:, 64 * u:64 * (u + 1)],
+                w1_second[u].rearrange("p j (m t) -> p m j t", t=4))
+        for t in range(4):
+            nc.vector.quantize_mx(w1_c[:, H + t * P:H + (t + 1) * P].bitcast(FP8X4),
+                                  w1_s[:, H + t * P:H + (t + 1) * P], w1_g[1][:, t * 512:(t + 1) * 512])
+
+        w4_g = keep.tile([P, 4 * N], BF16, name="w4_g", align_bytes=64)
+        w4_c = keep.tile([P, N], U32, name="w4_c", align_bytes=64)
+        w4_s = keep.tile([P, N], U8, name="w4_s", align_bytes=64)
+
+        def prepare_w4():
+            nc.scalar.copy(w4_g[:].rearrange("p (c i t) -> p c t i", i=4, t=4),
+                           w4_raw.rearrange("p (t c i) -> p c t i", i=4, t=4))
+            for c0, c1 in ((0, 256), (256, 384)):
+                nc.vector.quantize_mx(w4_c[:, c0:c1].bitcast(FP8X4), w4_s[:, c0:c1], w4_g[:, 4 * c0:4 * c1])
+
+        h_c = {}
+        h_s = {}
+
+        def hidden(qt):
+            hf, c0 = qt // 2, (qt % 2) * QUART
+            best = ring.tile([P, 4, QUART], F32, name="best", align_bytes=64)
+            for u in range(2):
+                bank = psum.tile([P, HALF], F32, name="goal_bank")
+                for tt in range(2):
+                    t = 2 * u + tt
+                    for a in range(PASSES):
+                        c = a * H + t * P
+                        nc.tensor.matmul_mx(
+                            bank[:, tt * QUART:(tt + 1) * QUART], lhsT=w1_c[:, c:c + P].bitcast(FP8X4),
+                            lhsT_scale=w1_s[:, c:c + P],
+                            rhs=v[a, hf][:, c0:c0 + QUART].bitcast(FP8X4),
+                            rhs_scale=plane(a, qt * QUART, QUART),
+                            start=(a == 0), stop=(a == PASSES - 1))
+                nc.vector.tensor_tensor(
+                    best[:, 2 * u:2 * u + 2, :], bank[:].rearrange("p (t c) -> p t c", t=2),
+                    inf_sb[hf][:, 2 * u:2 * u + 2, c0:c0 + QUART], ALU.max)
+            h_g = ring.tile([P, 4 * QUART], BF16, name="h_g", align_bytes=64)
+            nc.vector.tensor_tensor(
+                h_g[:].rearrange("p (c i t) -> p c t i", i=4, t=4),
+                best[:].rearrange("p t (c i) -> p c t i", i=4),
+                len_sb[hf][:, :, c0:c0 + QUART].rearrange("p t (c i) -> p c t i", i=4), ALU.subtract)
+            h_c[qt] = keep.tile([P, QUART], U32, name="h_c%d" % qt, align_bytes=64)
+            h_s[qt] = keep.tile([P, QUART], U8, name="h_s%d" % qt, align_bytes=64)
+            nc.vector.quantize_mx(h_c[qt][:].bitcast(FP8X4), h_s[qt][:], h_g[:])
+
+        out_rows = out.rearrange("(m p) j -> p m j", p=P)
+
+        def scores(qt):
+            banks = [psum.tile([P, HALF], F32, name="score_bank") for u in range(2)]
+            res = keep.tile([P, 3, QUART], F32, name="res%d" % qt, align_bytes=64)
+            for m in range(3):
+                acc = banks[m // 2][:, (m % 2) * QUART:(m % 2 + 1) * QUART]
+                nc.tensor.matmul_mx(
+                    acc, lhsT=w4_c[:, m * P:(m + 1) * P].bitcast(FP8X4), lhsT_scale=w4_s[:, m * P:(m + 1) * P],
+                    rhs=h_c[qt][:].bitcast(FP8X4), rhs_scale=h_s[qt][:], start=True, stop=True)
+            for m in range(3):
+                acc = banks[m // 2][:, (m % 2) * QUART:(m % 2 + 1) * QUART]
+                nc.scalar.activation(res[:, m, :], acc, ACT.Identity, bias=bo_t[:, m:m + 1])
+            nc.sync.dma_start(out_rows[:, :, qt * QUART:(qt + 1) * QUART], res[:])
+
+        infer(1, (0,))
+        infer(1, (1,))
+        hidden(0)
+        infer(1, (2,))
+        infer(1, (3,))
+        length(1, (0,))
+        hidden(1)
+        for t in range(1, 4):
+            length(1, (t,))
+        prepare_w4()
+        hidden(2)
+        scores(0)
+        hidden(3)
+        scores(1)
+        scores(2)
+        scores(3)

@@ -30,79 +30,83 @@ def tile_list_clause_evaluator_kernel(
     with ExitStack() as ctx:
         keep = ctx.enter_context(tc.tile_pool(name="keep", bufs=1))
         ring = ctx.enter_context(tc.tile_pool(name="ring", bufs=2))
-        psum = ctx.enter_context(tc.psum_pool(name="psum", bufs=2))
+        psum = ctx.enter_context(tc.psum_pool(name="psum", bufs=4))
 
         offsets = keep.tile([P, S // 16], U16, name="offsets")
         nc.sync.dma_start(offsets[:], offs)
 
-        ts_win = keep.tile([P, T], U8, name="ts_win", align_bytes=64)
-        ws_raw = keep.tile([P, 2 * H], U8, name="ws_raw", tag="ws_then_w2", align_bytes=64)
-        planes = keep.tile([P, PASSES * SROW], U8, name="planes", align_bytes=64)
+        ts_win = keep.tile([P, T], U8, name="ts_win", tag="win_then_staged", align_bytes=64)
+        ws_raw = keep.tile([P, 2 * H], U8, name="ws_raw", tag="ws_then_w3", align_bytes=64)
         nc.gpsimd.memset(ts_win[:].bitcast(I32), 0)
         nc.vector.memset(ws_raw[:].bitcast(I32), 0)
+        planes = keep.tile([P, PASSES * SROW], U8, name="planes", align_bytes=64)
         nc.vector.memset(planes[:].bitcast(I32), 0)
-        nc.scalar.dma_start(ts_win[0:P:4, :].bitcast(I32), tab_scales.bitcast(I32).rearrange("a q c -> q a c"))
-        nc.gpsimd.dma_start(ws_raw[0:P:4, 0:H].bitcast(I32), w2_scales.bitcast(I32).rearrange("a q c -> q a c"))
-        nc.gpsimd.dma_start(ws_raw[0:P:4, H:2 * H].bitcast(I32), w3_scales.bitcast(I32).rearrange("a q c -> q a c"))
 
-        w2_raw = keep.tile([P, PASSES, H // 2], I32, name="w2_raw", align_bytes=64)
-        w3_raw = keep.tile([P, PASSES, H], I32, name="w3_raw", align_bytes=64)
+        nc.scalar.dma_start(ts_win[0:P:4, :].bitcast(I32), tab_scales.bitcast(I32).rearrange("a q c -> q a c"))
+        nc.scalar.dma_start(ws_raw[0:P:4, 0:H].bitcast(I32), w2_scales.bitcast(I32).rearrange("a q c -> q a c"))
+        nc.scalar.dma_start(ws_raw[0:P:4, H:2 * H].bitcast(I32), w3_scales.bitcast(I32).rearrange("a q c -> q a c"))
+
+        lam_t = keep.tile([P, 13], F32, name="lam_t")
+        for e in range(4):
+            nc.gpsimd.dma_start(lam_t[e:P:4, :], lam.rearrange("(q r) -> q r", r=16)[:, e:e + 13])
+        w2_raw = keep.tile([P, PASSES, H // 2], I32, name="w2_raw", tag="tab1", align_bytes=64)
+        w3_raw = keep.tile([P, PASSES, H], I32, name="w3_raw", tag="w3_then_late", align_bytes=64)
         nc.sync.dma_start(w2_raw[:], w2_words.bitcast(I32).rearrange("a p c -> p a c"))
-        tab = []
-        for a in range(PASSES):
-            t_a = keep.tile([P, T], I32, name="tab%d" % a, align_bytes=64)
-            nc.sync.dma_start(t_a[:], tab_words[a].rearrange("p t i -> p (t i)").bitcast(I32))
-            tab.append(t_a)
         nc.sync.dma_start(
             w3_raw[:], w3_words.rearrange("a p c i -> a p (c i)").bitcast(I32).rearrange("a p c -> p a c"))
-        w1_first = keep.tile([P, 4 * H], F32, name="w1_first", align_bytes=64)
-        nc.sync.dma_start(w1_first[:], w1[0:512, :].rearrange("(p j) c -> p (j c)", j=4))
-
-        ts_got = keep.tile([P, S], U8, name="ts_got", tag="v0_0", align_bytes=64)
-        nc.vector.tensor_copy(ts_got[:], ts_win[:].indirect(offsets[:]))
-        staged = keep.tile([P, SROW], U8, name="staged", tag="staged_then_late", align_bytes=64)
-        nc.vector.tensor_copy(staged[:, 0:S].bitcast(I32), ts_got[:].bitcast(I32))
+        w2_c = keep.tile([P, PASSES * H // 2], I32, name="w2_c", align_bytes=64)
         nc.vector.tensor_copy(
-            staged[:, S:].rearrange("p (w t m) -> p w m t", w=2, t=4),
-            ws_raw[:].rearrange("p (w m t) -> p w m t", w=2, t=4))
-        for d in range(4):
+            w2_c[:].rearrange("p (a t q e) -> p a q t e", a=PASSES, t=4, e=2),
+            w2_raw[:].rearrange("p a (q t e) -> p a q t e", t=4, e=2))
+        tab = []
+        for a in range(PASSES):
+            t_a = keep.tile([P, T], I32, name="tab%d" % a, tag="tab%d" % a, align_bytes=64)
+            nc.sync.dma_start(t_a[:], tab_words[a].rearrange("p t i -> p (t i)").bitcast(I32))
+            tab.append(t_a)
+
+        ts_got = keep.tile([P, S], U8, name="ts_got", tag="got_then_v0", align_bytes=64)
+        nc.vector.tensor_copy(ts_got[:], ts_win[:].indirect(offsets[:]))
+        staged = keep.tile([P, SROW], U8, name="staged", tag="win_then_staged", align_bytes=64)
+        staged_w = staged[:].bitcast(I32)
+        nc.vector.tensor_copy(staged_w[:, 0:S // 4], ts_got[:].bitcast(I32))
+        nc.vector.tensor_copy(
+            staged_w[:, S // 4:].rearrange("p (w t q) -> p w q t", w=2, t=4),
+            ws_raw[:].bitcast(I32).rearrange("p (w q t) -> p w q t", w=2, t=4))
+        for d in (0, 2, 1, 3):
             nc.scalar.dma_start(
                 planes[32 * d:32 * d + 4, :].bitcast(I32).rearrange("p (a c) -> p a c", a=PASSES),
                 staged[32 * d:32 * d + 32:4, :].bitcast(I32))
 
-        late = keep.tile([P, 4 * H + 4 * N + 16], F32, name="late", tag="staged_then_late", align_bytes=64)
-        lam_t = late[:, 4 * H + 4 * N:4 * H + 4 * N + 4]
-        bo_t = late[:, 4 * H + 4 * N + 8:4 * H + 4 * N + 11]
-        nc.sync.dma_start(lam_t, lam.rearrange("(p t) -> p t", t=4))
-        w1_second = [late[:, u * 2 * H:(u + 1) * 2 * H].rearrange("p (j c) -> p j c", j=4) for u in range(2)]
+        w3_c = keep.tile([P, PASSES * H], I32, name="w3_c", tag="ws_then_w3", align_bytes=64)
+        nc.vector.tensor_copy(
+            w3_c[:].rearrange("p (a t q e) -> p a q t e", a=PASSES, t=4, e=4),
+            w3_raw[:].rearrange("p a (q t e) -> p a q t e", t=4, e=4))
+        late = keep.tile([P, 8 * H + 4 * N + 3], F32, name="late", tag="w3_then_late", align_bytes=64)
+        w1_first = late[:, 0:4 * H]
+        nc.sync.dma_start(w1_first, w1[0:512, :].rearrange("(p j) c -> p (j c)", j=4))
+        w1_second = [late[:, (2 + u) * 2 * H:(3 + u) * 2 * H].rearrange("p (j c) -> p j c", j=4) for u in range(2)]
         for u in range(2):
             nc.sync.dma_start(
                 w1_second[u], w1[512:1024, u * (H // 2):(u + 1) * (H // 2)].rearrange("(p j) c -> p j c", j=4))
-        w4_raw = late[:, 4 * H:4 * H + 4 * N]
-        nc.sync.dma_start(w4_raw, w4.rearrange("(p t) n -> p (t n)", t=4))
+        w4_raw = late[:, 8 * H:8 * H + 4 * N]
+        w4_rows = w4.rearrange("(q t e) n -> t q e n", t=4, e=4)
+        for t in range(4):
+            nc.sync.dma_start(w4_raw[:, t * N:(t + 1) * N], w4_rows[t])
+        bo_t = late[:, 8 * H + 4 * N:]
         with nc.allow_non_contiguous_dma(reason="one value a partition"):
             nc.sync.dma_start(bo_t, bo.rearrange("(m p) -> p m", p=P))
 
-        w2_c = keep.tile([P, PASSES * H], U16, name="w2_c", tag="ws_then_w2", align_bytes=64)
-        w3_c = keep.tile([P, PASSES * H], I32, name="w3_c", align_bytes=64)
-        nc.vector.tensor_copy(
-            w2_c[:].rearrange("p (a t m) -> p a m t", a=PASSES, t=4),
-            w2_raw[:].bitcast(U16).rearrange("p a (m t) -> p a m t", t=4))
 
         v = {}
+        got = keep.tile([P, S], U32, name="v0", tag="got_then_v0", align_bytes=64)
+        nc.vector.tensor_copy(got[:], tab[0][:].bitcast(U32).indirect(offsets[:]))
+        for hf in range(2):
+            v[0, hf] = got[:, hf * HALF:(hf + 1) * HALF]
+        for hf in range(2):
+            got = keep.tile([P, HALF], U32, name="v1_%d" % hf, align_bytes=64)
+            nc.vector.tensor_copy(got[:], tab[1][:].bitcast(U32).indirect(offsets[:, 32 * hf:32 * (hf + 1)]))
+            v[1, hf] = got[:]
 
-        def look_up(a, hf):
-            got = keep.tile([P, HALF], U32, name="v%d_%d" % (a, hf), tag="v%d_%d" % (a, hf), align_bytes=64)
-            nc.vector.tensor_copy(got[:], tab[a][:].bitcast(U32).indirect(offsets[:, 32 * hf:32 * (hf + 1)]))
-            v[a, hf] = got
-
-        look_up(0, 0)
-        look_up(1, 0)
-        nc.vector.tensor_copy(
-            w3_c[:].rearrange("p (a t m) -> p a m t", a=PASSES, t=4),
-            w3_raw[:].rearrange("p a (m t) -> p a m t", t=4))
-        look_up(0, 1)
-        look_up(1, 1)
 
         def plane(a, c0, n):
             return planes[:, a * SROW + c0:a * SROW + c0 + n]
@@ -110,43 +114,45 @@ def tile_list_clause_evaluator_kernel(
         inf_sb = [keep.tile([P, 4, HALF], F32, name="inf%d" % hf, align_bytes=64) for hf in range(2)]
         len_sb = [keep.tile([P, 4, HALF], F32, name="len%d" % hf, align_bytes=64) for hf in range(2)]
 
-        def side_product(hf, ts, codes, dtype, scale_col):
-            banks = {t: psum.tile([P, HALF], F32, name="side_bank", bufs=4) for t in ts}
+        def side_product(hf, ts, codes, per_word, dtype, scale_col):
+            banks = {t: psum.tile([P, HALF], F32, name="side_bank") for t in ts}
             for a in range(PASSES):
                 for t in ts:
                     c = a * H + t * P
                     nc.tensor.matmul_mx(
-                        banks[t][:], lhsT=codes[:, c:c + P].bitcast(dtype),
+                        banks[t][:], lhsT=codes[:, c // per_word:(c + P) // per_word].bitcast(dtype),
                         lhsT_scale=plane(a, scale_col + t * P, P),
-                        rhs=v[a, hf][:].bitcast(FP8X4), rhs_scale=plane(a, hf * HALF, HALF),
+                        rhs=v[a, hf].bitcast(FP8X4), rhs_scale=plane(a, hf * HALF, HALF),
                         start=(a == 0), stop=(a == PASSES - 1))
             return banks
 
         def infer(hf, ts):
-            banks = side_product(hf, ts, w2_c, FP4X4, S)
+            banks = side_product(hf, ts, w2_c, 2, FP4X4, S)
             for t in ts:
                 nc.scalar.copy(inf_sb[hf][:, t, :], banks[t][:])
 
         def length(hf, ts):
-            banks = side_product(hf, ts, w3_c, FP8X4, S + H)
+            banks = side_product(hf, ts, w3_c, 1, FP8X4, S + H)
             for t in ts:
-                nc.scalar.activation(len_sb[hf][:, t, :], banks[t][:], ACT.Copy, scale=lam_t[:, t:t + 1])
+                nc.scalar.activation(len_sb[hf][:, t, :], banks[t][:], ACT.Copy, scale=lam_t[:, 4 * t:4 * t + 1])
 
-        infer(0, (0, 1, 2, 3))
+        infer(0, (0, 1))
+        infer(0, (2,))
+        infer(0, (3,))
         for t in range(4):
             length(0, (t,))
 
         w1_c = keep.tile([P, PASSES * H], U32, name="w1_c", align_bytes=64)
         w1_s = keep.tile([P, PASSES * H], U8, name="w1_s", align_bytes=64)
-        w1_g = [keep.tile([P, 4 * H], BF16, name="w1_g%d" % a, align_bytes=64) for a in range(PASSES)]
+        w1_g = [keep.tile([P, 4 * H], BF16, name="w1_g%d" % a, tag="tab%d" % a, align_bytes=64) for a in range(PASSES)]
         nc.vector.tensor_copy(
-            w1_g[0][:].rearrange("p (t m j) -> p m j t", t=4, j=4),
-            w1_first[:].rearrange("p (j m t) -> p m j t", t=4, j=4))
+            w1_g[0][:].rearrange("p (t q e j) -> p q t j e", t=4, e=4, j=4),
+            w1_first.rearrange("p (j q t e) -> p q t j e", t=4, e=4, j=4))
         nc.vector.quantize_mx(w1_c[:, 0:H].bitcast(FP8X4), w1_s[:, 0:H], w1_g[0][:])
         for u in range(2):
             nc.vector.tensor_copy(
-                w1_g[1][:].rearrange("p (t m j) -> p m j t", t=4, j=4)[:, 64 * u:64 * (u + 1)],
-                w1_second[u].rearrange("p j (m t) -> p m j t", t=4))
+                w1_g[1][:].rearrange("p (t q e j) -> p q t j e", t=4, e=4, j=4)[:, 16 * u:16 * (u + 1)],
+                w1_second[u].rearrange("p j (q t e) -> p q t j e", t=4, e=4))
         for t in range(4):
             nc.vector.quantize_mx(w1_c[:, H + t * P:H + (t + 1) * P].bitcast(FP8X4),
                                   w1_s[:, H + t * P:H + (t + 1) * P], w1_g[1][:, t * 512:(t + 1) * 512])
@@ -155,18 +161,24 @@ def tile_list_clause_evaluator_kernel(
         w4_c = keep.tile([P, N], U32, name="w4_c", align_bytes=64)
         w4_s = keep.tile([P, N], U8, name="w4_s", align_bytes=64)
 
-        def prepare_w4():
+        def round_w4():
             nc.scalar.copy(w4_g[:].rearrange("p (c i t) -> p c t i", i=4, t=4),
                            w4_raw.rearrange("p (t c i) -> p c t i", i=4, t=4))
+
+        def quantise_w4():
             for c0, c1 in ((0, 256), (256, 384)):
                 nc.vector.quantize_mx(w4_c[:, c0:c1].bitcast(FP8X4), w4_s[:, c0:c1], w4_g[:, 4 * c0:4 * c1])
 
         h_c = {}
         h_s = {}
 
-        def hidden(qt):
+        best_of = {}
+        h_g_of = {}
+
+        def better_view(qt):
             hf, c0 = qt // 2, (qt % 2) * QUART
             best = ring.tile([P, 4, QUART], F32, name="best", align_bytes=64)
+            best_of[qt] = best
             for u in range(2):
                 bank = psum.tile([P, HALF], F32, name="goal_bank")
                 for tt in range(2):
@@ -182,43 +194,66 @@ def tile_list_clause_evaluator_kernel(
                 nc.vector.tensor_tensor(
                     best[:, 2 * u:2 * u + 2, :], bank[:].rearrange("p (t c) -> p t c", t=2),
                     inf_sb[hf][:, 2 * u:2 * u + 2, c0:c0 + QUART], ALU.max)
-            h_g = ring.tile([P, 4 * QUART], BF16, name="h_g", align_bytes=64)
+
+        def penalise(c0, n):
+            best = best_of[c0 // QUART][:, :, c0 % QUART:c0 % QUART + n]
+            h_g = ring.tile([P, 4 * n], BF16, name="h_g", align_bytes=64, bufs=3)
+            h_g_of[c0] = h_g
             nc.vector.tensor_tensor(
                 h_g[:].rearrange("p (c i t) -> p c t i", i=4, t=4),
-                best[:].rearrange("p t (c i) -> p c t i", i=4),
-                len_sb[hf][:, :, c0:c0 + QUART].rearrange("p t (c i) -> p c t i", i=4), ALU.subtract)
-            h_c[qt] = keep.tile([P, QUART], U32, name="h_c%d" % qt, align_bytes=64)
-            h_s[qt] = keep.tile([P, QUART], U8, name="h_s%d" % qt, align_bytes=64)
-            nc.vector.quantize_mx(h_c[qt][:].bitcast(FP8X4), h_s[qt][:], h_g[:])
+                best.rearrange("p t (c i) -> p c t i", i=4),
+                len_sb[c0 // HALF][:, :, c0 % HALF:c0 % HALF + n].rearrange("p t (c i) -> p c t i", i=4),
+                ALU.subtract)
+
+        def quantise(c0, n):
+            h_c[c0] = keep.tile([P, n], U32, name="h_c%d" % c0, align_bytes=64)
+            h_s[c0] = keep.tile([P, n], U8, name="h_s%d" % c0, align_bytes=64)
+            nc.vector.quantize_mx(h_c[c0][:].bitcast(FP8X4), h_s[c0][:], h_g_of[c0][:])
 
         out_rows = out.rearrange("(m p) j -> p m j", p=P)
 
-        def scores(qt):
-            banks = [psum.tile([P, HALF], F32, name="score_bank") for u in range(2)]
-            res = keep.tile([P, 3, QUART], F32, name="res%d" % qt, align_bytes=64)
+        def scores(c0, n, on_vector=False):
+            per_bank = HALF // n
+            banks = [psum.tile([P, HALF], F32, name="side_bank") for u in range(-(-3 // per_bank))]
+            res = keep.tile([P, 3, n], F32, name="res%d" % c0, align_bytes=64)
+            accs = [banks[m // per_bank][:, (m % per_bank) * n:(m % per_bank + 1) * n] for m in range(3)]
             for m in range(3):
-                acc = banks[m // 2][:, (m % 2) * QUART:(m % 2 + 1) * QUART]
                 nc.tensor.matmul_mx(
-                    acc, lhsT=w4_c[:, m * P:(m + 1) * P].bitcast(FP8X4), lhsT_scale=w4_s[:, m * P:(m + 1) * P],
-                    rhs=h_c[qt][:].bitcast(FP8X4), rhs_scale=h_s[qt][:], start=True, stop=True)
-            for m in range(3):
-                acc = banks[m // 2][:, (m % 2) * QUART:(m % 2 + 1) * QUART]
-                nc.scalar.activation(res[:, m, :], acc, ACT.Identity, bias=bo_t[:, m:m + 1])
-            nc.sync.dma_start(out_rows[:, :, qt * QUART:(qt + 1) * QUART], res[:])
+                    accs[m], lhsT=w4_c[:, m * P:(m + 1) * P].bitcast(FP8X4), lhsT_scale=w4_s[:, m * P:(m + 1) * P],
+                    rhs=h_c[c0][:].bitcast(FP8X4), rhs_scale=h_s[c0][:], start=True, stop=True)
+            if on_vector:
+                nc.vector.tensor_tensor(
+                    res[:], banks[0][:, 0:3 * n].rearrange("p (m c) -> p m c", m=3),
+                    bo_t.unsqueeze(2).broadcast_to([P, 3, n]), ALU.add)
+            else:
+                for m in range(3):
+                    nc.scalar.activation(res[:, m, :], accs[m], ACT.Identity, bias=bo_t[:, m:m + 1])
+            nc.sync.dma_start(out_rows[:, :, c0:c0 + n], res[:])
 
         infer(1, (0,))
         infer(1, (1,))
-        hidden(0)
+        better_view(0)
         infer(1, (2,))
         infer(1, (3,))
-        length(1, (0,))
-        hidden(1)
-        for t in range(1, 4):
+        penalise(0, QUART)
+        better_view(1)
+        for t in range(4):
             length(1, (t,))
-        prepare_w4()
-        hidden(2)
-        scores(0)
-        hidden(3)
-        scores(1)
-        scores(2)
-        scores(3)
+        quantise(0, QUART)
+        penalise(QUART, QUART)
+        better_view(2)
+        round_w4()
+        quantise(QUART, QUART)
+        penalise(2 * QUART, QUART)
+        quantise_w4()
+        scores(0, QUART)
+        better_view(3)
+        scores(QUART, QUART)
+        quantise(2 * QUART, QUART)
+        penalise(3 * QUART, P)
+        scores(2 * QUART, QUART)
+        penalise(3 * QUART + P, P)
+        quantise(3 * QUART, P)
+        quantise(3 * QUART + P, P)
+        scores(3 * QUART, P)
+        scores(3 * QUART + P, P, on_vector=True)

@@ -29,6 +29,7 @@ def tile_list_clause_evaluator_kernel(
     nc = tc.nc
     with ExitStack() as ctx:
         keep = ctx.enter_context(tc.tile_pool(name="keep", bufs=1))
+        reuse = ctx.enter_context(tc.tile_pool(name="reuse", bufs=1))
         ring = ctx.enter_context(tc.tile_pool(name="ring", bufs=2))
         psum = ctx.enter_context(tc.psum_pool(name="psum", bufs=4))
 
@@ -36,69 +37,69 @@ def tile_list_clause_evaluator_kernel(
         nc.sync.dma_start(offsets[:], offs)
 
         ts_win = keep.tile([P, T], U8, name="ts_win", tag="win_then_staged", align_bytes=64)
-        ws_raw = keep.tile([P, 2 * H], U8, name="ws_raw", tag="ws_then_w3", align_bytes=64)
-        nc.gpsimd.memset(ts_win[:].bitcast(I32), 0)
+        ws_raw = keep.tile([P, 2 * H], U8, name="ws_raw", tag="ws_then_late", align_bytes=64)
+        nc.vector.memset(ts_win[:].bitcast(I32), 0)
         nc.vector.memset(ws_raw[:].bitcast(I32), 0)
         planes = keep.tile([P, PASSES * SROW], U8, name="planes", align_bytes=64)
         nc.vector.memset(planes[:].bitcast(I32), 0)
 
-        nc.scalar.dma_start(ts_win[0:P:4, :].bitcast(I32), tab_scales.bitcast(I32).rearrange("a q c -> q a c"))
-        nc.scalar.dma_start(ws_raw[0:P:4, 0:H].bitcast(I32), w2_scales.bitcast(I32).rearrange("a q c -> q a c"))
-        nc.scalar.dma_start(ws_raw[0:P:4, H:2 * H].bitcast(I32), w3_scales.bitcast(I32).rearrange("a q c -> q a c"))
+        nc.sync.dma_start(ts_win[0:P:4, :].bitcast(I32), tab_scales.bitcast(I32).rearrange("a q c -> q a c"))
+        nc.sync.dma_start(ws_raw[0:P:4, 0:H].bitcast(I32), w2_scales.bitcast(I32).rearrange("a q c -> q a c"))
+        nc.sync.dma_start(ws_raw[0:P:4, H:2 * H].bitcast(I32), w3_scales.bitcast(I32).rearrange("a q c -> q a c"))
 
-        lam_t = keep.tile([P, 13], F32, name="lam_t")
-        for e in range(4):
-            nc.gpsimd.dma_start(lam_t[e:P:4, :], lam.rearrange("(q r) -> q r", r=16)[:, e:e + 13])
-        w2_raw = keep.tile([P, PASSES, H // 2], I32, name="w2_raw", tag="tab1", align_bytes=64)
-        w3_raw = keep.tile([P, PASSES, H], I32, name="w3_raw", tag="w3_then_late", align_bytes=64)
+        lam_t = keep.tile([P, 4], F32, name="lam_t")
+        nc.sync.dma_start(lam_t[:], lam.rearrange("(p t) -> p t", t=4))
+        w2_raw = keep.tile([P, PASSES, H // 2], I32, name="w2_raw", tag="tab0", align_bytes=64)
+        w3_raw = reuse.tile([P, PASSES, H], I32, name="w3_raw", offset=6144, align_bytes=64)
         nc.sync.dma_start(w2_raw[:], w2_words.bitcast(I32).rearrange("a p c -> p a c"))
         nc.sync.dma_start(
             w3_raw[:], w3_words.rearrange("a p c i -> a p (c i)").bitcast(I32).rearrange("a p c -> p a c"))
-        w2_c = keep.tile([P, PASSES * H // 2], I32, name="w2_c", align_bytes=64)
+        w4_raw = keep.tile([P, 4 * N], F32, name="w4_raw", align_bytes=64)
+        nc.sync.dma_start(w4_raw[:], w4.rearrange("(p t) n -> p (t n)", t=4))
+        w2_c = keep.tile([P, PASSES * H], U16, name="w2_c", align_bytes=64)
+        w3_c = keep.tile([P, PASSES * H], I32, name="w3_c", align_bytes=64)
         nc.vector.tensor_copy(
-            w2_c[:].rearrange("p (a t q e) -> p a q t e", a=PASSES, t=4, e=2),
-            w2_raw[:].rearrange("p a (q t e) -> p a q t e", t=4, e=2))
+            w2_c[:].rearrange("p (a t m) -> p a m t", a=PASSES, t=4),
+            w2_raw[:].bitcast(U16).rearrange("p a (m t) -> p a m t", t=4))
+        nc.vector.tensor_copy(
+            w3_c[:].rearrange("p (a t m) -> p a m t", a=PASSES, t=4),
+            w3_raw[:].rearrange("p a (m t) -> p a m t", t=4))
         tab = []
         for a in range(PASSES):
-            t_a = keep.tile([P, T], I32, name="tab%d" % a, tag="tab%d" % a, align_bytes=64)
+            if a == 0:
+                t_a = keep.tile([P, T], I32, name="tab0", tag="tab0", align_bytes=64)
+            else:
+                t_a = reuse.tile([P, T], I32, name="tab1", offset=0, align_bytes=64)
             nc.sync.dma_start(t_a[:], tab_words[a].rearrange("p t i -> p (t i)").bitcast(I32))
             tab.append(t_a)
 
-        ts_got = keep.tile([P, S], U8, name="ts_got", tag="got_then_v0", align_bytes=64)
+        ts_got = reuse.tile([P, S], U8, name="ts_got", offset=8192, align_bytes=64)
         nc.vector.tensor_copy(ts_got[:], ts_win[:].indirect(offsets[:]))
         staged = keep.tile([P, SROW], U8, name="staged", tag="win_then_staged", align_bytes=64)
         staged_w = staged[:].bitcast(I32)
         nc.vector.tensor_copy(staged_w[:, 0:S // 4], ts_got[:].bitcast(I32))
         nc.vector.tensor_copy(
-            staged_w[:, S // 4:].rearrange("p (w t q) -> p w q t", w=2, t=4),
-            ws_raw[:].bitcast(I32).rearrange("p (w q t) -> p w q t", w=2, t=4))
+            staged[:, S:].rearrange("p (w t m) -> p w m t", w=2, t=4),
+            ws_raw[:].rearrange("p (w m t) -> p w m t", w=2, t=4))
         for d in (0, 2, 1, 3):
-            nc.scalar.dma_start(
+            nc.sync.dma_start(
                 planes[32 * d:32 * d + 4, :].bitcast(I32).rearrange("p (a c) -> p a c", a=PASSES),
                 staged[32 * d:32 * d + 32:4, :].bitcast(I32))
 
-        w3_c = keep.tile([P, PASSES * H], I32, name="w3_c", tag="ws_then_w3", align_bytes=64)
-        nc.vector.tensor_copy(
-            w3_c[:].rearrange("p (a t q e) -> p a q t e", a=PASSES, t=4, e=4),
-            w3_raw[:].rearrange("p a (q t e) -> p a q t e", t=4, e=4))
-        late = keep.tile([P, 8 * H + 4 * N + 3], F32, name="late", tag="w3_then_late", align_bytes=64)
-        w1_first = late[:, 0:4 * H]
-        nc.sync.dma_start(w1_first, w1[0:512, :].rearrange("(p j) c -> p (j c)", j=4))
-        w1_second = [late[:, (2 + u) * 2 * H:(3 + u) * 2 * H].rearrange("p (j c) -> p j c", j=4) for u in range(2)]
-        for u in range(2):
+        late = keep.tile([P, 8 * H + 3], F32, name="late", tag="ws_then_late", align_bytes=64)
+        w1_late = []
+        for u, (a, hf) in enumerate(((0, 0), (0, 1), (1, 0), (1, 1))):
+            part = late[:, u * 2 * H:(u + 1) * 2 * H].rearrange("p (j c) -> p j c", j=4)
             nc.sync.dma_start(
-                w1_second[u], w1[512:1024, u * (H // 2):(u + 1) * (H // 2)].rearrange("(p j) c -> p j c", j=4))
-        w4_raw = late[:, 8 * H:8 * H + 4 * N]
-        w4_rows = w4.rearrange("(q t e) n -> t q e n", t=4, e=4)
-        for t in range(4):
-            nc.sync.dma_start(w4_raw[:, t * N:(t + 1) * N], w4_rows[t])
-        bo_t = late[:, 8 * H + 4 * N:]
+                part, w1[512 * a:512 * (a + 1), hf * (H // 2):(hf + 1) * (H // 2)].rearrange("(p j) c -> p j c", j=4))
+            w1_late.append((a, hf, part))
+        bo_t = late[:, 8 * H:]
         with nc.allow_non_contiguous_dma(reason="one value a partition"):
             nc.sync.dma_start(bo_t, bo.rearrange("(m p) -> p m", p=P))
 
 
         v = {}
-        got = keep.tile([P, S], U32, name="v0", tag="got_then_v0", align_bytes=64)
+        got = reuse.tile([P, S], U32, name="v0", offset=8192, align_bytes=64)
         nc.vector.tensor_copy(got[:], tab[0][:].bitcast(U32).indirect(offsets[:]))
         for hf in range(2):
             v[0, hf] = got[:, hf * HALF:(hf + 1) * HALF]
@@ -127,14 +128,29 @@ def tile_list_clause_evaluator_kernel(
             return banks
 
         def infer(hf, ts):
-            banks = side_product(hf, ts, w2_c, 2, FP4X4, S)
+            banks = side_product(hf, ts, w2_c, 1, FP4X4, S)
             for t in ts:
                 nc.scalar.copy(inf_sb[hf][:, t, :], banks[t][:])
 
         def length(hf, ts):
             banks = side_product(hf, ts, w3_c, 1, FP8X4, S + H)
             for t in ts:
-                nc.scalar.activation(len_sb[hf][:, t, :], banks[t][:], ACT.Copy, scale=lam_t[:, 4 * t:4 * t + 1])
+                nc.scalar.activation(len_sb[hf][:, t, :], banks[t][:], ACT.Copy, scale=lam_t[:, t:t + 1])
+
+        w1_c = keep.tile([P, PASSES * H], U32, name="w1_c", align_bytes=64)
+        w1_s = keep.tile([P, PASSES * H], U8, name="w1_s", align_bytes=64)
+        w1_g = [keep.tile([P, 4 * H], BF16, name="w1_g0", align_bytes=64),
+                reuse.tile([P, 4 * H], BF16, name="w1_g1", offset=0, align_bytes=64)]
+
+        for a, hf, part in w1_late:
+            (nc.scalar.copy if (a, hf) == (0, 0) else nc.vector.tensor_copy)(
+                w1_g[a][:].rearrange("p (t m j) -> p m j t", t=4, j=4)[:, 64 * hf:64 * (hf + 1)],
+                part.rearrange("p j (m t) -> p m j t", t=4))
+            if (a, hf) == (1, 0):
+                nc.vector.quantize_mx(w1_c[:, 0:H].bitcast(FP8X4), w1_s[:, 0:H], w1_g[0][:])
+        for t in range(4):
+            nc.vector.quantize_mx(w1_c[:, H + t * P:H + (t + 1) * P].bitcast(FP8X4),
+                                  w1_s[:, H + t * P:H + (t + 1) * P], w1_g[1][:, t * 512:(t + 1) * 512])
 
         infer(0, (0, 1))
         infer(0, (2,))
@@ -142,35 +158,22 @@ def tile_list_clause_evaluator_kernel(
         for t in range(4):
             length(0, (t,))
 
-        w1_c = keep.tile([P, PASSES * H], U32, name="w1_c", align_bytes=64)
-        w1_s = keep.tile([P, PASSES * H], U8, name="w1_s", align_bytes=64)
-        w1_g = [keep.tile([P, 4 * H], BF16, name="w1_g%d" % a, tag="tab%d" % a, align_bytes=64) for a in range(PASSES)]
-        nc.vector.tensor_copy(
-            w1_g[0][:].rearrange("p (t q e j) -> p q t j e", t=4, e=4, j=4),
-            w1_first.rearrange("p (j q t e) -> p q t j e", t=4, e=4, j=4))
-        nc.vector.quantize_mx(w1_c[:, 0:H].bitcast(FP8X4), w1_s[:, 0:H], w1_g[0][:])
-        for u in range(2):
-            nc.vector.tensor_copy(
-                w1_g[1][:].rearrange("p (t q e j) -> p q t j e", t=4, e=4, j=4)[:, 16 * u:16 * (u + 1)],
-                w1_second[u].rearrange("p j (q t e) -> p q t j e", t=4, e=4))
-        for t in range(4):
-            nc.vector.quantize_mx(w1_c[:, H + t * P:H + (t + 1) * P].bitcast(FP8X4),
-                                  w1_s[:, H + t * P:H + (t + 1) * P], w1_g[1][:, t * 512:(t + 1) * 512])
-
         w4_g = keep.tile([P, 4 * N], BF16, name="w4_g", align_bytes=64)
-        w4_c = keep.tile([P, N], U32, name="w4_c", align_bytes=64)
+        w4_c = keep.tile([P, N], U32, name="w4_c", tag="tab0", align_bytes=64)
         w4_s = keep.tile([P, N], U8, name="w4_s", align_bytes=64)
 
         def round_w4():
             nc.scalar.copy(w4_g[:].rearrange("p (c i t) -> p c t i", i=4, t=4),
-                           w4_raw.rearrange("p (t c i) -> p c t i", i=4, t=4))
+                           w4_raw[:].rearrange("p (t c i) -> p c t i", i=4, t=4))
 
         def quantise_w4():
             for c0, c1 in ((0, 256), (256, 384)):
                 nc.vector.quantize_mx(w4_c[:, c0:c1].bitcast(FP8X4), w4_s[:, c0:c1], w4_g[:, 4 * c0:4 * c1])
 
-        h_c = {}
-        h_s = {}
+        round_w4()
+        quantise_w4()
+        h_c = keep.tile([P, S], U32, name="h_c", align_bytes=64)
+        h_s = keep.tile([P, S], U8, name="h_s", align_bytes=64)
 
         best_of = {}
         h_g_of = {}
@@ -206,9 +209,7 @@ def tile_list_clause_evaluator_kernel(
                 ALU.subtract)
 
         def quantise(c0, n):
-            h_c[c0] = keep.tile([P, n], U32, name="h_c%d" % c0, align_bytes=64)
-            h_s[c0] = keep.tile([P, n], U8, name="h_s%d" % c0, align_bytes=64)
-            nc.vector.quantize_mx(h_c[c0][:].bitcast(FP8X4), h_s[c0][:], h_g_of[c0][:])
+            nc.vector.quantize_mx(h_c[:, c0:c0 + n].bitcast(FP8X4), h_s[:, c0:c0 + n], h_g_of[c0][:])
 
         out_rows = out.rearrange("(m p) j -> p m j", p=P)
 
@@ -220,7 +221,7 @@ def tile_list_clause_evaluator_kernel(
             for m in range(3):
                 nc.tensor.matmul_mx(
                     accs[m], lhsT=w4_c[:, m * P:(m + 1) * P].bitcast(FP8X4), lhsT_scale=w4_s[:, m * P:(m + 1) * P],
-                    rhs=h_c[c0][:].bitcast(FP8X4), rhs_scale=h_s[c0][:], start=True, stop=True)
+                    rhs=h_c[:, c0:c0 + n].bitcast(FP8X4), rhs_scale=h_s[:, c0:c0 + n], start=True, stop=True)
             if on_vector:
                 nc.vector.tensor_tensor(
                     res[:], banks[0][:, 0:3 * n].rearrange("p (m c) -> p m c", m=3),
@@ -242,13 +243,10 @@ def tile_list_clause_evaluator_kernel(
         quantise(0, QUART)
         penalise(QUART, QUART)
         better_view(2)
-        round_w4()
         quantise(QUART, QUART)
         penalise(2 * QUART, QUART)
-        quantise_w4()
-        scores(0, QUART)
+        scores(0, HALF)
         better_view(3)
-        scores(QUART, QUART)
         quantise(2 * QUART, QUART)
         penalise(3 * QUART, P)
         scores(2 * QUART, QUART)

@@ -31,83 +31,90 @@ def tile_list_clause_evaluator_kernel(
         keep = ctx.enter_context(tc.tile_pool(name="keep", bufs=1))
         reuse = ctx.enter_context(tc.tile_pool(name="reuse", bufs=1))
         ring = ctx.enter_context(tc.tile_pool(name="ring", bufs=2))
-        psum = ctx.enter_context(tc.psum_pool(name="psum", bufs=4))
+        psum = ctx.enter_context(tc.psum_pool(name="psum", bufs=1))
+
+        def bank_tile(i):
+            return psum.tile([P, HALF], F32, name="bank%d" % i)
+
 
         offsets = keep.tile([P, S // 16], U16, name="offsets")
         nc.sync.dma_start(offsets[:], offs)
 
-        ts_win = keep.tile([P, T], U8, name="ts_win", tag="win_then_staged", align_bytes=64)
-        ws_raw = keep.tile([P, 2 * H], U8, name="ws_raw", tag="ws_then_late", align_bytes=64)
+        ts_win = keep.tile([P, T], U8, name="ts_win", align_bytes=64)
+        ws_raw = reuse.tile([P, 2 * H], U8, name="ws_raw", offset=3584, align_bytes=64)
         nc.vector.memset(ts_win[:].bitcast(I32), 0)
         nc.vector.memset(ws_raw[:].bitcast(I32), 0)
         planes = keep.tile([P, PASSES * SROW], U8, name="planes", align_bytes=64)
         nc.vector.memset(planes[:].bitcast(I32), 0)
 
-        nc.sync.dma_start(ts_win[0:P:4, :].bitcast(I32), tab_scales.bitcast(I32).rearrange("a q c -> q a c"))
         nc.sync.dma_start(ws_raw[0:P:4, 0:H].bitcast(I32), w2_scales.bitcast(I32).rearrange("a q c -> q a c"))
         nc.sync.dma_start(ws_raw[0:P:4, H:2 * H].bitcast(I32), w3_scales.bitcast(I32).rearrange("a q c -> q a c"))
+        nc.sync.dma_start(ts_win[0:P:4, :].bitcast(I32), tab_scales.bitcast(I32).rearrange("a q c -> q a c"))
 
-        lam_t = keep.tile([P, 4], F32, name="lam_t")
-        nc.sync.dma_start(lam_t[:], lam.rearrange("(p t) -> p t", t=4))
-        w2_raw = keep.tile([P, PASSES, H // 2], I32, name="w2_raw", tag="tab0", align_bytes=64)
-        w3_raw = reuse.tile([P, PASSES, H], I32, name="w3_raw", offset=6144, align_bytes=64)
+        lam_t = [keep.tile([P, 1], F32, name="lam%d" % t) for t in range(4)]
+        w2_raw = keep.tile([P, PASSES, H // 2], I32, name="w2_raw", align_bytes=64)
+        bo_tile = keep.tile([P, 3], F32, name="bo_tile")
+        bo_t = bo_tile[:]
+        with nc.allow_non_contiguous_dma(reason="one value a partition"):
+            for t in range(4):
+                nc.gpsimd.dma_start(lam_t[t][:], lam.rearrange("(b t q) -> t b q", t=4, q=8)[t])
+            nc.gpsimd.dma_start(bo_t, bo.rearrange("(m p) -> p m", p=P))
         nc.sync.dma_start(w2_raw[:], w2_words.bitcast(I32).rearrange("a p c -> p a c"))
-        nc.sync.dma_start(
-            w3_raw[:], w3_words.rearrange("a p c i -> a p (c i)").bitcast(I32).rearrange("a p c -> p a c"))
-        w4_raw = keep.tile([P, 4 * N], F32, name="w4_raw", align_bytes=64)
-        nc.sync.dma_start(w4_raw[:], w4.rearrange("(p t) n -> p (t n)", t=4))
-        w2_c = keep.tile([P, PASSES * H], U16, name="w2_c", align_bytes=64)
-        w3_c = keep.tile([P, PASSES * H], I32, name="w3_c", align_bytes=64)
-        nc.vector.tensor_copy(
-            w2_c[:].rearrange("p (a t m) -> p a m t", a=PASSES, t=4),
-            w2_raw[:].bitcast(U16).rearrange("p a (m t) -> p a m t", t=4))
-        nc.vector.tensor_copy(
-            w3_c[:].rearrange("p (a t m) -> p a m t", a=PASSES, t=4),
-            w3_raw[:].rearrange("p a (m t) -> p a m t", t=4))
         tab = []
         for a in range(PASSES):
-            if a == 0:
-                t_a = keep.tile([P, T], I32, name="tab0", tag="tab0", align_bytes=64)
-            else:
-                t_a = reuse.tile([P, T], I32, name="tab1", offset=0, align_bytes=64)
+            t_a = keep.tile([P, T], I32, name="tab%d" % a, align_bytes=64)
             nc.sync.dma_start(t_a[:], tab_words[a].rearrange("p t i -> p (t i)").bitcast(I32))
             tab.append(t_a)
+        w3_c = keep.tile([P, PASSES * H], I32, name="w3_c", align_bytes=64)
 
-        ts_got = reuse.tile([P, S], U8, name="ts_got", offset=8192, align_bytes=64)
-        nc.vector.tensor_copy(ts_got[:], ts_win[:].indirect(offsets[:]))
-        staged = keep.tile([P, SROW], U8, name="staged", tag="win_then_staged", align_bytes=64)
+        staged = keep.tile([P, SROW], U8, name="staged", align_bytes=64)
         staged_w = staged[:].bitcast(I32)
-        nc.vector.tensor_copy(staged_w[:, 0:S // 4], ts_got[:].bitcast(I32))
         nc.vector.tensor_copy(
-            staged[:, S:].rearrange("p (w t m) -> p w m t", w=2, t=4),
-            ws_raw[:].rearrange("p (w m t) -> p w m t", w=2, t=4))
+            staged_w[:, S // 4:].rearrange("p (w t b e) -> p w b t e", w=2, t=4, e=2),
+            ws_raw[:].bitcast(I32).rearrange("p (w b t e) -> p w b t e", w=2, t=4, e=2))
+        ts_got = reuse.tile([P, 6144], U8, name="ts_got", offset=3584, align_bytes=64)
+        nc.vector.tensor_copy(ts_got[:, 0:S], ts_win[:].indirect(offsets[:]))
+        nc.vector.tensor_copy(staged_w[:, 0:S // 4], ts_got[:, 0:S].bitcast(I32))
         for d in (0, 2, 1, 3):
             nc.sync.dma_start(
                 planes[32 * d:32 * d + 4, :].bitcast(I32).rearrange("p (a c) -> p a c", a=PASSES),
                 staged[32 * d:32 * d + 32:4, :].bitcast(I32))
 
-        late = keep.tile([P, 8 * H + 3], F32, name="late", tag="ws_then_late", align_bytes=64)
+        late = reuse.tile([P, 8 * H + 4 * N], F32, name="late", offset=9216, align_bytes=64)
+        w3_raw = reuse.tile([P, PASSES, H], I32, name="w3_raw", offset=0, align_bytes=64)
+        nc.sync.dma_start(
+            w3_raw[:], w3_words.rearrange("a p c i -> a p (c i)").bitcast(I32).rearrange("a p c -> p a c"))
         w1_late = []
         for u, (a, hf) in enumerate(((0, 0), (0, 1), (1, 0), (1, 1))):
             part = late[:, u * 2 * H:(u + 1) * 2 * H].rearrange("p (j c) -> p j c", j=4)
             nc.sync.dma_start(
                 part, w1[512 * a:512 * (a + 1), hf * (H // 2):(hf + 1) * (H // 2)].rearrange("(p j) c -> p j c", j=4))
             w1_late.append((a, hf, part))
-        bo_t = late[:, 8 * H:]
-        with nc.allow_non_contiguous_dma(reason="one value a partition"):
-            nc.sync.dma_start(bo_t, bo.rearrange("(m p) -> p m", p=P))
-
+        w4_raw = late[:, 8 * H:8 * H + 4 * N]
+        for t in range(4):
+            nc.sync.dma_start(w4_raw[:, t * N:(t + 1) * N], w4.rearrange("(b t q) n -> t b q n", t=4, q=8)[t])
 
         v = {}
-        got = reuse.tile([P, S], U32, name="v0", offset=8192, align_bytes=64)
-        nc.vector.tensor_copy(got[:], tab[0][:].bitcast(U32).indirect(offsets[:]))
-        for hf in range(2):
-            v[0, hf] = got[:, hf * HALF:(hf + 1) * HALF]
-        for hf in range(2):
-            got = keep.tile([P, HALF], U32, name="v1_%d" % hf, align_bytes=64)
-            nc.vector.tensor_copy(got[:], tab[1][:].bitcast(U32).indirect(offsets[:, 32 * hf:32 * (hf + 1)]))
-            v[1, hf] = got[:]
 
+        def gather(a, hf, tag):
+            if tag is None:
+                got = reuse.tile([P, HALF], U32, name="v00", offset=4096, align_bytes=64)
+            else:
+                got = keep.tile([P, HALF], U32, name="v%d_%d" % (a, hf), tag=tag, align_bytes=64)
+            nc.vector.tensor_copy(got[:], tab[a][:].bitcast(U32).indirect(offsets[:, 32 * hf:32 * (hf + 1)]))
+            v[a, hf] = got[:]
+
+        w2_c = reuse.tile([P, PASSES * H // 2], I32, name="w2_c", offset=6144, align_bytes=64)
+        nc.vector.tensor_copy(
+            w2_c[:].rearrange("p (a t b e) -> p a b t e", a=PASSES, t=4, e=4),
+            w2_raw[:].rearrange("p a (b t e) -> p a b t e", t=4, e=4))
+        gather(0, 0, None)
+        gather(1, 0, "v10")
+        gather(1, 1, "v11")
+        nc.vector.tensor_copy(
+            w3_c[:].rearrange("p (a t b q) -> p a b t q", a=PASSES, t=4, q=8),
+            w3_raw[:].rearrange("p a (b t q) -> p a b t q", t=4, q=8))
+        gather(0, 1, "tab1")
 
         def plane(a, c0, n):
             return planes[:, a * SROW + c0:a * SROW + c0 + n]
@@ -115,63 +122,66 @@ def tile_list_clause_evaluator_kernel(
         inf_sb = [keep.tile([P, 4, HALF], F32, name="inf%d" % hf, align_bytes=64) for hf in range(2)]
         len_sb = [keep.tile([P, 4, HALF], F32, name="len%d" % hf, align_bytes=64) for hf in range(2)]
 
-        def side_product(hf, ts, codes, per_word, dtype, scale_col):
-            banks = {t: psum.tile([P, HALF], F32, name="side_bank") for t in ts}
-            for a in range(PASSES):
-                for t in ts:
-                    c = a * H + t * P
-                    nc.tensor.matmul_mx(
-                        banks[t][:], lhsT=codes[:, c // per_word:(c + P) // per_word].bitcast(dtype),
-                        lhsT_scale=plane(a, scale_col + t * P, P),
-                        rhs=v[a, hf].bitcast(FP8X4), rhs_scale=plane(a, hf * HALF, HALF),
-                        start=(a == 0), stop=(a == PASSES - 1))
-            return banks
+        def side_pass(bank, a, hf, t, codes, width, dtype, scale_col):
+            c = (4 * a + t) * width
+            nc.tensor.matmul_mx(
+                bank[:], lhsT=codes[:, c:c + width].bitcast(dtype), lhsT_scale=plane(a, scale_col + t * P, P),
+                rhs=v[a, hf].bitcast(FP8X4), rhs_scale=plane(a, hf * HALF, HALF),
+                start=(a == 0), stop=(a == PASSES - 1))
+
+        def infer_pass(bank, a, hf, t):
+            side_pass(bank, a, hf, t, w2_c, P // 2, FP4X4, S)
+            if a == PASSES - 1:
+                nc.scalar.copy(inf_sb[hf][:, t, :], bank[:])
+
+        def length_pass(bank, a, hf, t):
+            side_pass(bank, a, hf, t, w3_c, P, FP8X4, S + H)
+            if a == PASSES - 1:
+                nc.scalar.activation(len_sb[hf][:, t, :], bank[:], ACT.Copy, scale=lam_t[t][:])
 
         def infer(hf, ts):
-            banks = side_product(hf, ts, w2_c, 1, FP4X4, S)
             for t in ts:
-                nc.scalar.copy(inf_sb[hf][:, t, :], banks[t][:])
+                bank = bank_tile(t)
+                for a in range(PASSES):
+                    infer_pass(bank, a, hf, t)
 
         def length(hf, ts):
-            banks = side_product(hf, ts, w3_c, 1, FP8X4, S + H)
             for t in ts:
-                nc.scalar.activation(len_sb[hf][:, t, :], banks[t][:], ACT.Copy, scale=lam_t[:, t:t + 1])
+                bank = bank_tile(4 + t)
+                for a in range(PASSES):
+                    length_pass(bank, a, hf, t)
+
+        infer(0, range(4))
+        length(0, range(4))
+        infer(1, range(4))
 
         w1_c = keep.tile([P, PASSES * H], U32, name="w1_c", align_bytes=64)
         w1_s = keep.tile([P, PASSES * H], U8, name="w1_s", align_bytes=64)
-        w1_g = [keep.tile([P, 4 * H], BF16, name="w1_g0", align_bytes=64),
-                reuse.tile([P, 4 * H], BF16, name="w1_g1", offset=0, align_bytes=64)]
+        w1_g = [keep.tile([P, 4 * H], BF16, name="w1_g0", tag="tab0", align_bytes=64),
+                keep.tile([P, 4 * H], BF16, name="w1_g1", align_bytes=64)]
 
         for a, hf, part in w1_late:
-            (nc.scalar.copy if (a, hf) == (0, 0) else nc.vector.tensor_copy)(
-                w1_g[a][:].rearrange("p (t m j) -> p m j t", t=4, j=4)[:, 64 * hf:64 * (hf + 1)],
-                part.rearrange("p j (m t) -> p m j t", t=4))
+            nc.vector.tensor_copy(
+                w1_g[a][:].rearrange("p (t b q j) -> p b t j q", t=4, q=8, j=4)[:, 8 * hf:8 * (hf + 1)],
+                part.rearrange("p j (b t q) -> p b t j q", t=4, q=8))
             if (a, hf) == (1, 0):
                 nc.vector.quantize_mx(w1_c[:, 0:H].bitcast(FP8X4), w1_s[:, 0:H], w1_g[0][:])
         for t in range(4):
             nc.vector.quantize_mx(w1_c[:, H + t * P:H + (t + 1) * P].bitcast(FP8X4),
                                   w1_s[:, H + t * P:H + (t + 1) * P], w1_g[1][:, t * 512:(t + 1) * 512])
 
-        infer(0, (0, 1))
-        infer(0, (2,))
-        infer(0, (3,))
-        for t in range(4):
-            length(0, (t,))
-
-        w4_g = keep.tile([P, 4 * N], BF16, name="w4_g", align_bytes=64)
-        w4_c = keep.tile([P, N], U32, name="w4_c", tag="tab0", align_bytes=64)
+        w4_g = reuse.tile([P, 4 * N], BF16, name="w4_g", offset=6144, align_bytes=64)
+        w4_c = keep.tile([P, N], U32, name="w4_c", align_bytes=64)
         w4_s = keep.tile([P, N], U8, name="w4_s", align_bytes=64)
 
         def round_w4():
             nc.scalar.copy(w4_g[:].rearrange("p (c i t) -> p c t i", i=4, t=4),
-                           w4_raw[:].rearrange("p (t c i) -> p c t i", i=4, t=4))
+                           w4_raw.rearrange("p (t c i) -> p c t i", i=4, t=4))
 
         def quantise_w4():
             for c0, c1 in ((0, 256), (256, 384)):
                 nc.vector.quantize_mx(w4_c[:, c0:c1].bitcast(FP8X4), w4_s[:, c0:c1], w4_g[:, 4 * c0:4 * c1])
 
-        round_w4()
-        quantise_w4()
         h_c = keep.tile([P, S], U32, name="h_c", align_bytes=64)
         h_s = keep.tile([P, S], U8, name="h_s", align_bytes=64)
 
@@ -180,10 +190,10 @@ def tile_list_clause_evaluator_kernel(
 
         def better_view(qt):
             hf, c0 = qt // 2, (qt % 2) * QUART
-            best = ring.tile([P, 4, QUART], F32, name="best", align_bytes=64)
+            best = ring.tile([P, 4, QUART], F32, name="best", align_bytes=64, bufs=3)
             best_of[qt] = best
             for u in range(2):
-                bank = psum.tile([P, HALF], F32, name="goal_bank")
+                bank = bank_tile((4 + 2 * qt + u) % 8)
                 for tt in range(2):
                     t = 2 * u + tt
                     for a in range(PASSES):
@@ -213,9 +223,9 @@ def tile_list_clause_evaluator_kernel(
 
         out_rows = out.rearrange("(m p) j -> p m j", p=P)
 
-        def scores(c0, n, on_vector=False):
+        def scores(c0, n, first_bank, on_vector=False):
             per_bank = HALF // n
-            banks = [psum.tile([P, HALF], F32, name="side_bank") for u in range(-(-3 // per_bank))]
+            banks = [bank_tile(first_bank + u) for u in range(-(-3 // per_bank))]
             res = keep.tile([P, 3, n], F32, name="res%d" % c0, align_bytes=64)
             accs = [banks[m // per_bank][:, (m % per_bank) * n:(m % per_bank + 1) * n] for m in range(3)]
             for m in range(3):
@@ -231,27 +241,26 @@ def tile_list_clause_evaluator_kernel(
                     nc.scalar.activation(res[:, m, :], accs[m], ACT.Identity, bias=bo_t[:, m:m + 1])
             nc.sync.dma_start(out_rows[:, :, c0:c0 + n], res[:])
 
-        infer(1, (0,))
-        infer(1, (1,))
         better_view(0)
-        infer(1, (2,))
-        infer(1, (3,))
-        penalise(0, QUART)
+        round_w4()
         better_view(1)
-        for t in range(4):
-            length(1, (t,))
+        penalise(0, QUART)
+        length(1, (0, 1))
         quantise(0, QUART)
         penalise(QUART, QUART)
+        quantise_w4()
+        length(1, (2, 3))
         better_view(2)
+        scores(0, QUART, 4)
         quantise(QUART, QUART)
         penalise(2 * QUART, QUART)
-        scores(0, HALF)
+        scores(QUART, QUART, 6)
         better_view(3)
         quantise(2 * QUART, QUART)
         penalise(3 * QUART, P)
-        scores(2 * QUART, QUART)
+        scores(2 * QUART, QUART, 0)
         penalise(3 * QUART + P, P)
         quantise(3 * QUART, P)
         quantise(3 * QUART + P, P)
-        scores(3 * QUART, P)
-        scores(3 * QUART + P, P, on_vector=True)
+        scores(3 * QUART, P, 4)
+        scores(3 * QUART + P, P, 5, on_vector=True)

@@ -33,32 +33,27 @@ def tile_list_clause_evaluator_kernel(
         ring = ctx.enter_context(tc.tile_pool(name="ring", bufs=2))
         psum = ctx.enter_context(tc.psum_pool(name="psum", bufs=1))
 
+        psum_banks = [psum.tile([P, HALF], F32, name="bank%d" % i) for i in range(8)]
+
         def bank_tile(i):
-            return psum.tile([P, HALF], F32, name="bank%d" % i)
+            return psum_banks[i]
 
 
         offsets = keep.tile([P, S // 16], U16, name="offsets")
         nc.sync.dma_start(offsets[:], offs)
 
         ts_win = keep.tile([P, T], U8, name="ts_win", align_bytes=64)
-        ws_raw = reuse.tile([P, 2 * H], U8, name="ws_raw", offset=3584, align_bytes=64)
+        ws_raw = keep.tile([P, 2 * H], U8, name="ws_raw", align_bytes=64)
         nc.vector.memset(ts_win[:].bitcast(I32), 0)
-        nc.vector.memset(ws_raw[:].bitcast(I32), 0)
+        nc.gpsimd.memset(ws_raw[:].bitcast(I32), 0)
         planes = keep.tile([P, PASSES * SROW], U8, name="planes", align_bytes=64)
-        nc.vector.memset(planes[:].bitcast(I32), 0)
+        nc.gpsimd.memset(planes[:].bitcast(I32), 0)
 
+        nc.sync.dma_start(ts_win[0:P:4, :].bitcast(I32), tab_scales.bitcast(I32).rearrange("a q c -> q a c"))
         nc.sync.dma_start(ws_raw[0:P:4, 0:H].bitcast(I32), w2_scales.bitcast(I32).rearrange("a q c -> q a c"))
         nc.sync.dma_start(ws_raw[0:P:4, H:2 * H].bitcast(I32), w3_scales.bitcast(I32).rearrange("a q c -> q a c"))
-        nc.sync.dma_start(ts_win[0:P:4, :].bitcast(I32), tab_scales.bitcast(I32).rearrange("a q c -> q a c"))
 
-        lam_t = [keep.tile([P, 1], F32, name="lam%d" % t) for t in range(4)]
         w2_raw = keep.tile([P, PASSES, H // 2], I32, name="w2_raw", align_bytes=64)
-        bo_tile = keep.tile([P, 3], F32, name="bo_tile")
-        bo_t = bo_tile[:]
-        with nc.allow_non_contiguous_dma(reason="one value a partition"):
-            for t in range(4):
-                nc.gpsimd.dma_start(lam_t[t][:], lam.rearrange("(b t q) -> t b q", t=4, q=8)[t])
-            nc.gpsimd.dma_start(bo_t, bo.rearrange("(m p) -> p m", p=P))
         nc.sync.dma_start(w2_raw[:], w2_words.bitcast(I32).rearrange("a p c -> p a c"))
         tab = []
         for a in range(PASSES):
@@ -69,38 +64,43 @@ def tile_list_clause_evaluator_kernel(
 
         staged = keep.tile([P, SROW], U8, name="staged", align_bytes=64)
         staged_w = staged[:].bitcast(I32)
+        ts_got = reuse.tile([P, 13888], U8, name="ts_got", offset=3584, align_bytes=64)
+        nc.vector.tensor_copy(ts_got[:, 0:S], ts_win[:].indirect(offsets[:]))
         nc.vector.tensor_copy(
             staged_w[:, S // 4:].rearrange("p (w t b e) -> p w b t e", w=2, t=4, e=2),
             ws_raw[:].bitcast(I32).rearrange("p (w b t e) -> p w b t e", w=2, t=4, e=2))
-        ts_got = reuse.tile([P, 6144], U8, name="ts_got", offset=3584, align_bytes=64)
-        nc.vector.tensor_copy(ts_got[:, 0:S], ts_win[:].indirect(offsets[:]))
         nc.vector.tensor_copy(staged_w[:, 0:S // 4], ts_got[:, 0:S].bitcast(I32))
         for d in (0, 2, 1, 3):
             nc.sync.dma_start(
                 planes[32 * d:32 * d + 4, :].bitcast(I32).rearrange("p (a c) -> p a c", a=PASSES),
                 staged[32 * d:32 * d + 32:4, :].bitcast(I32))
 
-        late = reuse.tile([P, 8 * H + 4 * N], F32, name="late", offset=9216, align_bytes=64)
+        late = reuse.tile([P, 4 * H + 4 * N + 3], F32, name="late", offset=17408, align_bytes=64)
+        w1_first = reuse.tile([P, 4 * H], F32, name="w1_first", offset=9216, align_bytes=64)
+        w1_raw = [w1_first[:], late[:, 0:4 * H]]
+        for a in range(PASSES):
+            nc.sync.dma_start(w1_raw[a], w1[512 * a:512 * (a + 1), :].rearrange("(p j) c -> p (j c)", j=4))
         w3_raw = reuse.tile([P, PASSES, H], I32, name="w3_raw", offset=0, align_bytes=64)
         nc.sync.dma_start(
             w3_raw[:], w3_words.rearrange("a p c i -> a p (c i)").bitcast(I32).rearrange("a p c -> p a c"))
-        w1_late = []
-        for u, (a, hf) in enumerate(((0, 0), (0, 1), (1, 0), (1, 1))):
-            part = late[:, u * 2 * H:(u + 1) * 2 * H].rearrange("p (j c) -> p j c", j=4)
-            nc.sync.dma_start(
-                part, w1[512 * a:512 * (a + 1), hf * (H // 2):(hf + 1) * (H // 2)].rearrange("(p j) c -> p j c", j=4))
-            w1_late.append((a, hf, part))
-        w4_raw = late[:, 8 * H:8 * H + 4 * N]
+        lam_t = [reuse.tile([P, 1], F32, name="lam%d" % t, offset=8192 + 64 * t, align_bytes=64) for t in range(4)]
+        with nc.allow_non_contiguous_dma(reason="one value a partition"):
+            for t in range(4):
+                nc.sync.dma_start(lam_t[t][:], lam.rearrange("(b t q) -> t b q", t=4, q=8)[t])
+        w4_raw = late[:, 4 * H:4 * H + 4 * N]
         for t in range(4):
             nc.sync.dma_start(w4_raw[:, t * N:(t + 1) * N], w4.rearrange("(b t q) n -> t b q n", t=4, q=8)[t])
+        bo_t = late[:, 4 * H + 4 * N:]
+        with nc.allow_non_contiguous_dma(reason="one value a partition"):
+            nc.sync.dma_start(bo_t, bo.rearrange("(m p) -> p m", p=P))
 
         v = {}
 
-        def gather(a, hf, tag):
-            if tag is None:
-                got = reuse.tile([P, HALF], U32, name="v00", offset=4096, align_bytes=64)
+        def gather(a, hf, offset):
+            if offset is None:
+                got = keep.tile([P, HALF], U32, name="v%d_%d" % (a, hf), align_bytes=64)
             else:
-                got = keep.tile([P, HALF], U32, name="v%d_%d" % (a, hf), tag=tag, align_bytes=64)
+                got = reuse.tile([P, HALF], U32, name="v%d_%d" % (a, hf), offset=offset, align_bytes=64)
             nc.vector.tensor_copy(got[:], tab[a][:].bitcast(U32).indirect(offsets[:, 32 * hf:32 * (hf + 1)]))
             v[a, hf] = got[:]
 
@@ -108,18 +108,18 @@ def tile_list_clause_evaluator_kernel(
         nc.vector.tensor_copy(
             w2_c[:].rearrange("p (a t b e) -> p a b t e", a=PASSES, t=4, e=4),
             w2_raw[:].rearrange("p a (b t e) -> p a b t e", t=4, e=4))
-        gather(0, 0, None)
-        gather(1, 0, "v10")
-        gather(1, 1, "v11")
-        nc.vector.tensor_copy(
-            w3_c[:].rearrange("p (a t b q) -> p a b t q", a=PASSES, t=4, q=8),
-            w3_raw[:].rearrange("p a (b t q) -> p a b t q", t=4, q=8))
-        gather(0, 1, "tab1")
+        gather(0, 0, 4096)
+        gather(1, 0, None)
+        gather(1, 1, None)
+        gather(0, 1, None)
 
         def plane(a, c0, n):
             return planes[:, a * SROW + c0:a * SROW + c0 + n]
 
-        inf_sb = [keep.tile([P, 4, HALF], F32, name="inf%d" % hf, align_bytes=64) for hf in range(2)]
+        inf_sb = {(0, 0): keep.tile([P, 2, HALF], F32, name="inf00", align_bytes=64),
+                  (0, 1): reuse.tile([P, 2, HALF], F32, name="inf01", offset=9216, align_bytes=64),
+                  (1, 0): reuse.tile([P, 2, HALF], F32, name="inf10", offset=9216 + 4096, align_bytes=64),
+                  (1, 1): keep.tile([P, 2, HALF], F32, name="inf11", align_bytes=64)}
         len_sb = [keep.tile([P, 4, HALF], F32, name="len%d" % hf, align_bytes=64) for hf in range(2)]
 
         def side_pass(bank, a, hf, t, codes, width, dtype, scale_col):
@@ -132,7 +132,7 @@ def tile_list_clause_evaluator_kernel(
         def infer_pass(bank, a, hf, t):
             side_pass(bank, a, hf, t, w2_c, P // 2, FP4X4, S)
             if a == PASSES - 1:
-                nc.scalar.copy(inf_sb[hf][:, t, :], bank[:])
+                nc.scalar.copy(inf_sb[hf, t // 2][:, t % 2, :], bank[:])
 
         def length_pass(bank, a, hf, t):
             side_pass(bank, a, hf, t, w3_c, P, FP8X4, S + H)
@@ -141,7 +141,7 @@ def tile_list_clause_evaluator_kernel(
 
         def infer(hf, ts):
             for t in ts:
-                bank = bank_tile(t)
+                bank = bank_tile(4 * hf + t)
                 for a in range(PASSES):
                     infer_pass(bank, a, hf, t)
 
@@ -151,32 +151,51 @@ def tile_list_clause_evaluator_kernel(
                 for a in range(PASSES):
                     length_pass(bank, a, hf, t)
 
-        infer(0, range(4))
-        length(0, range(4))
-        infer(1, range(4))
+        def length_quarter(qt, first_bank):
+            hf, c0 = qt // 2, (qt % 2) * QUART
+            for u in range(2):
+                bank = bank_tile(first_bank + u)
+                for tt in range(2):
+                    t = 2 * u + tt
+                    for a in range(PASSES):
+                        c = a * H + t * P
+                        nc.tensor.matmul_mx(
+                            bank[:, tt * QUART:(tt + 1) * QUART], lhsT=w3_c[:, c:c + P].bitcast(FP8X4),
+                            lhsT_scale=plane(a, S + H + t * P, P),
+                            rhs=v[a, hf][:, c0:c0 + QUART].bitcast(FP8X4),
+                            rhs_scale=plane(a, qt * QUART, QUART),
+                            start=(a == 0), stop=(a == PASSES - 1))
+                for tt in range(2):
+                    t = 2 * u + tt
+                    nc.scalar.activation(len_sb[hf][:, t, c0:c0 + QUART], bank[:, tt * QUART:(tt + 1) * QUART],
+                                         ACT.Copy, scale=lam_t[t][:])
+
 
         w1_c = keep.tile([P, PASSES * H], U32, name="w1_c", align_bytes=64)
         w1_s = keep.tile([P, PASSES * H], U8, name="w1_s", align_bytes=64)
-        w1_g = [keep.tile([P, 4 * H], BF16, name="w1_g0", tag="tab0", align_bytes=64),
+        w1_g = [keep.tile([P, 4 * H], BF16, name="w1_g0", align_bytes=64),
                 keep.tile([P, 4 * H], BF16, name="w1_g1", align_bytes=64)]
 
-        for a, hf, part in w1_late:
-            nc.vector.tensor_copy(
-                w1_g[a][:].rearrange("p (t b q j) -> p b t j q", t=4, q=8, j=4)[:, 8 * hf:8 * (hf + 1)],
-                part.rearrange("p j (b t q) -> p b t j q", t=4, q=8))
-            if (a, hf) == (1, 0):
-                nc.vector.quantize_mx(w1_c[:, 0:H].bitcast(FP8X4), w1_s[:, 0:H], w1_g[0][:])
-        for t in range(4):
-            nc.vector.quantize_mx(w1_c[:, H + t * P:H + (t + 1) * P].bitcast(FP8X4),
-                                  w1_s[:, H + t * P:H + (t + 1) * P], w1_g[1][:, t * 512:(t + 1) * 512])
+        for a, copy in enumerate((nc.scalar.copy, nc.vector.tensor_copy)):
+            for u in range(2):
+                copy(w1_g[a][:].rearrange("p (t b q j) -> p t b q j", t=4, q=8, j=4)[:, 2 * u:2 * u + 2],
+                     w1_raw[a].rearrange("p (j b t q) -> p t b q j", j=4, t=4, q=8)[:, 2 * u:2 * u + 2])
+        nc.vector.quantize_mx(w1_c[:, 0:H].bitcast(FP8X4), w1_s[:, 0:H], w1_g[0][:])
+        for u in range(2):
+            c = H + 2 * u * P
+            nc.vector.quantize_mx(w1_c[:, c:c + 2 * P].bitcast(FP8X4), w1_s[:, c:c + 2 * P],
+                                  w1_g[1][:, u * 1024:(u + 1) * 1024])
 
-        w4_g = reuse.tile([P, 4 * N], BF16, name="w4_g", offset=6144, align_bytes=64)
+        nc.vector.tensor_copy(
+            w3_c[:].rearrange("p (a t b q) -> p a b t q", a=PASSES, t=4, q=8),
+            w3_raw[:].rearrange("p a (b t q) -> p a b t q", t=4, q=8))
+        w4_g = keep.tile([P, 4 * N], BF16, name="w4_g", align_bytes=64)
         w4_c = keep.tile([P, N], U32, name="w4_c", align_bytes=64)
         w4_s = keep.tile([P, N], U8, name="w4_s", align_bytes=64)
 
         def round_w4():
-            nc.scalar.copy(w4_g[:].rearrange("p (c i t) -> p c t i", i=4, t=4),
-                           w4_raw.rearrange("p (t c i) -> p c t i", i=4, t=4))
+            nc.gpsimd.tensor_scalar(w4_g[:].rearrange("p (c t) -> p c t", t=4),
+                                    w4_raw.rearrange("p (t c) -> p c t", t=4), 1.0, 0.0, ALU.mult, ALU.add)
 
         def quantise_w4():
             for c0, c1 in ((0, 256), (256, 384)):
@@ -188,12 +207,12 @@ def tile_list_clause_evaluator_kernel(
         best_of = {}
         h_g_of = {}
 
-        def better_view(qt):
+        def better_view(qt, first_bank):
             hf, c0 = qt // 2, (qt % 2) * QUART
-            best = ring.tile([P, 4, QUART], F32, name="best", align_bytes=64, bufs=3)
+            best = ring.tile([P, 4, QUART], F32, name="best", align_bytes=64, bufs=4)
             best_of[qt] = best
             for u in range(2):
-                bank = bank_tile((4 + 2 * qt + u) % 8)
+                bank = bank_tile(first_bank + u)
                 for tt in range(2):
                     t = 2 * u + tt
                     for a in range(PASSES):
@@ -206,13 +225,13 @@ def tile_list_clause_evaluator_kernel(
                             start=(a == 0), stop=(a == PASSES - 1))
                 nc.vector.tensor_tensor(
                     best[:, 2 * u:2 * u + 2, :], bank[:].rearrange("p (t c) -> p t c", t=2),
-                    inf_sb[hf][:, 2 * u:2 * u + 2, c0:c0 + QUART], ALU.max)
+                    inf_sb[hf, u][:, :, c0:c0 + QUART], ALU.max)
 
-        def penalise(c0, n):
+        def penalise(c0, n, engine):
             best = best_of[c0 // QUART][:, :, c0 % QUART:c0 % QUART + n]
-            h_g = ring.tile([P, 4 * n], BF16, name="h_g", align_bytes=64, bufs=3)
+            h_g = ring.tile([P, 4 * n], BF16, name="h_g", align_bytes=64, bufs=5)
             h_g_of[c0] = h_g
-            nc.vector.tensor_tensor(
+            engine.tensor_tensor(
                 h_g[:].rearrange("p (c i t) -> p c t i", i=4, t=4),
                 best.rearrange("p t (c i) -> p c t i", i=4),
                 len_sb[c0 // HALF][:, :, c0 % HALF:c0 % HALF + n].rearrange("p t (c i) -> p c t i", i=4),
@@ -241,26 +260,30 @@ def tile_list_clause_evaluator_kernel(
                     nc.scalar.activation(res[:, m, :], accs[m], ACT.Identity, bias=bo_t[:, m:m + 1])
             nc.sync.dma_start(out_rows[:, :, c0:c0 + n], res[:])
 
-        better_view(0)
+        infer(0, range(4))
+        infer(1, range(4))
         round_w4()
-        better_view(1)
-        penalise(0, QUART)
-        length(1, (0, 1))
-        quantise(0, QUART)
-        penalise(QUART, QUART)
+        better_view(0, 0)
+        length_quarter(0, 4)
+        better_view(1, 2)
+        length_quarter(1, 6)
+        penalise(0, QUART, nc.vector)
+        better_view(2, 0)
         quantise_w4()
-        length(1, (2, 3))
-        better_view(2)
-        scores(0, QUART, 4)
+        quantise(0, QUART)
+        length_quarter(2, 4)
+        penalise(QUART, QUART, nc.vector)
+        better_view(3, 2)
+        scores(0, QUART, 0)
         quantise(QUART, QUART)
-        penalise(2 * QUART, QUART)
-        scores(QUART, QUART, 6)
-        better_view(3)
+        length_quarter(3, 6)
+        penalise(2 * QUART, QUART, nc.vector)
+        scores(QUART, QUART, 4)
+        penalise(3 * QUART, P, nc.vector)
         quantise(2 * QUART, QUART)
-        penalise(3 * QUART, P)
-        scores(2 * QUART, QUART, 0)
-        penalise(3 * QUART + P, P)
+        scores(2 * QUART, QUART, 2)
+        penalise(3 * QUART + P, P, nc.vector)
         quantise(3 * QUART, P)
         quantise(3 * QUART + P, P)
-        scores(3 * QUART, P, 4)
-        scores(3 * QUART + P, P, 5, on_vector=True)
+        scores(3 * QUART, P, 0)
+        scores(3 * QUART + P, P, 1, on_vector=True)

@@ -30,7 +30,6 @@ def tile_list_clause_evaluator_kernel(
     with ExitStack() as ctx:
         keep = ctx.enter_context(tc.tile_pool(name="keep", bufs=1))
         reuse = ctx.enter_context(tc.tile_pool(name="reuse", bufs=1))
-        ring = ctx.enter_context(tc.tile_pool(name="ring", bufs=2))
         psum = ctx.enter_context(tc.psum_pool(name="psum", bufs=1))
 
         psum_banks = [psum.tile([P, HALF], F32, name="bank%d" % i) for i in range(8)]
@@ -45,14 +44,21 @@ def tile_list_clause_evaluator_kernel(
         ts_win = keep.tile([P, T], U8, name="ts_win", align_bytes=64)
         ws_raw = keep.tile([P, 2 * H], U8, name="ws_raw", align_bytes=64)
         nc.vector.memset(ts_win[:].bitcast(I32), 0)
-        nc.gpsimd.memset(ws_raw[:].bitcast(I32), 0)
+        nc.vector.memset(ws_raw[:].bitcast(I32), 0)
         planes = keep.tile([P, PASSES * SROW], U8, name="planes", align_bytes=64)
-        nc.gpsimd.memset(planes[:].bitcast(I32), 0)
+        nc.vector.memset(planes[:].bitcast(I32), 0)
 
         nc.sync.dma_start(ts_win[0:P:4, :].bitcast(I32), tab_scales.bitcast(I32).rearrange("a q c -> q a c"))
         nc.sync.dma_start(ws_raw[0:P:4, 0:H].bitcast(I32), w2_scales.bitcast(I32).rearrange("a q c -> q a c"))
         nc.sync.dma_start(ws_raw[0:P:4, H:2 * H].bitcast(I32), w3_scales.bitcast(I32).rearrange("a q c -> q a c"))
 
+        lam_t = [keep.tile([P, 1], F32, name="lam%d" % t) for t in range(4)]
+        bo_tile = keep.tile([P, 3], F32, name="bo_tile")
+        bo_t = bo_tile[:]
+        with nc.allow_non_contiguous_dma(reason="one value a partition"):
+            for t in range(4):
+                nc.gpsimd.dma_start(lam_t[t][:], lam.rearrange("(b t q) -> t b q", t=4, q=8)[t])
+            nc.gpsimd.dma_start(bo_t, bo.rearrange("(m p) -> p m", p=P))
         w2_raw = keep.tile([P, PASSES, H // 2], I32, name="w2_raw", align_bytes=64)
         nc.sync.dma_start(w2_raw[:], w2_words.bitcast(I32).rearrange("a p c -> p a c"))
         tab = []
@@ -64,7 +70,7 @@ def tile_list_clause_evaluator_kernel(
 
         staged = keep.tile([P, SROW], U8, name="staged", align_bytes=64)
         staged_w = staged[:].bitcast(I32)
-        ts_got = reuse.tile([P, 13888], U8, name="ts_got", offset=3584, align_bytes=64)
+        ts_got = reuse.tile([P, 23104], U8, name="ts_got", offset=3584, align_bytes=64)
         nc.vector.tensor_copy(ts_got[:, 0:S], ts_win[:].indirect(offsets[:]))
         nc.vector.tensor_copy(
             staged_w[:, S // 4:].rearrange("p (w t b e) -> p w b t e", w=2, t=4, e=2),
@@ -75,24 +81,18 @@ def tile_list_clause_evaluator_kernel(
                 planes[32 * d:32 * d + 4, :].bitcast(I32).rearrange("p (a c) -> p a c", a=PASSES),
                 staged[32 * d:32 * d + 32:4, :].bitcast(I32))
 
-        late = reuse.tile([P, 4 * H + 4 * N + 3], F32, name="late", offset=17408, align_bytes=64)
-        w1_first = reuse.tile([P, 4 * H], F32, name="w1_first", offset=9216, align_bytes=64)
-        w1_raw = [w1_first[:], late[:, 0:4 * H]]
+        w1_first = reuse.tile([P, 4 * H], F32, name="w1_first", offset=10240, align_bytes=64)
+        w1_second = reuse.tile([P, 4 * H], F32, name="w1_second", offset=18432, align_bytes=64)
+        w1_raw = [w1_first[:], w1_second[:]]
         for a in range(PASSES):
             nc.sync.dma_start(w1_raw[a], w1[512 * a:512 * (a + 1), :].rearrange("(p j) c -> p (j c)", j=4))
         w3_raw = reuse.tile([P, PASSES, H], I32, name="w3_raw", offset=0, align_bytes=64)
         nc.sync.dma_start(
             w3_raw[:], w3_words.rearrange("a p c i -> a p (c i)").bitcast(I32).rearrange("a p c -> p a c"))
-        lam_t = [reuse.tile([P, 1], F32, name="lam%d" % t, offset=8192 + 64 * t, align_bytes=64) for t in range(4)]
-        with nc.allow_non_contiguous_dma(reason="one value a partition"):
-            for t in range(4):
-                nc.sync.dma_start(lam_t[t][:], lam.rearrange("(b t q) -> t b q", t=4, q=8)[t])
-        w4_raw = late[:, 4 * H:4 * H + 4 * N]
+        w4_tile = reuse.tile([P, 4 * N], F32, name="w4_tile", offset=26624, align_bytes=64)
+        w4_raw = w4_tile[:]
         for t in range(4):
             nc.sync.dma_start(w4_raw[:, t * N:(t + 1) * N], w4.rearrange("(b t q) n -> t b q n", t=4, q=8)[t])
-        bo_t = late[:, 4 * H + 4 * N:]
-        with nc.allow_non_contiguous_dma(reason="one value a partition"):
-            nc.sync.dma_start(bo_t, bo.rearrange("(m p) -> p m", p=P))
 
         v = {}
 
@@ -111,15 +111,15 @@ def tile_list_clause_evaluator_kernel(
         gather(0, 0, 4096)
         gather(1, 0, None)
         gather(1, 1, None)
-        gather(0, 1, None)
+        gather(0, 1, 8192)
 
         def plane(a, c0, n):
             return planes[:, a * SROW + c0:a * SROW + c0 + n]
 
         inf_sb = {(0, 0): keep.tile([P, 2, HALF], F32, name="inf00", align_bytes=64),
-                  (0, 1): reuse.tile([P, 2, HALF], F32, name="inf01", offset=9216, align_bytes=64),
-                  (1, 0): reuse.tile([P, 2, HALF], F32, name="inf10", offset=9216 + 4096, align_bytes=64),
-                  (1, 1): keep.tile([P, 2, HALF], F32, name="inf11", align_bytes=64)}
+                  (0, 1): keep.tile([P, 2, HALF], F32, name="inf01", align_bytes=64),
+                  (1, 0): reuse.tile([P, 2, HALF], F32, name="inf10", offset=18432, align_bytes=64),
+                  (1, 1): reuse.tile([P, 2, HALF], F32, name="inf11", offset=18432 + 4096, align_bytes=64)}
         len_sb = [keep.tile([P, 4, HALF], F32, name="len%d" % hf, align_bytes=64) for hf in range(2)]
 
         def side_pass(bank, a, hf, t, codes, width, dtype, scale_col):
@@ -139,9 +139,9 @@ def tile_list_clause_evaluator_kernel(
             if a == PASSES - 1:
                 nc.scalar.activation(len_sb[hf][:, t, :], bank[:], ACT.Copy, scale=lam_t[t][:])
 
-        def infer(hf, ts):
+        def infer(hf, ts, first_bank):
             for t in ts:
-                bank = bank_tile(4 * hf + t)
+                bank = bank_tile(first_bank + t - ts[0])
                 for a in range(PASSES):
                     infer_pass(bank, a, hf, t)
 
@@ -176,11 +176,13 @@ def tile_list_clause_evaluator_kernel(
         w1_g = [keep.tile([P, 4 * H], BF16, name="w1_g0", align_bytes=64),
                 keep.tile([P, 4 * H], BF16, name="w1_g1", align_bytes=64)]
 
-        for a, copy in enumerate((nc.scalar.copy, nc.vector.tensor_copy)):
+        for a in range(PASSES):
             for u in range(2):
-                copy(w1_g[a][:].rearrange("p (t b q j) -> p t b q j", t=4, q=8, j=4)[:, 2 * u:2 * u + 2],
-                     w1_raw[a].rearrange("p (j b t q) -> p t b q j", j=4, t=4, q=8)[:, 2 * u:2 * u + 2])
-        nc.vector.quantize_mx(w1_c[:, 0:H].bitcast(FP8X4), w1_s[:, 0:H], w1_g[0][:])
+                (nc.scalar.copy if (a, u) == (1, 1) else nc.vector.tensor_copy)(
+                    w1_g[a][:].rearrange("p (t b q j) -> p t b q j", t=4, q=8, j=4)[:, 2 * u:2 * u + 2],
+                    w1_raw[a].rearrange("p (j b t q) -> p t b q j", j=4, t=4, q=8)[:, 2 * u:2 * u + 2])
+            if a == 0:
+                nc.vector.quantize_mx(w1_c[:, 0:H].bitcast(FP8X4), w1_s[:, 0:H], w1_g[0][:])
         for u in range(2):
             c = H + 2 * u * P
             nc.vector.quantize_mx(w1_c[:, c:c + 2 * P].bitcast(FP8X4), w1_s[:, c:c + 2 * P],
@@ -190,14 +192,17 @@ def tile_list_clause_evaluator_kernel(
             w3_c[:].rearrange("p (a t b q) -> p a b t q", a=PASSES, t=4, q=8),
             w3_raw[:].rearrange("p a (b t q) -> p a b t q", t=4, q=8))
         w4_g = keep.tile([P, 4 * N], BF16, name="w4_g", align_bytes=64)
-        w4_c = keep.tile([P, N], U32, name="w4_c", align_bytes=64)
         w4_s = keep.tile([P, N], U8, name="w4_s", align_bytes=64)
 
+        w4_codes = []
+
         def round_w4():
-            nc.gpsimd.tensor_scalar(w4_g[:].rearrange("p (c t) -> p c t", t=4),
-                                    w4_raw.rearrange("p (t c) -> p c t", t=4), 1.0, 0.0, ALU.mult, ALU.add)
+            nc.scalar.copy(w4_g[:].rearrange("p (c i t) -> p c t i", i=4, t=4),
+                           w4_raw.rearrange("p (t c i) -> p c t i", i=4, t=4))
 
         def quantise_w4():
+            w4_c = keep.tile([P, N], U32, name="w4_c", tag="best0", align_bytes=64)
+            w4_codes.append(w4_c)
             for c0, c1 in ((0, 256), (256, 384)):
                 nc.vector.quantize_mx(w4_c[:, c0:c1].bitcast(FP8X4), w4_s[:, c0:c1], w4_g[:, 4 * c0:4 * c1])
 
@@ -209,7 +214,7 @@ def tile_list_clause_evaluator_kernel(
 
         def better_view(qt, first_bank):
             hf, c0 = qt // 2, (qt % 2) * QUART
-            best = ring.tile([P, 4, QUART], F32, name="best", align_bytes=64, bufs=4)
+            best = keep.tile([P, 4, QUART], F32, name="best%d" % qt, align_bytes=64)
             best_of[qt] = best
             for u in range(2):
                 bank = bank_tile(first_bank + u)
@@ -229,7 +234,8 @@ def tile_list_clause_evaluator_kernel(
 
         def penalise(c0, n, engine):
             best = best_of[c0 // QUART][:, :, c0 % QUART:c0 % QUART + n]
-            h_g = ring.tile([P, 4 * n], BF16, name="h_g", align_bytes=64, bufs=5)
+            h_g = keep.tile([P, 4 * n], BF16, name="h_g%d" % c0, tag="w4_g" if c0 == QUART else "h_g%d" % c0,
+                            align_bytes=64)
             h_g_of[c0] = h_g
             engine.tensor_tensor(
                 h_g[:].rearrange("p (c i t) -> p c t i", i=4, t=4),
@@ -249,7 +255,7 @@ def tile_list_clause_evaluator_kernel(
             accs = [banks[m // per_bank][:, (m % per_bank) * n:(m % per_bank + 1) * n] for m in range(3)]
             for m in range(3):
                 nc.tensor.matmul_mx(
-                    accs[m], lhsT=w4_c[:, m * P:(m + 1) * P].bitcast(FP8X4), lhsT_scale=w4_s[:, m * P:(m + 1) * P],
+                    accs[m], lhsT=w4_codes[0][:, m * P:(m + 1) * P].bitcast(FP8X4), lhsT_scale=w4_s[:, m * P:(m + 1) * P],
                     rhs=h_c[:, c0:c0 + n].bitcast(FP8X4), rhs_scale=h_s[:, c0:c0 + n], start=True, stop=True)
             if on_vector:
                 nc.vector.tensor_tensor(
@@ -260,30 +266,30 @@ def tile_list_clause_evaluator_kernel(
                     nc.scalar.activation(res[:, m, :], accs[m], ACT.Identity, bias=bo_t[:, m:m + 1])
             nc.sync.dma_start(out_rows[:, :, c0:c0 + n], res[:])
 
-        infer(0, range(4))
-        infer(1, range(4))
-        round_w4()
+        infer(0, (0, 1, 2, 3), 0)
+        infer(1, (0, 1, 2, 3), 4)
         better_view(0, 0)
         length_quarter(0, 4)
         better_view(1, 2)
+        round_w4()
         length_quarter(1, 6)
         penalise(0, QUART, nc.vector)
         better_view(2, 0)
         quantise_w4()
         quantise(0, QUART)
-        length_quarter(2, 4)
+        scores(0, QUART, 2)
         penalise(QUART, QUART, nc.vector)
-        better_view(3, 2)
-        scores(0, QUART, 0)
+        length_quarter(2, 4)
+        better_view(3, 0)
         quantise(QUART, QUART)
+        scores(QUART, QUART, 2)
         length_quarter(3, 6)
         penalise(2 * QUART, QUART, nc.vector)
-        scores(QUART, QUART, 4)
         penalise(3 * QUART, P, nc.vector)
         quantise(2 * QUART, QUART)
-        scores(2 * QUART, QUART, 2)
+        scores(2 * QUART, QUART, 4)
         penalise(3 * QUART + P, P, nc.vector)
         quantise(3 * QUART, P)
         quantise(3 * QUART + P, P)
-        scores(3 * QUART, P, 0)
-        scores(3 * QUART + P, P, 1, on_vector=True)
+        scores(3 * QUART, P, 6)
+        scores(3 * QUART + P, P, 7, on_vector=True)

@@ -116,11 +116,10 @@ def tile_list_clause_evaluator_kernel(
         def plane(a, c0, n):
             return planes[:, a * SROW + c0:a * SROW + c0 + n]
 
-        inf_sb = {(0, 0): keep.tile([P, 2, HALF], F32, name="inf00", align_bytes=64),
-                  (0, 1): keep.tile([P, 2, HALF], F32, name="inf01", align_bytes=64),
-                  (1, 0): reuse.tile([P, 2, HALF], F32, name="inf10", offset=18432, align_bytes=64),
-                  (1, 1): reuse.tile([P, 2, HALF], F32, name="inf11", offset=18432 + 4096, align_bytes=64)}
-        len_sb = [keep.tile([P, 4, HALF], F32, name="len%d" % hf, align_bytes=64) for hf in range(2)]
+        inf_sb = [keep.tile([P, 4, HALF], F32, name="inf0", align_bytes=64),
+                  reuse.tile([P, 4, HALF], F32, name="inf1", offset=18432, align_bytes=64)]
+        minus_lam = keep.tile([P, 4], F32, name="minus_lam")
+        length_banks = {}
 
         def side_pass(bank, a, hf, t, codes, width, dtype, scale_col):
             c = (4 * a + t) * width
@@ -132,24 +131,13 @@ def tile_list_clause_evaluator_kernel(
         def infer_pass(bank, a, hf, t):
             side_pass(bank, a, hf, t, w2_c, P // 2, FP4X4, S)
             if a == PASSES - 1:
-                nc.scalar.copy(inf_sb[hf, t // 2][:, t % 2, :], bank[:])
-
-        def length_pass(bank, a, hf, t):
-            side_pass(bank, a, hf, t, w3_c, P, FP8X4, S + H)
-            if a == PASSES - 1:
-                nc.scalar.activation(len_sb[hf][:, t, :], bank[:], ACT.Copy, scale=lam_t[t][:])
+                nc.scalar.copy(inf_sb[hf][:, t, :], bank[:])
 
         def infer(hf, ts, first_bank):
             for t in ts:
                 bank = bank_tile(first_bank + t - ts[0])
                 for a in range(PASSES):
                     infer_pass(bank, a, hf, t)
-
-        def length(hf, ts):
-            for t in ts:
-                bank = bank_tile(4 + t)
-                for a in range(PASSES):
-                    length_pass(bank, a, hf, t)
 
         def length_quarter(qt, first_bank):
             hf, c0 = qt // 2, (qt % 2) * QUART
@@ -165,10 +153,7 @@ def tile_list_clause_evaluator_kernel(
                             rhs=v[a, hf][:, c0:c0 + QUART].bitcast(FP8X4),
                             rhs_scale=plane(a, qt * QUART, QUART),
                             start=(a == 0), stop=(a == PASSES - 1))
-                for tt in range(2):
-                    t = 2 * u + tt
-                    nc.scalar.activation(len_sb[hf][:, t, c0:c0 + QUART], bank[:, tt * QUART:(tt + 1) * QUART],
-                                         ACT.Copy, scale=lam_t[t][:])
+                length_banks[qt, u] = bank
 
 
         w1_c = keep.tile([P, PASSES * H], U32, name="w1_c", align_bytes=64)
@@ -230,18 +215,36 @@ def tile_list_clause_evaluator_kernel(
                             start=(a == 0), stop=(a == PASSES - 1))
                 nc.vector.tensor_tensor(
                     best[:, 2 * u:2 * u + 2, :], bank[:].rearrange("p (t c) -> p t c", t=2),
-                    inf_sb[hf, u][:, :, c0:c0 + QUART], ALU.max)
+                    inf_sb[hf][:, 2 * u:2 * u + 2, c0:c0 + QUART], ALU.max)
 
-        def penalise(c0, n, engine):
-            best = best_of[c0 // QUART][:, :, c0 % QUART:c0 % QUART + n]
-            h_g = keep.tile([P, 4 * n], BF16, name="h_g%d" % c0, tag="w4_g" if c0 == QUART else "h_g%d" % c0,
-                            align_bytes=64)
+        def better_view_narrow(c0, bank_index):
+            hf, ch = c0 // HALF, c0 % HALF
+            if c0 % QUART == 0:
+                best_of[c0 // QUART] = keep.tile([P, 4, QUART], F32, name="best%d" % (c0 // QUART), align_bytes=64)
+            bank = bank_tile(bank_index)
+            for t in range(4):
+                for a in range(PASSES):
+                    c = a * H + t * P
+                    nc.tensor.matmul_mx(
+                        bank[:, t * P:(t + 1) * P], lhsT=w1_c[:, c:c + P].bitcast(FP8X4), lhsT_scale=w1_s[:, c:c + P],
+                        rhs=v[a, hf][:, ch:ch + P].bitcast(FP8X4), rhs_scale=plane(a, c0, P),
+                        start=(a == 0), stop=(a == PASSES - 1))
+            nc.vector.tensor_tensor(
+                best_of[c0 // QUART][:, :, c0 % QUART:c0 % QUART + P], bank[:].rearrange("p (t c) -> p t c", t=4),
+                inf_sb[hf][:, :, ch:ch + P], ALU.max)
+
+        def penalise(c0, n, interleave):
+            qt, cq = c0 // QUART, c0 % QUART
+            h_rows = keep.tile([P, 4, n], BF16, name="h_rows%d" % c0, align_bytes=64)
+            for t in range(4):
+                col = (t % 2) * QUART + cq
+                nc.vector.scalar_tensor_tensor(
+                    h_rows[:, t, :], length_banks[qt, t // 2][:, col:col + n], minus_lam[:, t:t + 1],
+                    best_of[qt][:, t, cq:cq + n], ALU.mult, ALU.add)
+            h_g = keep.tile([P, 4 * n], BF16, name="h_g%d" % c0, align_bytes=64)
             h_g_of[c0] = h_g
-            engine.tensor_tensor(
-                h_g[:].rearrange("p (c i t) -> p c t i", i=4, t=4),
-                best.rearrange("p t (c i) -> p c t i", i=4),
-                len_sb[c0 // HALF][:, :, c0 % HALF:c0 % HALF + n].rearrange("p t (c i) -> p c t i", i=4),
-                ALU.subtract)
+            interleave(h_g[:].rearrange("p (c i t) -> p c t i", i=4, t=4),
+                       h_rows[:].rearrange("p t (c i) -> p c t i", i=4))
 
         def quantise(c0, n):
             nc.vector.quantize_mx(h_c[:, c0:c0 + n].bitcast(FP8X4), h_s[:, c0:c0 + n], h_g_of[c0][:])
@@ -268,28 +271,31 @@ def tile_list_clause_evaluator_kernel(
 
         infer(0, (0, 1, 2, 3), 0)
         infer(1, (0, 1, 2, 3), 4)
+        for t in range(4):
+            nc.scalar.activation(minus_lam[:, t:t + 1], lam_t[t][:], ACT.Copy, scale=-1.0)
         better_view(0, 0)
         length_quarter(0, 4)
-        better_view(1, 2)
         round_w4()
+        penalise(0, QUART, nc.scalar.copy)
+        better_view(1, 2)
         length_quarter(1, 6)
-        penalise(0, QUART, nc.vector)
-        better_view(2, 0)
         quantise_w4()
         quantise(0, QUART)
         scores(0, QUART, 2)
-        penalise(QUART, QUART, nc.vector)
+        penalise(QUART, QUART, nc.scalar.copy)
+        better_view(2, 0)
         length_quarter(2, 4)
-        better_view(3, 0)
         quantise(QUART, QUART)
         scores(QUART, QUART, 2)
+        penalise(2 * QUART, QUART, nc.scalar.copy)
+        better_view_narrow(3 * QUART, 0)
         length_quarter(3, 6)
-        penalise(2 * QUART, QUART, nc.vector)
-        penalise(3 * QUART, P, nc.vector)
+        penalise(3 * QUART, P, nc.scalar.copy)
         quantise(2 * QUART, QUART)
         scores(2 * QUART, QUART, 4)
-        penalise(3 * QUART + P, P, nc.vector)
+        better_view_narrow(3 * QUART + P, 1)
         quantise(3 * QUART, P)
+        scores(3 * QUART, P, 0)
+        penalise(3 * QUART + P, P, nc.vector.tensor_copy)
         quantise(3 * QUART + P, P)
-        scores(3 * QUART, P, 6)
-        scores(3 * QUART + P, P, 7, on_vector=True)
+        scores(3 * QUART + P, P, 1, on_vector=True)

@@ -20,7 +20,17 @@ P = 128
 PASSES = 2
 HALF = 512
 QUART = 256
-SROW = S + 2 * H
+SROW = S + H
+
+W3_AT = 0
+V00_AT = 4096
+W2C_AT = 6144
+V01_AT = 8192
+W1_AT = (10240, 18432)
+W4_AT = 26624
+W3S_AT = 32768
+GATHERED_AT = V00_AT - 512
+GATHERED_BYTES = W3S_AT + 64 - GATHERED_AT
 
 
 def tile_list_clause_evaluator_kernel(
@@ -32,25 +42,20 @@ def tile_list_clause_evaluator_kernel(
         reuse = ctx.enter_context(tc.tile_pool(name="reuse", bufs=1))
         psum = ctx.enter_context(tc.psum_pool(name="psum", bufs=1))
 
-        psum_banks = [psum.tile([P, HALF], F32, name="bank%d" % i) for i in range(8)]
-
-        def bank_tile(i):
-            return psum_banks[i]
-
+        banks = [psum.tile([P, HALF], F32, name="bank%d" % i) for i in range(8)]
 
         offsets = keep.tile([P, S // 16], U16, name="offsets")
         nc.sync.dma_start(offsets[:], offs)
 
-        ts_win = keep.tile([P, T], U8, name="ts_win", align_bytes=64)
-        ws_raw = keep.tile([P, 2 * H], U8, name="ws_raw", align_bytes=64)
-        nc.vector.memset(ts_win[:].bitcast(I32), 0)
-        nc.vector.memset(ws_raw[:].bitcast(I32), 0)
-        planes = keep.tile([P, PASSES * SROW], U8, name="planes", align_bytes=64)
-        nc.vector.memset(planes[:].bitcast(I32), 0)
+        tab_scale_rows = keep.tile([P, T], U8, name="tab_scale_rows", align_bytes=64)
+        w2_scale_rows = keep.tile([P, H], U8, name="w2_scale_rows", align_bytes=64)
+        nc.vector.memset(tab_scale_rows[:].bitcast(I32), 0)
+        nc.vector.memset(w2_scale_rows[:].bitcast(I32), 0)
+        moved = keep.tile([P, PASSES * SROW], U8, name="moved", align_bytes=64)
+        nc.vector.memset(moved[:].bitcast(I32), 0)
 
-        nc.sync.dma_start(ts_win[0:P:4, :].bitcast(I32), tab_scales.bitcast(I32).rearrange("a q c -> q a c"))
-        nc.sync.dma_start(ws_raw[0:P:4, 0:H].bitcast(I32), w2_scales.bitcast(I32).rearrange("a q c -> q a c"))
-        nc.sync.dma_start(ws_raw[0:P:4, H:2 * H].bitcast(I32), w3_scales.bitcast(I32).rearrange("a q c -> q a c"))
+        nc.sync.dma_start(tab_scale_rows[0:P:4, :].bitcast(I32), tab_scales.bitcast(I32).rearrange("a q c -> q a c"))
+        nc.sync.dma_start(w2_scale_rows[0:P:4, 0:H].bitcast(I32), w2_scales.bitcast(I32).rearrange("a q c -> q a c"))
 
         lam_t = [keep.tile([P, 1], F32, name="lam%d" % t) for t in range(4)]
         bo_tile = keep.tile([P, 3], F32, name="bo_tile")
@@ -63,133 +68,131 @@ def tile_list_clause_evaluator_kernel(
         nc.sync.dma_start(w2_raw[:], w2_words.bitcast(I32).rearrange("a p c -> p a c"))
         tab = []
         for a in range(PASSES):
-            t_a = keep.tile([P, T], I32, name="tab%d" % a, align_bytes=64)
-            nc.sync.dma_start(t_a[:], tab_words[a].rearrange("p t i -> p (t i)").bitcast(I32))
-            tab.append(t_a)
+            tab_pass = keep.tile([P, T], I32, name="tab%d" % a, align_bytes=64)
+            nc.sync.dma_start(tab_pass[:], tab_words[a].rearrange("p t i -> p (t i)").bitcast(I32))
+            tab.append(tab_pass)
         w3_c = keep.tile([P, PASSES * H], I32, name="w3_c", align_bytes=64)
 
         staged = keep.tile([P, SROW], U8, name="staged", align_bytes=64)
         staged_w = staged[:].bitcast(I32)
-        ts_got = reuse.tile([P, 23104], U8, name="ts_got", offset=3584, align_bytes=64)
-        nc.vector.tensor_copy(ts_got[:, 0:S], ts_win[:].indirect(offsets[:]))
+        gathered = reuse.tile([P, GATHERED_BYTES], U8, name="gathered", offset=GATHERED_AT, align_bytes=64)
+        nc.vector.tensor_copy(gathered[:, 0:S], tab_scale_rows[:].indirect(offsets[:]))
         nc.vector.tensor_copy(
-            staged_w[:, S // 4:].rearrange("p (w t b e) -> p w b t e", w=2, t=4, e=2),
-            ws_raw[:].bitcast(I32).rearrange("p (w b t e) -> p w b t e", w=2, t=4, e=2))
-        nc.vector.tensor_copy(staged_w[:, 0:S // 4], ts_got[:, 0:S].bitcast(I32))
+            staged_w[:, S // 4:].rearrange("p (t b e) -> p b t e", t=4, e=2),
+            w2_scale_rows[:].bitcast(I32).rearrange("p (b t e) -> p b t e", t=4, e=2))
+        nc.vector.tensor_copy(staged_w[:, 0:S // 4], gathered[:, 0:S].bitcast(I32))
         for d in (0, 2, 1, 3):
             nc.sync.dma_start(
-                planes[32 * d:32 * d + 4, :].bitcast(I32).rearrange("p (a c) -> p a c", a=PASSES),
+                moved[32 * d:32 * d + 4, :].bitcast(I32).rearrange("p (a c) -> p a c", a=PASSES),
                 staged[32 * d:32 * d + 32:4, :].bitcast(I32))
 
-        w1_first = reuse.tile([P, 4 * H], F32, name="w1_first", offset=10240, align_bytes=64)
-        w1_second = reuse.tile([P, 4 * H], F32, name="w1_second", offset=18432, align_bytes=64)
-        w1_raw = [w1_first[:], w1_second[:]]
+        w1_raw = [reuse.tile([P, 4 * H], F32, name="w1_raw%d" % a, offset=W1_AT[a], align_bytes=64)[:]
+                  for a in range(PASSES)]
         for a in range(PASSES):
             nc.sync.dma_start(w1_raw[a], w1[512 * a:512 * (a + 1), :].rearrange("(p j) c -> p (j c)", j=4))
-        w3_raw = reuse.tile([P, PASSES, H], I32, name="w3_raw", offset=0, align_bytes=64)
+        w3_raw = reuse.tile([P, PASSES, H], I32, name="w3_raw", offset=W3_AT, align_bytes=64)
         nc.sync.dma_start(
             w3_raw[:], w3_words.rearrange("a p c i -> a p (c i)").bitcast(I32).rearrange("a p c -> p a c"))
-        w4_tile = reuse.tile([P, 4 * N], F32, name="w4_tile", offset=26624, align_bytes=64)
+        w3_scale_rows = reuse.tile([P, H], U8, name="w3_scale_rows", offset=W3S_AT, align_bytes=64)
+        nc.vector.memset(w3_scale_rows[:].bitcast(I32), 0)
+        for d in range(4):
+            nc.sync.dma_start(w3_scale_rows[32 * d + 4:32 * d + 12, :].bitcast(I32),
+                              w3_scales.bitcast(I32)[:, 4 * d:4 * d + 4, :])
+        w4_tile = reuse.tile([P, 4 * N], F32, name="w4_tile", offset=W4_AT, align_bytes=64)
         w4_raw = w4_tile[:]
         for t in range(4):
             nc.sync.dma_start(w4_raw[:, t * N:(t + 1) * N], w4.rearrange("(b t q) n -> t b q n", t=4, q=8)[t])
 
         v = {}
 
-        def gather(a, hf, offset):
-            if offset is None:
-                got = keep.tile([P, HALF], U32, name="v%d_%d" % (a, hf), align_bytes=64)
-            else:
-                got = reuse.tile([P, HALF], U32, name="v%d_%d" % (a, hf), offset=offset, align_bytes=64)
-            nc.vector.tensor_copy(got[:], tab[a][:].bitcast(U32).indirect(offsets[:, 32 * hf:32 * (hf + 1)]))
-            v[a, hf] = got[:]
+        def gather(a, hf, picked):
+            nc.vector.tensor_copy(picked[:], tab[a][:].bitcast(U32).indirect(offsets[:, 32 * hf:32 * (hf + 1)]))
+            v[a, hf] = picked[:]
 
-        w2_c = reuse.tile([P, PASSES * H // 2], I32, name="w2_c", offset=6144, align_bytes=64)
+        w2_c = reuse.tile([P, PASSES * H // 2], I32, name="w2_c", offset=W2C_AT, align_bytes=64)
         nc.vector.tensor_copy(
             w2_c[:].rearrange("p (a t b e) -> p a b t e", a=PASSES, t=4, e=4),
             w2_raw[:].rearrange("p a (b t e) -> p a b t e", t=4, e=4))
-        gather(0, 0, 4096)
-        gather(1, 0, None)
-        gather(1, 1, None)
-        gather(0, 1, 8192)
+        gather(0, 0, reuse.tile([P, HALF], U32, name="v0_0", offset=V00_AT, align_bytes=64))
+        gather(1, 0, keep.tile([P, HALF], U32, name="v1_0", align_bytes=64))
+        gather(1, 1, keep.tile([P, HALF], U32, name="v1_1", align_bytes=64))
+        gather(0, 1, reuse.tile([P, HALF], U32, name="v0_1", offset=V01_AT, align_bytes=64))
 
-        def plane(a, c0, n):
-            return planes[:, a * SROW + c0:a * SROW + c0 + n]
+        def moved_scales(a, c0, n):
+            return moved[:, a * SROW + c0:a * SROW + c0 + n]
 
         inf_sb = [keep.tile([P, 4, HALF], F32, name="inf0", align_bytes=64),
-                  reuse.tile([P, 4, HALF], F32, name="inf1", offset=18432, align_bytes=64)]
-        minus_lam = keep.tile([P, 4], F32, name="minus_lam")
+                  reuse.tile([P, 4, HALF], F32, name="inf1", offset=W1_AT[1] - 64, align_bytes=64)]
+        minus_lam = reuse.tile([P, 4], F32, name="minus_lam", offset=W4_AT - 64, align_bytes=64)
         length_banks = {}
 
-        def side_pass(bank, a, hf, t, codes, width, dtype, scale_col):
-            c = (4 * a + t) * width
-            nc.tensor.matmul_mx(
-                bank[:], lhsT=codes[:, c:c + width].bitcast(dtype), lhsT_scale=plane(a, scale_col + t * P, P),
-                rhs=v[a, hf].bitcast(FP8X4), rhs_scale=plane(a, hf * HALF, HALF),
-                start=(a == 0), stop=(a == PASSES - 1))
-
-        def infer_pass(bank, a, hf, t):
-            side_pass(bank, a, hf, t, w2_c, P // 2, FP4X4, S)
-            if a == PASSES - 1:
+        def infer(hf, first_bank):
+            for t in range(4):
+                bank = banks[first_bank + t]
+                for a in range(PASSES):
+                    c = (4 * a + t) * (P // 2)
+                    nc.tensor.matmul_mx(
+                        bank[:], lhsT=w2_c[:, c:c + P // 2].bitcast(FP4X4), lhsT_scale=moved_scales(a, S + t * P, P),
+                        rhs=v[a, hf].bitcast(FP8X4), rhs_scale=moved_scales(a, hf * HALF, HALF),
+                        start=(a == 0), stop=(a == PASSES - 1))
                 nc.scalar.copy(inf_sb[hf][:, t, :], bank[:])
 
-        def infer(hf, ts, first_bank):
-            for t in ts:
-                bank = bank_tile(first_bank + t - ts[0])
-                for a in range(PASSES):
-                    infer_pass(bank, a, hf, t)
+        def table_product(acc, codes, scales, c0, n):
+            hf, ch = c0 // HALF, c0 % HALF
+            for a in range(PASSES):
+                nc.tensor.matmul_mx(
+                    acc, lhsT=codes[a].bitcast(FP8X4), lhsT_scale=scales[a],
+                    rhs=v[a, hf][:, ch:ch + n].bitcast(FP8X4), rhs_scale=moved_scales(a, c0, n),
+                    start=(a == 0), stop=(a == PASSES - 1))
 
-        def length_quarter(qt, first_bank):
-            hf, c0 = qt // 2, (qt % 2) * QUART
-            for u in range(2):
-                bank = bank_tile(first_bank + u)
-                for tt in range(2):
-                    t = 2 * u + tt
-                    for a in range(PASSES):
-                        c = a * H + t * P
-                        nc.tensor.matmul_mx(
-                            bank[:, tt * QUART:(tt + 1) * QUART], lhsT=w3_c[:, c:c + P].bitcast(FP8X4),
-                            lhsT_scale=plane(a, S + H + t * P, P),
-                            rhs=v[a, hf][:, c0:c0 + QUART].bitcast(FP8X4),
-                            rhs_scale=plane(a, qt * QUART, QUART),
-                            start=(a == 0), stop=(a == PASSES - 1))
-                length_banks[qt, u] = bank
+        def tile_columns(operand, t):
+            return [operand[:, a * H + t * P:a * H + (t + 1) * P] for a in range(PASSES)]
 
+        def length(qt, first_bank):
+            for t in range(4):
+                bank = banks[first_bank + t // 2]
+                acc = bank[:, (t % 2) * QUART:(t % 2 + 1) * QUART]
+                table_product(acc, tile_columns(w3_c, t),
+                              [w3_s[4 + 4 * a:P, t * P:(t + 1) * P] for a in range(PASSES)], qt * QUART, QUART)
+                length_banks[qt, t // 2] = bank
 
         w1_c = keep.tile([P, PASSES * H], U32, name="w1_c", align_bytes=64)
         w1_s = keep.tile([P, PASSES * H], U8, name="w1_s", align_bytes=64)
-        w1_g = [keep.tile([P, 4 * H], BF16, name="w1_g0", align_bytes=64),
-                keep.tile([P, 4 * H], BF16, name="w1_g1", align_bytes=64)]
+        w1_g = [keep.tile([P, 4 * H], BF16, name="w1_g%d" % a, align_bytes=64) for a in range(PASSES)]
 
-        for a in range(PASSES):
-            for u in range(2):
-                (nc.scalar.copy if (a, u) == (1, 1) else nc.vector.tensor_copy)(
-                    w1_g[a][:].rearrange("p (t b q j) -> p t b q j", t=4, q=8, j=4)[:, 2 * u:2 * u + 2],
-                    w1_raw[a].rearrange("p (j b t q) -> p t b q j", j=4, t=4, q=8)[:, 2 * u:2 * u + 2])
-            if a == 0:
-                nc.vector.quantize_mx(w1_c[:, 0:H].bitcast(FP8X4), w1_s[:, 0:H], w1_g[0][:])
+        def round_w1(a, u, copy):
+            copy(w1_g[a][:].rearrange("p (t b q j) -> p t b q j", t=4, q=8, j=4)[:, 2 * u:2 * u + 2],
+                 w1_raw[a].rearrange("p (j b t q) -> p t b q j", j=4, t=4, q=8)[:, 2 * u:2 * u + 2])
+
+        round_w1(0, 0, nc.vector.tensor_copy)
+        round_w1(0, 1, nc.vector.tensor_copy)
+        nc.vector.quantize_mx(w1_c[:, 0:H].bitcast(FP8X4), w1_s[:, 0:H], w1_g[0][:])
+        round_w1(1, 0, nc.vector.tensor_copy)
+        round_w1(1, 1, nc.scalar.copy)
         for u in range(2):
             c = H + 2 * u * P
             nc.vector.quantize_mx(w1_c[:, c:c + 2 * P].bitcast(FP8X4), w1_s[:, c:c + 2 * P],
-                                  w1_g[1][:, u * 1024:(u + 1) * 1024])
+                                  w1_g[1][:, 4 * (c - H):4 * (c - H + 2 * P)])
 
         nc.vector.tensor_copy(
             w3_c[:].rearrange("p (a t b q) -> p a b t q", a=PASSES, t=4, q=8),
             w3_raw[:].rearrange("p a (b t q) -> p a b t q", t=4, q=8))
+        w3_s = keep.tile([P, H], U8, name="w3_s", align_bytes=64)
+        nc.vector.tensor_copy(
+            w3_s[:].bitcast(I32).rearrange("p (t b e) -> p b t e", t=4, e=2),
+            w3_scale_rows[:].bitcast(I32).rearrange("p (b t e) -> p b t e", t=4, e=2))
         w4_g = keep.tile([P, 4 * N], BF16, name="w4_g", align_bytes=64)
         w4_s = keep.tile([P, N], U8, name="w4_s", align_bytes=64)
-
-        w4_codes = []
 
         def round_w4():
             nc.scalar.copy(w4_g[:].rearrange("p (c i t) -> p c t i", i=4, t=4),
                            w4_raw.rearrange("p (t c i) -> p c t i", i=4, t=4))
 
         def quantise_w4():
-            w4_c = keep.tile([P, N], U32, name="w4_c", tag="best0", align_bytes=64)
-            w4_codes.append(w4_c)
-            for c0, c1 in ((0, 256), (256, 384)):
-                nc.vector.quantize_mx(w4_c[:, c0:c1].bitcast(FP8X4), w4_s[:, c0:c1], w4_g[:, 4 * c0:4 * c1])
+            codes = keep.tile([P, N], U32, name="w4_c", tag="best0", align_bytes=64)
+            for c0, c1 in ((0, 256), (256, N)):
+                nc.vector.quantize_mx(codes[:, c0:c1].bitcast(FP8X4), w4_s[:, c0:c1], w4_g[:, 4 * c0:4 * c1])
+            return codes
 
         h_c = keep.tile([P, S], U32, name="h_c", align_bytes=64)
         h_s = keep.tile([P, S], U8, name="h_s", align_bytes=64)
@@ -197,41 +200,19 @@ def tile_list_clause_evaluator_kernel(
         best_of = {}
         h_g_of = {}
 
-        def better_view(qt, first_bank):
-            hf, c0 = qt // 2, (qt % 2) * QUART
-            best = keep.tile([P, 4, QUART], F32, name="best%d" % qt, align_bytes=64)
-            best_of[qt] = best
-            for u in range(2):
-                bank = bank_tile(first_bank + u)
-                for tt in range(2):
-                    t = 2 * u + tt
-                    for a in range(PASSES):
-                        c = a * H + t * P
-                        nc.tensor.matmul_mx(
-                            bank[:, tt * QUART:(tt + 1) * QUART], lhsT=w1_c[:, c:c + P].bitcast(FP8X4),
-                            lhsT_scale=w1_s[:, c:c + P],
-                            rhs=v[a, hf][:, c0:c0 + QUART].bitcast(FP8X4),
-                            rhs_scale=plane(a, qt * QUART, QUART),
-                            start=(a == 0), stop=(a == PASSES - 1))
+        def better_view(c0, n, first_bank):
+            hf, ch, qt, cq = c0 // HALF, c0 % HALF, c0 // QUART, c0 % QUART
+            if cq == 0:
+                best_of[qt] = keep.tile([P, 4, QUART], F32, name="best%d" % qt, align_bytes=64)
+            per_bank = HALF // n
+            for t0 in range(0, 4, per_bank):
+                bank = banks[first_bank + t0 // per_bank]
+                for t in range(t0, t0 + per_bank):
+                    table_product(bank[:, (t - t0) * n:(t - t0 + 1) * n], tile_columns(w1_c, t), tile_columns(w1_s, t),
+                                  c0, n)
                 nc.vector.tensor_tensor(
-                    best[:, 2 * u:2 * u + 2, :], bank[:].rearrange("p (t c) -> p t c", t=2),
-                    inf_sb[hf][:, 2 * u:2 * u + 2, c0:c0 + QUART], ALU.max)
-
-        def better_view_narrow(c0, bank_index):
-            hf, ch = c0 // HALF, c0 % HALF
-            if c0 % QUART == 0:
-                best_of[c0 // QUART] = keep.tile([P, 4, QUART], F32, name="best%d" % (c0 // QUART), align_bytes=64)
-            bank = bank_tile(bank_index)
-            for t in range(4):
-                for a in range(PASSES):
-                    c = a * H + t * P
-                    nc.tensor.matmul_mx(
-                        bank[:, t * P:(t + 1) * P], lhsT=w1_c[:, c:c + P].bitcast(FP8X4), lhsT_scale=w1_s[:, c:c + P],
-                        rhs=v[a, hf][:, ch:ch + P].bitcast(FP8X4), rhs_scale=plane(a, c0, P),
-                        start=(a == 0), stop=(a == PASSES - 1))
-            nc.vector.tensor_tensor(
-                best_of[c0 // QUART][:, :, c0 % QUART:c0 % QUART + P], bank[:].rearrange("p (t c) -> p t c", t=4),
-                inf_sb[hf][:, :, ch:ch + P], ALU.max)
+                    best_of[qt][:, t0:t0 + per_bank, cq:cq + n], bank[:].rearrange("p (t c) -> p t c", t=per_bank),
+                    inf_sb[hf][:, t0:t0 + per_bank, ch:ch + n], ALU.max)
 
         def penalise(c0, n, interleave):
             qt, cq = c0 // QUART, c0 % QUART
@@ -251,51 +232,57 @@ def tile_list_clause_evaluator_kernel(
 
         out_rows = out.rearrange("(m p) j -> p m j", p=P)
 
-        def scores(c0, n, first_bank, on_vector=False):
+        def score_products(c0, n, first_bank):
             per_bank = HALF // n
-            banks = [bank_tile(first_bank + u) for u in range(-(-3 // per_bank))]
-            res = keep.tile([P, 3, n], F32, name="res%d" % c0, align_bytes=64)
-            accs = [banks[m // per_bank][:, (m % per_bank) * n:(m % per_bank + 1) * n] for m in range(3)]
+            accs = [banks[first_bank + m // per_bank][:, (m % per_bank) * n:(m % per_bank + 1) * n] for m in range(3)]
             for m in range(3):
                 nc.tensor.matmul_mx(
-                    accs[m], lhsT=w4_codes[0][:, m * P:(m + 1) * P].bitcast(FP8X4), lhsT_scale=w4_s[:, m * P:(m + 1) * P],
+                    accs[m], lhsT=w4_c[:, m * P:(m + 1) * P].bitcast(FP8X4), lhsT_scale=w4_s[:, m * P:(m + 1) * P],
                     rhs=h_c[:, c0:c0 + n].bitcast(FP8X4), rhs_scale=h_s[:, c0:c0 + n], start=True, stop=True)
-            if on_vector:
-                nc.vector.tensor_tensor(
-                    res[:], banks[0][:, 0:3 * n].rearrange("p (m c) -> p m c", m=3),
-                    bo_t.unsqueeze(2).broadcast_to([P, 3, n]), ALU.add)
-            else:
-                for m in range(3):
-                    nc.scalar.activation(res[:, m, :], accs[m], ACT.Identity, bias=bo_t[:, m:m + 1])
+            return accs
+
+        def scores(c0, n, first_bank):
+            res = keep.tile([P, 3, n], F32, name="res%d" % c0, align_bytes=64)
+            accs = score_products(c0, n, first_bank)
+            for m in range(3):
+                nc.scalar.activation(res[:, m, :], accs[m], ACT.Identity, bias=bo_t[:, m:m + 1])
             nc.sync.dma_start(out_rows[:, :, c0:c0 + n], res[:])
 
-        infer(0, (0, 1, 2, 3), 0)
-        infer(1, (0, 1, 2, 3), 4)
+        def last_scores(c0, bank_index):
+            res = keep.tile([P, 3, P], F32, name="res%d" % c0, align_bytes=64)
+            score_products(c0, P, bank_index)
+            nc.vector.tensor_tensor(
+                res[:], banks[bank_index][:, 0:3 * P].rearrange("p (m c) -> p m c", m=3),
+                bo_t.unsqueeze(2).broadcast_to([P, 3, P]), ALU.add)
+            nc.sync.dma_start(out_rows[:, :, c0:c0 + P], res[:])
+
+        infer(0, 0)
+        infer(1, 4)
         for t in range(4):
             nc.scalar.activation(minus_lam[:, t:t + 1], lam_t[t][:], ACT.Copy, scale=-1.0)
-        better_view(0, 0)
-        length_quarter(0, 4)
+        better_view(0, QUART, 0)
+        length(0, 4)
         round_w4()
         penalise(0, QUART, nc.scalar.copy)
-        better_view(1, 2)
-        length_quarter(1, 6)
-        quantise_w4()
+        better_view(QUART, QUART, 2)
+        length(1, 6)
+        w4_c = quantise_w4()
         quantise(0, QUART)
         scores(0, QUART, 2)
         penalise(QUART, QUART, nc.scalar.copy)
-        better_view(2, 0)
-        length_quarter(2, 4)
+        better_view(2 * QUART, QUART, 0)
+        length(2, 4)
         quantise(QUART, QUART)
         scores(QUART, QUART, 2)
         penalise(2 * QUART, QUART, nc.scalar.copy)
-        better_view_narrow(3 * QUART, 0)
-        length_quarter(3, 6)
+        better_view(3 * QUART, P, 0)
+        length(3, 6)
         penalise(3 * QUART, P, nc.scalar.copy)
         quantise(2 * QUART, QUART)
         scores(2 * QUART, QUART, 4)
-        better_view_narrow(3 * QUART + P, 1)
+        better_view(3 * QUART + P, P, 1)
         quantise(3 * QUART, P)
         scores(3 * QUART, P, 0)
         penalise(3 * QUART + P, P, nc.vector.tensor_copy)
         quantise(3 * QUART + P, P)
-        scores(3 * QUART + P, P, 1, on_vector=True)
+        last_scores(3 * QUART + P, 1)

@@ -20,17 +20,19 @@ P = 128
 PASSES = 2
 HALF = 512
 QUART = 256
-SROW = S + H
+SROW = S + 2 * H
 
-W3_AT = 0
-V00_AT = 4096
-W2C_AT = 6144
-V01_AT = 8192
-W1_AT = (10240, 18432)
-W4_AT = 26624
-W3S_AT = 32768
-GATHERED_AT = V00_AT - 512
-GATHERED_BYTES = W3S_AT + 64 - GATHERED_AT
+W1A_AT = 0
+V00_AT = 8192
+W1B_AT = V00_AT + 2048
+W3_AT = W1B_AT + 8192
+LAM_AT = W3_AT + 4096
+BO_AT = LAM_AT + 128
+W4_AT = BO_AT + 64
+TAB1_AT = W4_AT + 6144
+INF0_AT = TAB1_AT + 8192
+PICKED_AT = W1A_AT + 7168
+PICKED_BYTES = W4_AT + 64 - PICKED_AT
 
 
 def tile_list_clause_evaluator_kernel(
@@ -41,67 +43,60 @@ def tile_list_clause_evaluator_kernel(
         keep = ctx.enter_context(tc.tile_pool(name="keep", bufs=1))
         reuse = ctx.enter_context(tc.tile_pool(name="reuse", bufs=1))
         psum = ctx.enter_context(tc.psum_pool(name="psum", bufs=1))
-
         banks = [psum.tile([P, HALF], F32, name="bank%d" % i) for i in range(8)]
 
         offsets = keep.tile([P, S // 16], U16, name="offsets")
         nc.sync.dma_start(offsets[:], offs)
 
         tab_scale_rows = keep.tile([P, T], U8, name="tab_scale_rows", align_bytes=64)
-        w2_scale_rows = keep.tile([P, H], U8, name="w2_scale_rows", align_bytes=64)
         nc.vector.memset(tab_scale_rows[:].bitcast(I32), 0)
-        nc.vector.memset(w2_scale_rows[:].bitcast(I32), 0)
+        w_scale_rows = keep.tile([P, 2, H], U8, name="w_scale_rows", align_bytes=64)
+        nc.vector.memset(w_scale_rows[:].bitcast(I32), 0)
         moved = keep.tile([P, PASSES * SROW], U8, name="moved", align_bytes=64)
         nc.vector.memset(moved[:].bitcast(I32), 0)
 
         nc.sync.dma_start(tab_scale_rows[0:P:4, :].bitcast(I32), tab_scales.bitcast(I32).rearrange("a q c -> q a c"))
-        nc.sync.dma_start(w2_scale_rows[0:P:4, 0:H].bitcast(I32), w2_scales.bitcast(I32).rearrange("a q c -> q a c"))
-
-        lam_t = [keep.tile([P, 1], F32, name="lam%d" % t) for t in range(4)]
-        bo_tile = keep.tile([P, 3], F32, name="bo_tile")
-        bo_t = bo_tile[:]
-        with nc.allow_non_contiguous_dma(reason="one value a partition"):
-            for t in range(4):
-                nc.gpsimd.dma_start(lam_t[t][:], lam.rearrange("(b t q) -> t b q", t=4, q=8)[t])
-            nc.gpsimd.dma_start(bo_t, bo.rearrange("(m p) -> p m", p=P))
+        for hf, scales in enumerate((w2_scales, w3_scales)):
+            nc.sync.dma_start(w_scale_rows[0:P:4, hf, :].bitcast(I32), scales.bitcast(I32).rearrange("a q c -> q a c"))
         w2_raw = keep.tile([P, PASSES, H // 2], I32, name="w2_raw", align_bytes=64)
         nc.sync.dma_start(w2_raw[:], w2_words.bitcast(I32).rearrange("a p c -> p a c"))
-        tab = []
+        tab = [keep.tile([P, T], I32, name="tab0", align_bytes=64),
+               reuse.tile([P, T], I32, name="tab1", offset=TAB1_AT, align_bytes=64)]
         for a in range(PASSES):
-            tab_pass = keep.tile([P, T], I32, name="tab%d" % a, align_bytes=64)
-            nc.sync.dma_start(tab_pass[:], tab_words[a].rearrange("p t i -> p (t i)").bitcast(I32))
-            tab.append(tab_pass)
-        w3_c = keep.tile([P, PASSES * H], I32, name="w3_c", align_bytes=64)
+            nc.sync.dma_start(tab[a][:], tab_words[a].rearrange("p t i -> p (t i)").bitcast(I32))
 
         staged = keep.tile([P, SROW], U8, name="staged", align_bytes=64)
         staged_w = staged[:].bitcast(I32)
-        gathered = reuse.tile([P, GATHERED_BYTES], U8, name="gathered", offset=GATHERED_AT, align_bytes=64)
-        nc.vector.tensor_copy(gathered[:, 0:S], tab_scale_rows[:].indirect(offsets[:]))
+        picked = reuse.tile([P, PICKED_BYTES], U8, name="picked", offset=PICKED_AT, align_bytes=64)
+        nc.vector.tensor_copy(picked[:, 0:S], tab_scale_rows[:].indirect(offsets[:]))
         nc.vector.tensor_copy(
-            staged_w[:, S // 4:].rearrange("p (t b e) -> p b t e", t=4, e=2),
-            w2_scale_rows[:].bitcast(I32).rearrange("p (b t e) -> p b t e", t=4, e=2))
-        nc.vector.tensor_copy(staged_w[:, 0:S // 4], gathered[:, 0:S].bitcast(I32))
+            staged_w[:, S // 4:].rearrange("p (w t b e) -> p w b t e", w=2, t=4, e=2),
+            w_scale_rows[:].bitcast(I32).rearrange("p w (b t e) -> p w b t e", t=4, e=2))
+        nc.vector.tensor_copy(staged_w[:, 0:S // 4], picked[:, 0:S].bitcast(I32))
         for d in (0, 2, 1, 3):
             nc.sync.dma_start(
                 moved[32 * d:32 * d + 4, :].bitcast(I32).rearrange("p (a c) -> p a c", a=PASSES),
                 staged[32 * d:32 * d + 32:4, :].bitcast(I32))
-
-        w1_raw = [reuse.tile([P, 4 * H], F32, name="w1_raw%d" % a, offset=W1_AT[a], align_bytes=64)[:]
-                  for a in range(PASSES)]
+        w1_raw = []
         for a in range(PASSES):
-            nc.sync.dma_start(w1_raw[a], w1[512 * a:512 * (a + 1), :].rearrange("(p j) c -> p (j c)", j=4))
+            raw = reuse.tile([P, 4 * H], F32, name="w1_raw%d" % a, offset=(W1A_AT, W1B_AT)[a], align_bytes=64)
+            nc.sync.dma_start(raw[:], w1[512 * a:512 * (a + 1), :].rearrange("(p j) c -> p (j c)", j=4))
+            w1_raw.append(raw[:])
+
         w3_raw = reuse.tile([P, PASSES, H], I32, name="w3_raw", offset=W3_AT, align_bytes=64)
         nc.sync.dma_start(
             w3_raw[:], w3_words.rearrange("a p c i -> a p (c i)").bitcast(I32).rearrange("a p c -> p a c"))
-        w3_scale_rows = reuse.tile([P, H], U8, name="w3_scale_rows", offset=W3S_AT, align_bytes=64)
-        nc.vector.memset(w3_scale_rows[:].bitcast(I32), 0)
-        for d in range(4):
-            nc.sync.dma_start(w3_scale_rows[32 * d + 4:32 * d + 12, :].bitcast(I32),
-                              w3_scales.bitcast(I32)[:, 4 * d:4 * d + 4, :])
+        lam_t = [reuse.tile([P, 1], F32, name="lam%d" % t, offset=LAM_AT + 32 * t) for t in range(4)]
+        bo_tile = reuse.tile([P, 3], F32, name="bo_tile", offset=BO_AT)
+        bo_t = bo_tile[:]
         w4_tile = reuse.tile([P, 4 * N], F32, name="w4_tile", offset=W4_AT, align_bytes=64)
         w4_raw = w4_tile[:]
-        for t in range(4):
-            nc.sync.dma_start(w4_raw[:, t * N:(t + 1) * N], w4.rearrange("(b t q) n -> t b q n", t=4, q=8)[t])
+        with nc.allow_non_contiguous_dma(reason="one value a partition"):
+            for t in range(4):
+                nc.sync.dma_start(lam_t[t][:], lam.rearrange("(b t q) -> t b q", t=4, q=8)[t])
+            for t in range(4):
+                nc.sync.dma_start(w4_raw[:, t * N:(t + 1) * N], w4.rearrange("(b t q) n -> t b q n", t=4, q=8)[t])
+            nc.sync.dma_start(bo_t, bo.rearrange("(m p) -> p m", p=P))
 
         v = {}
 
@@ -109,52 +104,38 @@ def tile_list_clause_evaluator_kernel(
             nc.vector.tensor_copy(picked[:], tab[a][:].bitcast(U32).indirect(offsets[:, 32 * hf:32 * (hf + 1)]))
             v[a, hf] = picked[:]
 
-        w2_c = reuse.tile([P, PASSES * H // 2], I32, name="w2_c", offset=W2C_AT, align_bytes=64)
+        w2_c = keep.tile([P, PASSES * H // 2], I32, name="w2_c", align_bytes=64)
         nc.vector.tensor_copy(
             w2_c[:].rearrange("p (a t b e) -> p a b t e", a=PASSES, t=4, e=4),
             w2_raw[:].rearrange("p a (b t e) -> p a b t e", t=4, e=4))
         gather(0, 0, reuse.tile([P, HALF], U32, name="v0_0", offset=V00_AT, align_bytes=64))
         gather(1, 0, keep.tile([P, HALF], U32, name="v1_0", align_bytes=64))
         gather(1, 1, keep.tile([P, HALF], U32, name="v1_1", align_bytes=64))
-        gather(0, 1, reuse.tile([P, HALF], U32, name="v0_1", offset=V01_AT, align_bytes=64))
+        gather(0, 1, reuse.tile([P, HALF], U32, name="v0_1", offset=TAB1_AT, align_bytes=64))
 
-        def moved_scales(a, c0, n):
-            return moved[:, a * SROW + c0:a * SROW + c0 + n]
+        def table_scales(a, c0, n):
+            c = a * SROW + c0
+            return moved[:, c:c + n]
 
-        inf_sb = [keep.tile([P, 4, HALF], F32, name="inf0", align_bytes=64),
-                  reuse.tile([P, 4, HALF], F32, name="inf1", offset=W1_AT[1] - 64, align_bytes=64)]
-        minus_lam = reuse.tile([P, 4], F32, name="minus_lam", offset=W4_AT - 64, align_bytes=64)
-        length_banks = {}
+        def weight_scales(which, a, t):
+            c = a * SROW + S + which * H + t * P
+            return moved[:, c:c + P]
 
-        def infer(hf, first_bank):
-            for t in range(4):
-                bank = banks[first_bank + t]
-                for a in range(PASSES):
-                    c = (4 * a + t) * (P // 2)
-                    nc.tensor.matmul_mx(
-                        bank[:], lhsT=w2_c[:, c:c + P // 2].bitcast(FP4X4), lhsT_scale=moved_scales(a, S + t * P, P),
-                        rhs=v[a, hf].bitcast(FP8X4), rhs_scale=moved_scales(a, hf * HALF, HALF),
-                        start=(a == 0), stop=(a == PASSES - 1))
-                nc.scalar.copy(inf_sb[hf][:, t, :], bank[:])
+        inf_sb = [reuse.tile([P, 4, HALF], F32, name="inf0", offset=INF0_AT, align_bytes=64),
+                  reuse.tile([P, 4, HALF], F32, name="inf1", offset=W1B_AT, align_bytes=64)]
 
-        def table_product(acc, codes, scales, c0, n):
+        def one_pass(acc, codes, scales, a, c0, n):
             hf, ch = c0 // HALF, c0 % HALF
-            for a in range(PASSES):
-                nc.tensor.matmul_mx(
-                    acc, lhsT=codes[a].bitcast(FP8X4), lhsT_scale=scales[a],
-                    rhs=v[a, hf][:, ch:ch + n].bitcast(FP8X4), rhs_scale=moved_scales(a, c0, n),
-                    start=(a == 0), stop=(a == PASSES - 1))
+            nc.tensor.matmul_mx(
+                acc, lhsT=codes, lhsT_scale=scales, rhs=v[a, hf][:, ch:ch + n].bitcast(FP8X4),
+                rhs_scale=table_scales(a, c0, n), start=(a == 0), stop=(a == PASSES - 1))
 
-        def tile_columns(operand, t):
-            return [operand[:, a * H + t * P:a * H + (t + 1) * P] for a in range(PASSES)]
+        def infer_pass(a, hf, t, bank):
+            c = (4 * a + t) * (P // 2)
+            one_pass(banks[bank][:], w2_c[:, c:c + P // 2].bitcast(FP4X4), weight_scales(0, a, t), a, hf * HALF, HALF)
 
-        def length(qt, first_bank):
-            for t in range(4):
-                bank = banks[first_bank + t // 2]
-                acc = bank[:, (t % 2) * QUART:(t % 2 + 1) * QUART]
-                table_product(acc, tile_columns(w3_c, t),
-                              [w3_s[4 + 4 * a:P, t * P:(t + 1) * P] for a in range(PASSES)], qt * QUART, QUART)
-                length_banks[qt, t // 2] = bank
+        def infer_copy(hf, t, bank):
+            nc.scalar.copy(inf_sb[hf][:, t, :], banks[bank][:])
 
         w1_c = keep.tile([P, PASSES * H], U32, name="w1_c", align_bytes=64)
         w1_s = keep.tile([P, PASSES * H], U8, name="w1_s", align_bytes=64)
@@ -164,71 +145,63 @@ def tile_list_clause_evaluator_kernel(
             copy(w1_g[a][:].rearrange("p (t b q j) -> p t b q j", t=4, q=8, j=4)[:, 2 * u:2 * u + 2],
                  w1_raw[a].rearrange("p (j b t q) -> p t b q j", j=4, t=4, q=8)[:, 2 * u:2 * u + 2])
 
-        round_w1(0, 0, nc.vector.tensor_copy)
-        round_w1(0, 1, nc.vector.tensor_copy)
-        nc.vector.quantize_mx(w1_c[:, 0:H].bitcast(FP8X4), w1_s[:, 0:H], w1_g[0][:])
-        round_w1(1, 0, nc.vector.tensor_copy)
-        round_w1(1, 1, nc.scalar.copy)
-        for u in range(2):
-            c = H + 2 * u * P
-            nc.vector.quantize_mx(w1_c[:, c:c + 2 * P].bitcast(FP8X4), w1_s[:, c:c + 2 * P],
-                                  w1_g[1][:, 4 * (c - H):4 * (c - H + 2 * P)])
+        def quantise_w1(c, n):
+            a, cg = c // H, c % H
+            nc.vector.quantize_mx(w1_c[:, c:c + n].bitcast(FP8X4), w1_s[:, c:c + n], w1_g[a][:, 4 * cg:4 * (cg + n)])
 
-        nc.vector.tensor_copy(
-            w3_c[:].rearrange("p (a t b q) -> p a b t q", a=PASSES, t=4, q=8),
-            w3_raw[:].rearrange("p a (b t q) -> p a b t q", t=4, q=8))
-        w3_s = keep.tile([P, H], U8, name="w3_s", align_bytes=64)
-        nc.vector.tensor_copy(
-            w3_s[:].bitcast(I32).rearrange("p (t b e) -> p b t e", t=4, e=2),
-            w3_scale_rows[:].bitcast(I32).rearrange("p (b t e) -> p b t e", t=4, e=2))
-        w4_g = keep.tile([P, 4 * N], BF16, name="w4_g", align_bytes=64)
+        def goal_pass(a, hf, t, bank):
+            c = a * H + t * P
+            one_pass(banks[bank][:], w1_c[:, c:c + P].bitcast(FP8X4), w1_s[:, c:c + P], a, hf * HALF, HALF)
+
+        best = [keep.tile([P, 4, HALF], F32, name="best%d" % hf, align_bytes=64) for hf in range(2)]
+
+        def maximum(hf, t, bank):
+            nc.vector.tensor_tensor(best[hf][:, t, :], banks[bank][:], inf_sb[hf][:, t, :], ALU.max)
+
+        w3_c = keep.tile([P, PASSES * H], I32, name="w3_c", align_bytes=64)
+
+        def order_w3():
+            nc.vector.tensor_copy(
+                w3_c[:].rearrange("p (a t b q) -> p a b t q", a=PASSES, t=4, q=8),
+                w3_raw[:].rearrange("p a (b t q) -> p a b t q", t=4, q=8))
+
+        weighted = [keep.tile([P, 4, QUART], F32, name="weighted%d" % qt, align_bytes=64) for qt in range(4)]
+
+        def length(qt, pair, bank):
+            for t in (2 * pair, 2 * pair + 1):
+                for a in range(PASSES):
+                    c = a * H + t * P
+                    one_pass(banks[bank][:, (t % 2) * QUART:(t % 2 + 1) * QUART], w3_c[:, c:c + P].bitcast(FP8X4),
+                             weight_scales(1, a, t), a, qt * QUART, QUART)
+            for t in (2 * pair, 2 * pair + 1):
+                nc.scalar.activation(weighted[qt][:, t, :], banks[bank][:, (t % 2) * QUART:(t % 2 + 1) * QUART],
+                                     ACT.Copy, scale=lam_t[t][:])
+
+        w4_g = reuse.tile([P, 4 * N], BF16, name="w4_g", offset=INF0_AT, align_bytes=64)
+        w4_c = keep.tile([P, N], U32, name="w4_c", align_bytes=64)
         w4_s = keep.tile([P, N], U8, name="w4_s", align_bytes=64)
 
-        def round_w4():
-            nc.scalar.copy(w4_g[:].rearrange("p (c i t) -> p c t i", i=4, t=4),
-                           w4_raw.rearrange("p (t c i) -> p c t i", i=4, t=4))
+        def round_w4(m):
+            nc.scalar.copy(w4_g[:].rearrange("p (c i t) -> p c t i", i=4, t=4)[:, 32 * m:32 * (m + 1)],
+                           w4_raw.rearrange("p (t c i) -> p c t i", i=4, t=4)[:, 32 * m:32 * (m + 1)])
 
         def quantise_w4():
-            codes = keep.tile([P, N], U32, name="w4_c", tag="best0", align_bytes=64)
             for c0, c1 in ((0, 256), (256, N)):
-                nc.vector.quantize_mx(codes[:, c0:c1].bitcast(FP8X4), w4_s[:, c0:c1], w4_g[:, 4 * c0:4 * c1])
-            return codes
+                nc.vector.quantize_mx(w4_c[:, c0:c1].bitcast(FP8X4), w4_s[:, c0:c1], w4_g[:, 4 * c0:4 * c1])
 
+        h_g = keep.tile([P, 4 * S], BF16, name="h_g", align_bytes=64)
         h_c = keep.tile([P, S], U32, name="h_c", align_bytes=64)
         h_s = keep.tile([P, S], U8, name="h_s", align_bytes=64)
 
-        best_of = {}
-        h_g_of = {}
-
-        def better_view(c0, n, first_bank):
+        def penalise(c0, n):
             hf, ch, qt, cq = c0 // HALF, c0 % HALF, c0 // QUART, c0 % QUART
-            if cq == 0:
-                best_of[qt] = keep.tile([P, 4, QUART], F32, name="best%d" % qt, align_bytes=64)
-            per_bank = HALF // n
-            for t0 in range(0, 4, per_bank):
-                bank = banks[first_bank + t0 // per_bank]
-                for t in range(t0, t0 + per_bank):
-                    table_product(bank[:, (t - t0) * n:(t - t0 + 1) * n], tile_columns(w1_c, t), tile_columns(w1_s, t),
-                                  c0, n)
-                nc.vector.tensor_tensor(
-                    best_of[qt][:, t0:t0 + per_bank, cq:cq + n], bank[:].rearrange("p (t c) -> p t c", t=per_bank),
-                    inf_sb[hf][:, t0:t0 + per_bank, ch:ch + n], ALU.max)
-
-        def penalise(c0, n, interleave):
-            qt, cq = c0 // QUART, c0 % QUART
-            h_rows = keep.tile([P, 4, n], BF16, name="h_rows%d" % c0, align_bytes=64)
-            for t in range(4):
-                col = (t % 2) * QUART + cq
-                nc.vector.scalar_tensor_tensor(
-                    h_rows[:, t, :], length_banks[qt, t // 2][:, col:col + n], minus_lam[:, t:t + 1],
-                    best_of[qt][:, t, cq:cq + n], ALU.mult, ALU.add)
-            h_g = keep.tile([P, 4 * n], BF16, name="h_g%d" % c0, align_bytes=64)
-            h_g_of[c0] = h_g
-            interleave(h_g[:].rearrange("p (c i t) -> p c t i", i=4, t=4),
-                       h_rows[:].rearrange("p t (c i) -> p c t i", i=4))
+            nc.vector.tensor_tensor(
+                h_g[:, 4 * c0:4 * (c0 + n)].rearrange("p (c i t) -> p c t i", i=4, t=4),
+                best[hf][:, :, ch:ch + n].rearrange("p t (c i) -> p c t i", i=4),
+                weighted[qt][:, :, cq:cq + n].rearrange("p t (c i) -> p c t i", i=4), ALU.subtract)
 
         def quantise(c0, n):
-            nc.vector.quantize_mx(h_c[:, c0:c0 + n].bitcast(FP8X4), h_s[:, c0:c0 + n], h_g_of[c0][:])
+            nc.vector.quantize_mx(h_c[:, c0:c0 + n].bitcast(FP8X4), h_s[:, c0:c0 + n], h_g[:, 4 * c0:4 * (c0 + n)])
 
         out_rows = out.rearrange("(m p) j -> p m j", p=P)
 
@@ -256,33 +229,63 @@ def tile_list_clause_evaluator_kernel(
                 bo_t.unsqueeze(2).broadcast_to([P, 3, P]), ALU.add)
             nc.sync.dma_start(out_rows[:, :, c0:c0 + P], res[:])
 
-        infer(0, 0)
-        infer(1, 4)
+        for a in range(PASSES):
+            for t in range(4):
+                infer_pass(a, 0, t, t)
         for t in range(4):
-            nc.scalar.activation(minus_lam[:, t:t + 1], lam_t[t][:], ACT.Copy, scale=-1.0)
-        better_view(0, QUART, 0)
-        length(0, 4)
-        round_w4()
-        penalise(0, QUART, nc.scalar.copy)
-        better_view(QUART, QUART, 2)
-        length(1, 6)
-        w4_c = quantise_w4()
+            infer_copy(0, t, t)
+        round_w1(0, 0, nc.vector.tensor_copy)
+        round_w1(0, 1, nc.vector.tensor_copy)
+        quantise_w1(0, H)
+        round_w1(1, 0, nc.vector.tensor_copy)
+        round_w1(1, 1, nc.scalar.copy)
+        for t in range(2):
+            for a in range(PASSES):
+                infer_pass(a, 1, t, t)
+            infer_copy(1, t, t)
+        for t in range(4):
+            goal_pass(0, 0, t, 4 + t)
+        quantise_w1(H, 2 * P)
+        quantise_w1(H + 2 * P, 2 * P)
+        for t in range(4):
+            goal_pass(1, 0, t, 4 + t)
+        order_w3()
+        for t in range(4):
+            maximum(0, t, 4 + t)
+        length(0, 0, 2)
+        length(0, 1, 3)
+        length(1, 0, 0)
+        length(1, 1, 1)
+        penalise(0, QUART)
+        for t in range(2, 4):
+            for a in range(PASSES):
+                infer_pass(a, 1, t, 2 + t)
+            infer_copy(1, t, 2 + t)
+        penalise(QUART, QUART)
+        for m in range(3):
+            round_w4(m)
         quantise(0, QUART)
-        scores(0, QUART, 2)
-        penalise(QUART, QUART, nc.scalar.copy)
-        better_view(2 * QUART, QUART, 0)
-        length(2, 4)
-        quantise(QUART, QUART)
+        for t in range(4):
+            bank = (6, 7, 2, 3)[t]
+            for a in range(PASSES):
+                goal_pass(a, 1, t, bank)
+            maximum(1, t, bank)
+            if t == 0:
+                quantise(QUART, QUART)
+            if t == 1:
+                quantise_w4()
+        length(2, 0, 0)
+        length(2, 1, 1)
+        scores(0, QUART, 4)
+        length(3, 0, 6)
+        length(3, 1, 7)
+        penalise(2 * QUART, QUART)
         scores(QUART, QUART, 2)
-        penalise(2 * QUART, QUART, nc.scalar.copy)
-        better_view(3 * QUART, P, 0)
-        length(3, 6)
-        penalise(3 * QUART, P, nc.scalar.copy)
+        penalise(3 * QUART, P)
         quantise(2 * QUART, QUART)
-        scores(2 * QUART, QUART, 4)
-        better_view(3 * QUART + P, P, 1)
+        scores(2 * QUART, QUART, 0)
+        penalise(3 * QUART + P, P)
         quantise(3 * QUART, P)
-        scores(3 * QUART, P, 0)
-        penalise(3 * QUART + P, P, nc.vector.tensor_copy)
+        scores(3 * QUART, P, 4)
         quantise(3 * QUART + P, P)
-        last_scores(3 * QUART + P, 1)
+        last_scores(3 * QUART + P, 5)

@@ -20,18 +20,20 @@ P = 128
 PASSES = 2
 HALF = 512
 QUART = 256
-SROW = S + 2 * H
 
 W1A_AT = 0
-V00_AT = 8192
-W1B_AT = V00_AT + 2048
-W3_AT = W1B_AT + 8192
+ROWS_AT = 8192 - 64
+W1B_AT = ROWS_AT + 2048 - 64
+HELD_AT = W1B_AT + 64
+W3_AT = HELD_AT + 8192
 LAM_AT = W3_AT + 4096
 BO_AT = LAM_AT + 128
 W4_AT = BO_AT + 64
 TAB1_AT = W4_AT + 6144
 INF0_AT = TAB1_AT + 8192
-PICKED_AT = W1A_AT + 7168
+W3C_AT = INF0_AT + 4096
+W3ROWS_AT = ROWS_AT + 512
+PICKED_AT = LAM_AT - 1024
 PICKED_BYTES = W4_AT + 64 - PICKED_AT
 
 
@@ -48,44 +50,57 @@ def tile_list_clause_evaluator_kernel(
         offsets = keep.tile([P, S // 16], U16, name="offsets")
         nc.sync.dma_start(offsets[:], offs)
 
-        tab_scale_rows = keep.tile([P, T], U8, name="tab_scale_rows", align_bytes=64)
+        tab_scale_rows = reuse.tile([P, T], U8, name="tab_scale_rows", offset=ROWS_AT, align_bytes=64)
         nc.vector.memset(tab_scale_rows[:].bitcast(I32), 0)
-        w_scale_rows = keep.tile([P, 2, H], U8, name="w_scale_rows", align_bytes=64)
+        w_scale_rows = keep.tile([P, PASSES * H], U8, name="w_scale_rows", align_bytes=64)
         nc.vector.memset(w_scale_rows[:].bitcast(I32), 0)
-        moved = keep.tile([P, PASSES * SROW], U8, name="moved", align_bytes=64)
+        moved = keep.tile([P, PASSES * S], U8, name="moved", align_bytes=64)
         nc.vector.memset(moved[:].bitcast(I32), 0)
 
-        nc.sync.dma_start(tab_scale_rows[0:P:4, :].bitcast(I32), tab_scales.bitcast(I32).rearrange("a q c -> q a c"))
-        for hf, scales in enumerate((w2_scales, w3_scales)):
-            nc.sync.dma_start(w_scale_rows[0:P:4, hf, :].bitcast(I32), scales.bitcast(I32).rearrange("a q c -> q a c"))
+        def load_scale_rows(rows, scales):
+            for d in range(4):
+                nc.sync.dma_start(
+                    rows[32 * d:32 * d + 4, :].bitcast(I32).rearrange("p (a c) -> p a c", a=PASSES),
+                    scales.bitcast(I32)[:, 4 * d:4 * d + 4, :].rearrange("a r c -> r a c"))
+
+        def order_scales(ordered, rows):
+            nc.scalar.copy(
+                ordered[:].bitcast(U32).rearrange("p (a t b e) -> p a t b e", a=PASSES, t=4, e=2),
+                rows[:].bitcast(U32).rearrange("p (a b t e) -> p a t b e", a=PASSES, t=4, e=2))
+            return ordered
+
         w2_raw = keep.tile([P, PASSES, H // 2], I32, name="w2_raw", align_bytes=64)
         nc.sync.dma_start(w2_raw[:], w2_words.bitcast(I32).rearrange("a p c -> p a c"))
+        nc.sync.dma_start(tab_scale_rows[0:P:4, :].bitcast(I32), tab_scales.bitcast(I32).rearrange("a q c -> q a c"))
         tab = [keep.tile([P, T], I32, name="tab0", align_bytes=64),
                reuse.tile([P, T], I32, name="tab1", offset=TAB1_AT, align_bytes=64)]
         for a in range(PASSES):
             nc.sync.dma_start(tab[a][:], tab_words[a].rearrange("p t i -> p (t i)").bitcast(I32))
+            if a == 0:
+                load_scale_rows(w_scale_rows, w2_scales)
 
-        staged = keep.tile([P, SROW], U8, name="staged", align_bytes=64)
-        staged_w = staged[:].bitcast(I32)
         picked = reuse.tile([P, PICKED_BYTES], U8, name="picked", offset=PICKED_AT, align_bytes=64)
         nc.vector.tensor_copy(picked[:, 0:S], tab_scale_rows[:].indirect(offsets[:]))
-        nc.vector.tensor_copy(
-            staged_w[:, S // 4:].rearrange("p (w t b e) -> p w b t e", w=2, t=4, e=2),
-            w_scale_rows[:].bitcast(I32).rearrange("p w (b t e) -> p w b t e", t=4, e=2))
-        nc.vector.tensor_copy(staged_w[:, 0:S // 4], picked[:, 0:S].bitcast(I32))
+        w3_scale_rows = reuse.tile([P, H], U8, name="w3_scale_rows", offset=W3ROWS_AT, align_bytes=64)
+        nc.vector.memset(w3_scale_rows[:].bitcast(I32), 0)
         for d in (0, 2, 1, 3):
             nc.sync.dma_start(
                 moved[32 * d:32 * d + 4, :].bitcast(I32).rearrange("p (a c) -> p a c", a=PASSES),
-                staged[32 * d:32 * d + 32:4, :].bitcast(I32))
+                picked[32 * d:32 * d + 32:4, 0:S].bitcast(I32))
         w1_raw = []
         for a in range(PASSES):
             raw = reuse.tile([P, 4 * H], F32, name="w1_raw%d" % a, offset=(W1A_AT, W1B_AT)[a], align_bytes=64)
             nc.sync.dma_start(raw[:], w1[512 * a:512 * (a + 1), :].rearrange("(p j) c -> p (j c)", j=4))
             w1_raw.append(raw[:])
+            if a == 0:
+                for d in range(4):
+                    nc.sync.dma_start(w3_scale_rows[32 * d:32 * d + 8, :].bitcast(I32),
+                                      w3_scales.bitcast(I32)[:, 4 * d:4 * d + 4, :])
 
         w3_raw = reuse.tile([P, PASSES, H], I32, name="w3_raw", offset=W3_AT, align_bytes=64)
         nc.sync.dma_start(
             w3_raw[:], w3_words.rearrange("a p c i -> a p (c i)").bitcast(I32).rearrange("a p c -> p a c"))
+        w_s = [order_scales(keep.tile([P, PASSES * H], U8, name="w2_s", align_bytes=64), w_scale_rows)]
         lam_t = [reuse.tile([P, 1], F32, name="lam%d" % t, offset=LAM_AT + 32 * t) for t in range(4)]
         bo_tile = reuse.tile([P, 3], F32, name="bo_tile", offset=BO_AT)
         bo_t = bo_tile[:]
@@ -105,24 +120,26 @@ def tile_list_clause_evaluator_kernel(
             v[a, hf] = picked[:]
 
         w2_c = keep.tile([P, PASSES * H // 2], I32, name="w2_c", align_bytes=64)
-        nc.vector.tensor_copy(
-            w2_c[:].rearrange("p (a t b e) -> p a b t e", a=PASSES, t=4, e=4),
-            w2_raw[:].rearrange("p a (b t e) -> p a b t e", t=4, e=4))
-        gather(0, 0, reuse.tile([P, HALF], U32, name="v0_0", offset=V00_AT, align_bytes=64))
+        nc.scalar.copy(
+            w2_c[:].bitcast(U32).rearrange("p (a t b e) -> p a t b e", a=PASSES, t=4, e=4),
+            w2_raw[:].bitcast(U32).rearrange("p a (b t e) -> p a t b e", t=4, e=4))
+        gather(0, 0, keep.tile([P, HALF], U32, name="v0_0", align_bytes=64))
+        gather(0, 1, keep.tile([P, HALF], U32, name="v0_1", align_bytes=64))
         gather(1, 0, keep.tile([P, HALF], U32, name="v1_0", align_bytes=64))
         gather(1, 1, keep.tile([P, HALF], U32, name="v1_1", align_bytes=64))
-        gather(0, 1, reuse.tile([P, HALF], U32, name="v0_1", offset=TAB1_AT, align_bytes=64))
 
         def table_scales(a, c0, n):
-            c = a * SROW + c0
+            c = a * S + c0
             return moved[:, c:c + n]
 
         def weight_scales(which, a, t):
-            c = a * SROW + S + which * H + t * P
-            return moved[:, c:c + P]
+            c = a * H + t * P
+            return w_s[which][:, c:c + P]
 
-        inf_sb = [reuse.tile([P, 4, HALF], F32, name="inf0", offset=INF0_AT, align_bytes=64),
-                  reuse.tile([P, 4, HALF], F32, name="inf1", offset=W1B_AT, align_bytes=64)]
+        inf_at = {(0, 0): INF0_AT, (0, 1): INF0_AT + 2048, (0, 2): HELD_AT, (0, 3): HELD_AT + 2048,
+                  (1, 0): HELD_AT + 4096, (1, 1): HELD_AT + 6144, (1, 2): TAB1_AT, (1, 3): TAB1_AT + 2048}
+        inf_sb = {key: reuse.tile([P, HALF], F32, name="inf%d_%d" % key, offset=at, align_bytes=64)
+                  for key, at in inf_at.items()}
 
         def one_pass(acc, codes, scales, a, c0, n):
             hf, ch = c0 // HALF, c0 % HALF
@@ -135,19 +152,21 @@ def tile_list_clause_evaluator_kernel(
             one_pass(banks[bank][:], w2_c[:, c:c + P // 2].bitcast(FP4X4), weight_scales(0, a, t), a, hf * HALF, HALF)
 
         def infer_copy(hf, t, bank):
-            nc.scalar.copy(inf_sb[hf][:, t, :], banks[bank][:])
+            nc.scalar.copy(inf_sb[hf, t][:], banks[bank][:])
 
         w1_c = keep.tile([P, PASSES * H], U32, name="w1_c", align_bytes=64)
         w1_s = keep.tile([P, PASSES * H], U8, name="w1_s", align_bytes=64)
-        w1_g = [keep.tile([P, 4 * H], BF16, name="w1_g%d" % a, align_bytes=64) for a in range(PASSES)]
+        w1_g0 = keep.tile([P, 4 * H], BF16, name="w1_g0", align_bytes=64)
+        w1_g10 = reuse.tile([P, 2 * H], BF16, name="w1_g10", offset=W3C_AT, align_bytes=64)
+        w1_g11 = keep.tile([P, 2 * H], BF16, name="w1_g11", align_bytes=64)
+        w1_g = {(0, 0): w1_g0[:, 0:2 * H], (0, 1): w1_g0[:, 2 * H:], (1, 0): w1_g10[:], (1, 1): w1_g11[:]}
 
         def round_w1(a, u, copy):
-            copy(w1_g[a][:].rearrange("p (t b q j) -> p t b q j", t=4, q=8, j=4)[:, 2 * u:2 * u + 2],
+            copy(w1_g[a, u].rearrange("p (t b q j) -> p t b q j", t=2, q=8, j=4),
                  w1_raw[a].rearrange("p (j b t q) -> p t b q j", j=4, t=4, q=8)[:, 2 * u:2 * u + 2])
 
-        def quantise_w1(c, n):
-            a, cg = c // H, c % H
-            nc.vector.quantize_mx(w1_c[:, c:c + n].bitcast(FP8X4), w1_s[:, c:c + n], w1_g[a][:, 4 * cg:4 * (cg + n)])
+        def quantise_w1(c, n, rounded):
+            nc.vector.quantize_mx(w1_c[:, c:c + n].bitcast(FP8X4), w1_s[:, c:c + n], rounded)
 
         def goal_pass(a, hf, t, bank):
             c = a * H + t * P
@@ -156,14 +175,14 @@ def tile_list_clause_evaluator_kernel(
         best = [keep.tile([P, 4, HALF], F32, name="best%d" % hf, align_bytes=64) for hf in range(2)]
 
         def maximum(hf, t, bank):
-            nc.vector.tensor_tensor(best[hf][:, t, :], banks[bank][:], inf_sb[hf][:, t, :], ALU.max)
+            nc.vector.tensor_tensor(best[hf][:, t, :], banks[bank][:], inf_sb[hf, t][:], ALU.max)
 
-        w3_c = keep.tile([P, PASSES * H], I32, name="w3_c", align_bytes=64)
+        w3_c = reuse.tile([P, PASSES * H], I32, name="w3_c", offset=W3C_AT, align_bytes=64)
 
         def order_w3():
             nc.vector.tensor_copy(
-                w3_c[:].rearrange("p (a t b q) -> p a b t q", a=PASSES, t=4, q=8),
-                w3_raw[:].rearrange("p a (b t q) -> p a b t q", t=4, q=8))
+                w3_c[:].rearrange("p (a t b q) -> p a t b q", a=PASSES, t=4, q=8),
+                w3_raw[:].rearrange("p a (b t q) -> p a t b q", t=4, q=8))
 
         weighted = [keep.tile([P, 4, QUART], F32, name="weighted%d" % qt, align_bytes=64) for qt in range(4)]
 
@@ -172,12 +191,12 @@ def tile_list_clause_evaluator_kernel(
                 for a in range(PASSES):
                     c = a * H + t * P
                     one_pass(banks[bank][:, (t % 2) * QUART:(t % 2 + 1) * QUART], w3_c[:, c:c + P].bitcast(FP8X4),
-                             weight_scales(1, a, t), a, qt * QUART, QUART)
+                             w3_s[4 * a:P, t * P:(t + 1) * P], a, qt * QUART, QUART)
             for t in (2 * pair, 2 * pair + 1):
                 nc.scalar.activation(weighted[qt][:, t, :], banks[bank][:, (t % 2) * QUART:(t % 2 + 1) * QUART],
                                      ACT.Copy, scale=lam_t[t][:])
 
-        w4_g = reuse.tile([P, 4 * N], BF16, name="w4_g", offset=INF0_AT, align_bytes=64)
+        w4_g = reuse.tile([P, 4 * N], BF16, name="w4_g", offset=HELD_AT + 1024, align_bytes=64)
         w4_c = keep.tile([P, N], U32, name="w4_c", align_bytes=64)
         w4_s = keep.tile([P, N], U8, name="w4_s", align_bytes=64)
 
@@ -232,24 +251,29 @@ def tile_list_clause_evaluator_kernel(
         for a in range(PASSES):
             for t in range(4):
                 infer_pass(a, 0, t, t)
-        for t in range(4):
+        w3_s = keep.tile([P, H], U8, name="w3_s", align_bytes=64)
+        nc.scalar.copy(w3_s[:].bitcast(U32).rearrange("p (t b e) -> p t b e", t=4, e=2),
+                       w3_scale_rows[:].bitcast(U32).rearrange("p (b t e) -> p t b e", t=4, e=2))
+        for t in range(2):
             infer_copy(0, t, t)
         round_w1(0, 0, nc.vector.tensor_copy)
         round_w1(0, 1, nc.vector.tensor_copy)
-        quantise_w1(0, H)
+        quantise_w1(0, H, w1_g0[:])
         round_w1(1, 0, nc.vector.tensor_copy)
         round_w1(1, 1, nc.scalar.copy)
+        for t in range(2, 4):
+            infer_copy(0, t, t)
         for t in range(2):
             for a in range(PASSES):
                 infer_pass(a, 1, t, t)
             infer_copy(1, t, t)
         for t in range(4):
             goal_pass(0, 0, t, 4 + t)
-        quantise_w1(H, 2 * P)
-        quantise_w1(H + 2 * P, 2 * P)
+        quantise_w1(H, 2 * P, w1_g[1, 0])
+        order_w3()
+        quantise_w1(H + 2 * P, 2 * P, w1_g[1, 1])
         for t in range(4):
             goal_pass(1, 0, t, 4 + t)
-        order_w3()
         for t in range(4):
             maximum(0, t, 4 + t)
         length(0, 0, 2)

@@ -31,8 +31,9 @@ BO_AT = LAM_AT + 128
 W4_AT = BO_AT + 64
 TAB1_AT = W4_AT + 6144
 INF0_AT = TAB1_AT + 8192
-W3C_AT = INF0_AT + 4096
+W3C_AT = INF0_AT + 8192
 W3ROWS_AT = ROWS_AT + 512
+BEST0_AT = W3ROWS_AT + 64 - 8192
 PICKED_AT = LAM_AT - 1024
 PICKED_BYTES = W4_AT + 64 - PICKED_AT
 
@@ -94,7 +95,7 @@ def tile_list_clause_evaluator_kernel(
             w1_raw.append(raw[:])
             if a == 0:
                 for d in range(4):
-                    nc.sync.dma_start(w3_scale_rows[32 * d:32 * d + 8, :].bitcast(I32),
+                    nc.sync.dma_start(w3_scale_rows[32 * d + 8:32 * d + 16, :].bitcast(I32),
                                       w3_scales.bitcast(I32)[:, 4 * d:4 * d + 4, :])
 
         w3_raw = reuse.tile([P, PASSES, H], I32, name="w3_raw", offset=W3_AT, align_bytes=64)
@@ -136,8 +137,8 @@ def tile_list_clause_evaluator_kernel(
             c = a * H + t * P
             return w_s[which][:, c:c + P]
 
-        inf_at = {(0, 0): INF0_AT, (0, 1): INF0_AT + 2048, (0, 2): HELD_AT, (0, 3): HELD_AT + 2048,
-                  (1, 0): HELD_AT + 4096, (1, 1): HELD_AT + 6144, (1, 2): TAB1_AT, (1, 3): TAB1_AT + 2048}
+        inf_at = {(0, 0): INF0_AT, (0, 1): INF0_AT + 2048, (0, 2): INF0_AT + 4096, (0, 3): INF0_AT + 6144,
+                  (1, 0): HELD_AT, (1, 1): HELD_AT + 2048, (1, 2): HELD_AT + 4096, (1, 3): HELD_AT + 6144}
         inf_sb = {key: reuse.tile([P, HALF], F32, name="inf%d_%d" % key, offset=at, align_bytes=64)
                   for key, at in inf_at.items()}
 
@@ -172,7 +173,8 @@ def tile_list_clause_evaluator_kernel(
             c = a * H + t * P
             one_pass(banks[bank][:], w1_c[:, c:c + P].bitcast(FP8X4), w1_s[:, c:c + P], a, hf * HALF, HALF)
 
-        best = [keep.tile([P, 4, HALF], F32, name="best%d" % hf, align_bytes=64) for hf in range(2)]
+        best = [reuse.tile([P, 4, HALF], F32, name="best0", offset=BEST0_AT, align_bytes=64),
+                keep.tile([P, 4, HALF], F32, name="best1", align_bytes=64)]
 
         def maximum(hf, t, bank):
             nc.vector.tensor_tensor(best[hf][:, t, :], banks[bank][:], inf_sb[hf, t][:], ALU.max)
@@ -191,12 +193,12 @@ def tile_list_clause_evaluator_kernel(
                 for a in range(PASSES):
                     c = a * H + t * P
                     one_pass(banks[bank][:, (t % 2) * QUART:(t % 2 + 1) * QUART], w3_c[:, c:c + P].bitcast(FP8X4),
-                             w3_s[4 * a:P, t * P:(t + 1) * P], a, qt * QUART, QUART)
+                             w3_s[8 + 4 * a:P, t * P:(t + 1) * P], a, qt * QUART, QUART)
             for t in (2 * pair, 2 * pair + 1):
                 nc.scalar.activation(weighted[qt][:, t, :], banks[bank][:, (t % 2) * QUART:(t % 2 + 1) * QUART],
                                      ACT.Copy, scale=lam_t[t][:])
 
-        w4_g = reuse.tile([P, 4 * N], BF16, name="w4_g", offset=HELD_AT + 1024, align_bytes=64)
+        w4_g = reuse.tile([P, 4 * N], BF16, name="w4_g", offset=INF0_AT + 5120, align_bytes=64)
         w4_c = keep.tile([P, N], U32, name="w4_c", align_bytes=64)
         w4_s = keep.tile([P, N], U8, name="w4_s", align_bytes=64)
 
@@ -251,18 +253,13 @@ def tile_list_clause_evaluator_kernel(
         for a in range(PASSES):
             for t in range(4):
                 infer_pass(a, 0, t, t)
-        w3_s = keep.tile([P, H], U8, name="w3_s", align_bytes=64)
-        nc.scalar.copy(w3_s[:].bitcast(U32).rearrange("p (t b e) -> p t b e", t=4, e=2),
-                       w3_scale_rows[:].bitcast(U32).rearrange("p (b t e) -> p t b e", t=4, e=2))
-        for t in range(2):
+        for t in range(4):
             infer_copy(0, t, t)
         round_w1(0, 0, nc.vector.tensor_copy)
         round_w1(0, 1, nc.vector.tensor_copy)
         quantise_w1(0, H, w1_g0[:])
         round_w1(1, 0, nc.vector.tensor_copy)
         round_w1(1, 1, nc.scalar.copy)
-        for t in range(2, 4):
-            infer_copy(0, t, t)
         for t in range(2):
             for a in range(PASSES):
                 infer_pass(a, 1, t, t)
@@ -272,6 +269,9 @@ def tile_list_clause_evaluator_kernel(
         quantise_w1(H, 2 * P, w1_g[1, 0])
         order_w3()
         quantise_w1(H + 2 * P, 2 * P, w1_g[1, 1])
+        w3_s = keep.tile([P, H], U8, name="w3_s", align_bytes=64)
+        nc.vector.tensor_copy(w3_s[:].bitcast(I32).rearrange("p (t b e) -> p t b e", t=4, e=2),
+                              w3_scale_rows[:].bitcast(I32).rearrange("p (b t e) -> p t b e", t=4, e=2))
         for t in range(4):
             goal_pass(1, 0, t, 4 + t)
         for t in range(4):

@@ -18,24 +18,27 @@ ACT = mybir.ActivationFunctionType
 
 P = 128
 PASSES = 2
+TILES = 4
 HALF = 512
 QUART = 256
+EARLY = 2
 
+LAP = 64
 W1A_AT = 0
-ROWS_AT = 8192 - 64
-W1B_AT = ROWS_AT + 2048 - 64
-HELD_AT = W1B_AT + 64
-W3_AT = HELD_AT + 8192
+ROWS_AT = W1A_AT + 8192 - LAP
+W1B_AT = ROWS_AT + T - LAP
+W3ROWS_AT = ROWS_AT + 512
+BEST0_AT = W3ROWS_AT + LAP - 8192
+LATE_INF_AT = W1B_AT + LAP
+W3_AT = LATE_INF_AT + 8192
 LAM_AT = W3_AT + 4096
 BO_AT = LAM_AT + 128
 W4_AT = BO_AT + 64
+PICKED_AT = LAM_AT - 256
 TAB1_AT = W4_AT + 6144
-INF0_AT = TAB1_AT + 8192
-W3C_AT = INF0_AT + 8192
-W3ROWS_AT = ROWS_AT + 512
-BEST0_AT = W3ROWS_AT + 64 - 8192
-PICKED_AT = LAM_AT - 1024
-PICKED_BYTES = W4_AT + 64 - PICKED_AT
+EARLY_INF_AT = TAB1_AT + 8192
+W4G_AT = EARLY_INF_AT + 5120
+W3C_AT = EARLY_INF_AT + 8192
 
 
 def tile_list_clause_evaluator_kernel(
@@ -53,118 +56,102 @@ def tile_list_clause_evaluator_kernel(
 
         tab_scale_rows = reuse.tile([P, T], U8, name="tab_scale_rows", offset=ROWS_AT, align_bytes=64)
         nc.vector.memset(tab_scale_rows[:].bitcast(I32), 0)
-        w_scale_rows = keep.tile([P, PASSES * H], U8, name="w_scale_rows", align_bytes=64)
-        nc.vector.memset(w_scale_rows[:].bitcast(I32), 0)
-        moved = keep.tile([P, PASSES * S], U8, name="moved", align_bytes=64)
-        nc.vector.memset(moved[:].bitcast(I32), 0)
-
-        def load_scale_rows(rows, scales):
-            for d in range(4):
-                nc.sync.dma_start(
-                    rows[32 * d:32 * d + 4, :].bitcast(I32).rearrange("p (a c) -> p a c", a=PASSES),
-                    scales.bitcast(I32)[:, 4 * d:4 * d + 4, :].rearrange("a r c -> r a c"))
-
-        def order_scales(ordered, rows):
-            nc.scalar.copy(
-                ordered[:].bitcast(U32).rearrange("p (a t b e) -> p a t b e", a=PASSES, t=4, e=2),
-                rows[:].bitcast(U32).rearrange("p (a b t e) -> p a t b e", a=PASSES, t=4, e=2))
-            return ordered
+        w2_scale_rows = keep.tile([P, PASSES * H], U8, name="w2_scale_rows", align_bytes=64)
+        nc.vector.memset(w2_scale_rows[:].bitcast(I32), 0)
+        v_s = keep.tile([P, PASSES * S], U8, name="v_s", align_bytes=64)
+        nc.vector.memset(v_s[:].bitcast(I32), 0)
 
         w2_raw = keep.tile([P, PASSES, H // 2], I32, name="w2_raw", align_bytes=64)
         nc.sync.dma_start(w2_raw[:], w2_words.bitcast(I32).rearrange("a p c -> p a c"))
         nc.sync.dma_start(tab_scale_rows[0:P:4, :].bitcast(I32), tab_scales.bitcast(I32).rearrange("a q c -> q a c"))
         tab = [keep.tile([P, T], I32, name="tab0", align_bytes=64),
                reuse.tile([P, T], I32, name="tab1", offset=TAB1_AT, align_bytes=64)]
-        for a in range(PASSES):
-            nc.sync.dma_start(tab[a][:], tab_words[a].rearrange("p t i -> p (t i)").bitcast(I32))
-            if a == 0:
-                load_scale_rows(w_scale_rows, w2_scales)
 
-        picked = reuse.tile([P, PICKED_BYTES], U8, name="picked", offset=PICKED_AT, align_bytes=64)
+        def load_table(a):
+            nc.sync.dma_start(tab[a][:], tab_words[a].rearrange("p t i -> p (t i)").bitcast(I32))
+
+        load_table(0)
+        for d in range(4):
+            nc.sync.dma_start(
+                w2_scale_rows[32 * d:32 * d + 4, :].bitcast(I32).rearrange("p (a c) -> p a c", a=PASSES),
+                w2_scales.bitcast(I32)[:, 4 * d:4 * d + 4, :].rearrange("a s c -> s a c"))
+        load_table(1)
+
+        picked = reuse.tile([P, S], U8, name="picked", offset=PICKED_AT, align_bytes=64)
         nc.vector.tensor_copy(picked[:, 0:S], tab_scale_rows[:].indirect(offsets[:]))
         w3_scale_rows = reuse.tile([P, H], U8, name="w3_scale_rows", offset=W3ROWS_AT, align_bytes=64)
         nc.vector.memset(w3_scale_rows[:].bitcast(I32), 0)
         for d in (0, 2, 1, 3):
             nc.sync.dma_start(
-                moved[32 * d:32 * d + 4, :].bitcast(I32).rearrange("p (a c) -> p a c", a=PASSES),
+                v_s[32 * d:32 * d + 4, :].bitcast(I32).rearrange("p (a c) -> p a c", a=PASSES),
                 picked[32 * d:32 * d + 32:4, 0:S].bitcast(I32))
-        w1_raw = []
-        for a in range(PASSES):
-            raw = reuse.tile([P, 4 * H], F32, name="w1_raw%d" % a, offset=(W1A_AT, W1B_AT)[a], align_bytes=64)
-            nc.sync.dma_start(raw[:], w1[512 * a:512 * (a + 1), :].rearrange("(p j) c -> p (j c)", j=4))
-            w1_raw.append(raw[:])
-            if a == 0:
-                for d in range(4):
-                    nc.sync.dma_start(w3_scale_rows[32 * d + 8:32 * d + 16, :].bitcast(I32),
-                                      w3_scales.bitcast(I32)[:, 4 * d:4 * d + 4, :])
+
+        w1_raw = [reuse.tile([P, 4 * H], F32, name="w1_raw%d" % a, offset=at, align_bytes=64)
+                  for a, at in enumerate((W1A_AT, W1B_AT))]
+
+        def load_w1(a):
+            nc.sync.dma_start(w1_raw[a][:], w1[512 * a:512 * (a + 1), :].rearrange("(p i) c -> p (i c)", i=4))
+
+        load_w1(0)
+        for d in range(4):
+            nc.sync.dma_start(w3_scale_rows[32 * d + 8:32 * d + 16, :].bitcast(I32),
+                              w3_scales.bitcast(I32)[:, 4 * d:4 * d + 4, :])
+        load_w1(1)
 
         w3_raw = reuse.tile([P, PASSES, H], I32, name="w3_raw", offset=W3_AT, align_bytes=64)
         nc.sync.dma_start(
             w3_raw[:], w3_words.rearrange("a p c i -> a p (c i)").bitcast(I32).rearrange("a p c -> p a c"))
-        w_s = [order_scales(keep.tile([P, PASSES * H], U8, name="w2_s", align_bytes=64), w_scale_rows)]
-        lam_t = [reuse.tile([P, 1], F32, name="lam%d" % t, offset=LAM_AT + 32 * t) for t in range(4)]
-        bo_tile = reuse.tile([P, 3], F32, name="bo_tile", offset=BO_AT)
-        bo_t = bo_tile[:]
-        w4_tile = reuse.tile([P, 4 * N], F32, name="w4_tile", offset=W4_AT, align_bytes=64)
-        w4_raw = w4_tile[:]
+        w2_s = keep.tile([P, PASSES * H], U8, name="w2_s", align_bytes=64)
+        nc.scalar.copy(
+            w2_s[:].bitcast(U32).rearrange("p (a t b e) -> p a t b e", a=PASSES, t=TILES, e=2),
+            w2_scale_rows[:].bitcast(U32).rearrange("p (a b t e) -> p a t b e", a=PASSES, t=TILES, e=2))
+        lam_t = [reuse.tile([P, 1], F32, name="lam%d" % t, offset=LAM_AT + 32 * t) for t in range(TILES)]
+        bo_t = reuse.tile([P, 3], F32, name="bo_t", offset=BO_AT)
+        w4_raw = reuse.tile([P, TILES * N], F32, name="w4_raw", offset=W4_AT, align_bytes=64)
         with nc.allow_non_contiguous_dma(reason="one value a partition"):
-            for t in range(4):
-                nc.sync.dma_start(lam_t[t][:], lam.rearrange("(b t q) -> t b q", t=4, q=8)[t])
-            for t in range(4):
-                nc.sync.dma_start(w4_raw[:, t * N:(t + 1) * N], w4.rearrange("(b t q) n -> t b q n", t=4, q=8)[t])
-            nc.sync.dma_start(bo_t, bo.rearrange("(m p) -> p m", p=P))
-
-        v = {}
-
-        def gather(a, hf, picked):
-            nc.vector.tensor_copy(picked[:], tab[a][:].bitcast(U32).indirect(offsets[:, 32 * hf:32 * (hf + 1)]))
-            v[a, hf] = picked[:]
+            for t in range(TILES):
+                nc.sync.dma_start(lam_t[t][:], lam.rearrange("(b t j) -> t b j", t=TILES, j=8)[t])
+            for t in range(TILES):
+                nc.sync.dma_start(w4_raw[:, t * N:(t + 1) * N], w4.rearrange("(b t j) n -> t b j n", t=TILES, j=8)[t])
+            nc.sync.dma_start(bo_t[:], bo.rearrange("(m p) -> p m", p=P))
 
         w2_c = keep.tile([P, PASSES * H // 2], I32, name="w2_c", align_bytes=64)
         nc.scalar.copy(
-            w2_c[:].bitcast(U32).rearrange("p (a t b e) -> p a t b e", a=PASSES, t=4, e=4),
-            w2_raw[:].bitcast(U32).rearrange("p a (b t e) -> p a t b e", t=4, e=4))
-        gather(0, 0, keep.tile([P, HALF], U32, name="v0_0", align_bytes=64))
-        gather(0, 1, keep.tile([P, HALF], U32, name="v0_1", align_bytes=64))
-        gather(1, 0, keep.tile([P, HALF], U32, name="v1_0", align_bytes=64))
-        gather(1, 1, keep.tile([P, HALF], U32, name="v1_1", align_bytes=64))
-
-        def table_scales(a, c0, n):
-            c = a * S + c0
-            return moved[:, c:c + n]
-
-        def weight_scales(which, a, t):
-            c = a * H + t * P
-            return w_s[which][:, c:c + P]
-
-        inf_at = {(0, 0): INF0_AT, (0, 1): INF0_AT + 2048, (0, 2): INF0_AT + 4096, (0, 3): INF0_AT + 6144,
-                  (1, 0): HELD_AT, (1, 1): HELD_AT + 2048, (1, 2): HELD_AT + 4096, (1, 3): HELD_AT + 6144}
-        inf_sb = {key: reuse.tile([P, HALF], F32, name="inf%d_%d" % key, offset=at, align_bytes=64)
-                  for key, at in inf_at.items()}
+            w2_c[:].bitcast(U32).rearrange("p (a t b e) -> p a t b e", a=PASSES, t=TILES, e=4),
+            w2_raw[:].bitcast(U32).rearrange("p a (b t e) -> p a t b e", t=TILES, e=4))
+        v_c = {}
+        for a in range(PASSES):
+            for hf in range(2):
+                v_c[a, hf] = keep.tile([P, HALF], U32, name="v%d_%d" % (a, hf), align_bytes=64)
+                nc.vector.tensor_copy(
+                    v_c[a, hf][:], tab[a][:].bitcast(U32).indirect(offsets[:, 32 * hf:32 * (hf + 1)]))
 
         def one_pass(acc, codes, scales, a, c0, n):
             hf, ch = c0 // HALF, c0 % HALF
             nc.tensor.matmul_mx(
-                acc, lhsT=codes, lhsT_scale=scales, rhs=v[a, hf][:, ch:ch + n].bitcast(FP8X4),
-                rhs_scale=table_scales(a, c0, n), start=(a == 0), stop=(a == PASSES - 1))
+                acc, lhsT=codes, lhsT_scale=scales, rhs=v_c[a, hf][:, ch:ch + n].bitcast(FP8X4),
+                rhs_scale=v_s[:, a * S + c0:a * S + c0 + n], start=(a == 0), stop=(a == PASSES - 1))
+
+        infer = {(hf, t): reuse.tile([P, HALF], F32, name="infer%d_%d" % (hf, t), offset=at + 2048 * t, align_bytes=64)
+                 for hf, at in enumerate((EARLY_INF_AT, LATE_INF_AT)) for t in range(TILES)}
 
         def infer_pass(a, hf, t, bank):
-            c = (4 * a + t) * (P // 2)
-            one_pass(banks[bank][:], w2_c[:, c:c + P // 2].bitcast(FP4X4), weight_scales(0, a, t), a, hf * HALF, HALF)
+            c = a * H + t * P
+            one_pass(banks[bank][:], w2_c[:, c // 2:(c + P) // 2].bitcast(FP4X4), w2_s[:, c:c + P], a, hf * HALF, HALF)
 
         def infer_copy(hf, t, bank):
-            nc.scalar.copy(inf_sb[hf, t][:], banks[bank][:])
+            nc.scalar.copy(infer[hf, t][:], banks[bank][:])
 
         w1_c = keep.tile([P, PASSES * H], U32, name="w1_c", align_bytes=64)
         w1_s = keep.tile([P, PASSES * H], U8, name="w1_s", align_bytes=64)
         w1_g0 = keep.tile([P, 4 * H], BF16, name="w1_g0", align_bytes=64)
-        w1_g10 = reuse.tile([P, 2 * H], BF16, name="w1_g10", offset=W3C_AT, align_bytes=64)
-        w1_g11 = keep.tile([P, 2 * H], BF16, name="w1_g11", align_bytes=64)
+        w1_g10 = keep.tile([P, 2 * H], BF16, name="w1_g10", align_bytes=64)
+        w1_g11 = reuse.tile([P, 2 * H], BF16, name="w1_g11", offset=W3C_AT, align_bytes=64)
         w1_g = {(0, 0): w1_g0[:, 0:2 * H], (0, 1): w1_g0[:, 2 * H:], (1, 0): w1_g10[:], (1, 1): w1_g11[:]}
 
-        def round_w1(a, u, copy):
-            copy(w1_g[a, u].rearrange("p (t b q j) -> p t b q j", t=2, q=8, j=4),
-                 w1_raw[a].rearrange("p (j b t q) -> p t b q j", j=4, t=4, q=8)[:, 2 * u:2 * u + 2])
+        def round_w1(a, t0, count, copy):
+            copy(w1_g[a, t0 // 2].rearrange("p (t b j i) -> p t b j i", t=2, j=8, i=4)[:, t0 % 2:t0 % 2 + count],
+                 w1_raw[a][:].rearrange("p (i b t j) -> p t b j i", i=4, t=TILES, j=8)[:, t0:t0 + count])
 
         def quantise_w1(c, n, rounded):
             nc.vector.quantize_mx(w1_c[:, c:c + n].bitcast(FP8X4), w1_s[:, c:c + n], rounded)
@@ -173,55 +160,60 @@ def tile_list_clause_evaluator_kernel(
             c = a * H + t * P
             one_pass(banks[bank][:], w1_c[:, c:c + P].bitcast(FP8X4), w1_s[:, c:c + P], a, hf * HALF, HALF)
 
-        best = [reuse.tile([P, 4, HALF], F32, name="best0", offset=BEST0_AT, align_bytes=64),
-                keep.tile([P, 4, HALF], F32, name="best1", align_bytes=64)]
+        best = [reuse.tile([P, TILES, HALF], F32, name="best0", offset=BEST0_AT, align_bytes=64),
+                keep.tile([P, TILES, HALF], F32, name="best1", align_bytes=64)]
 
         def maximum(hf, t, bank):
-            nc.vector.tensor_tensor(best[hf][:, t, :], banks[bank][:], inf_sb[hf, t][:], ALU.max)
+            nc.vector.tensor_tensor(best[hf][:, t, :], banks[bank][:], infer[hf, t][:], ALU.max)
 
         w3_c = reuse.tile([P, PASSES * H], I32, name="w3_c", offset=W3C_AT, align_bytes=64)
-
-        def order_w3():
-            nc.vector.tensor_copy(
-                w3_c[:].rearrange("p (a t b q) -> p a t b q", a=PASSES, t=4, q=8),
-                w3_raw[:].rearrange("p a (b t q) -> p a t b q", t=4, q=8))
-
-        weighted = [keep.tile([P, 4, QUART], F32, name="weighted%d" % qt, align_bytes=64) for qt in range(4)]
-
-        def length(qt, pair, bank):
-            for t in (2 * pair, 2 * pair + 1):
-                for a in range(PASSES):
-                    c = a * H + t * P
-                    one_pass(banks[bank][:, (t % 2) * QUART:(t % 2 + 1) * QUART], w3_c[:, c:c + P].bitcast(FP8X4),
-                             w3_s[8 + 4 * a:P, t * P:(t + 1) * P], a, qt * QUART, QUART)
-            for t in (2 * pair, 2 * pair + 1):
-                nc.scalar.activation(weighted[qt][:, t, :], banks[bank][:, (t % 2) * QUART:(t % 2 + 1) * QUART],
-                                     ACT.Copy, scale=lam_t[t][:])
-
-        w4_g = reuse.tile([P, 4 * N], BF16, name="w4_g", offset=INF0_AT + 5120, align_bytes=64)
+        weighted = [keep.tile([P, TILES, QUART], F32, name="weighted%d" % qt, align_bytes=64) for qt in range(4)]
+        w4_g = reuse.tile([P, TILES * N], BF16, name="w4_g", offset=W4G_AT, align_bytes=64)
         w4_c = keep.tile([P, N], U32, name="w4_c", align_bytes=64)
         w4_s = keep.tile([P, N], U8, name="w4_s", align_bytes=64)
+        h_g = keep.tile([P, TILES * S], BF16, name="h_g", align_bytes=64)
+        h_c = keep.tile([P, S], U32, name="h_c", align_bytes=64)
+        h_s = keep.tile([P, S], U8, name="h_s", align_bytes=64)
+        w3_s = keep.tile([P, H], U8, name="w3_s", align_bytes=64)
+
+        def order_w3_words():
+            nc.vector.tensor_copy(
+                w3_c[:].rearrange("p (a t b j) -> p a t b j", a=PASSES, t=TILES, j=8),
+                w3_raw[:].rearrange("p a (b t j) -> p a t b j", t=TILES, j=8))
+
+        def order_w3_scales():
+            nc.vector.tensor_copy(
+                w3_s[:].bitcast(I32).rearrange("p (t b e) -> p t b e", t=TILES, e=2),
+                w3_scale_rows[:].bitcast(I32).rearrange("p (b t e) -> p t b e", t=TILES, e=2))
+
+        def length(qt, first_bank):
+            for pair in range(2):
+                tiles = (2 * pair, 2 * pair + 1)
+                accs = {t: banks[first_bank + pair][:, (t % 2) * QUART:(t % 2 + 1) * QUART] for t in tiles}
+                for t in tiles:
+                    for a in range(PASSES):
+                        c = a * H + t * P
+                        one_pass(accs[t], w3_c[:, c:c + P].bitcast(FP8X4), w3_s[8 + 4 * a:P, t * P:(t + 1) * P],
+                                 a, qt * QUART, QUART)
+                for t in tiles:
+                    nc.scalar.activation(weighted[qt][:, t, :], accs[t], ACT.Copy, scale=lam_t[t][:])
 
         def round_w4(m):
-            nc.scalar.copy(w4_g[:].rearrange("p (c i t) -> p c t i", i=4, t=4)[:, 32 * m:32 * (m + 1)],
-                           w4_raw.rearrange("p (t c i) -> p c t i", i=4, t=4)[:, 32 * m:32 * (m + 1)])
+            nc.scalar.copy(w4_g[:].rearrange("p (c e t) -> p c t e", e=4, t=TILES)[:, 32 * m:32 * (m + 1)],
+                           w4_raw[:].rearrange("p (t c e) -> p c t e", e=4, t=TILES)[:, 32 * m:32 * (m + 1)])
 
         def quantise_w4():
             for c0, c1 in ((0, 256), (256, N)):
                 nc.vector.quantize_mx(w4_c[:, c0:c1].bitcast(FP8X4), w4_s[:, c0:c1], w4_g[:, 4 * c0:4 * c1])
 
-        h_g = keep.tile([P, 4 * S], BF16, name="h_g", align_bytes=64)
-        h_c = keep.tile([P, S], U32, name="h_c", align_bytes=64)
-        h_s = keep.tile([P, S], U8, name="h_s", align_bytes=64)
-
         def penalise(c0, n):
             hf, ch, qt, cq = c0 // HALF, c0 % HALF, c0 // QUART, c0 % QUART
             nc.vector.tensor_tensor(
-                h_g[:, 4 * c0:4 * (c0 + n)].rearrange("p (c i t) -> p c t i", i=4, t=4),
-                best[hf][:, :, ch:ch + n].rearrange("p t (c i) -> p c t i", i=4),
-                weighted[qt][:, :, cq:cq + n].rearrange("p t (c i) -> p c t i", i=4), ALU.subtract)
+                h_g[:, 4 * c0:4 * (c0 + n)].rearrange("p (c e t) -> p c t e", e=4, t=TILES),
+                best[hf][:, :, ch:ch + n].rearrange("p t (c e) -> p c t e", e=4),
+                weighted[qt][:, :, cq:cq + n].rearrange("p t (c e) -> p c t e", e=4), ALU.subtract)
 
-        def quantise(c0, n):
+        def quantise_h(c0, n):
             nc.vector.quantize_mx(h_c[:, c0:c0 + n].bitcast(FP8X4), h_s[:, c0:c0 + n], h_g[:, 4 * c0:4 * (c0 + n)])
 
         out_rows = out.rearrange("(m p) j -> p m j", p=P)
@@ -242,74 +234,70 @@ def tile_list_clause_evaluator_kernel(
                 nc.scalar.activation(res[:, m, :], accs[m], ACT.Identity, bias=bo_t[:, m:m + 1])
             nc.sync.dma_start(out_rows[:, :, c0:c0 + n], res[:])
 
-        def last_scores(c0, bank_index):
+        def last_scores(c0, bank):
             res = keep.tile([P, 3, P], F32, name="res%d" % c0, align_bytes=64)
-            score_products(c0, P, bank_index)
+            score_products(c0, P, bank)
             nc.vector.tensor_tensor(
-                res[:], banks[bank_index][:, 0:3 * P].rearrange("p (m c) -> p m c", m=3),
-                bo_t.unsqueeze(2).broadcast_to([P, 3, P]), ALU.add)
+                res[:], banks[bank][:, 0:3 * P].rearrange("p (m c) -> p m c", m=3),
+                bo_t[:].unsqueeze(2).broadcast_to([P, 3, P]), ALU.add)
             nc.sync.dma_start(out_rows[:, :, c0:c0 + P], res[:])
 
         for a in range(PASSES):
-            for t in range(4):
+            for t in range(TILES):
                 infer_pass(a, 0, t, t)
-        for t in range(4):
+        for t in range(TILES):
             infer_copy(0, t, t)
-        round_w1(0, 0, nc.vector.tensor_copy)
-        round_w1(0, 1, nc.vector.tensor_copy)
+        round_w1(0, 0, 2, nc.vector.tensor_copy)
+        round_w1(0, 2, 2, nc.vector.tensor_copy)
         quantise_w1(0, H, w1_g0[:])
-        round_w1(1, 0, nc.vector.tensor_copy)
-        round_w1(1, 1, nc.scalar.copy)
-        for t in range(2):
+        round_w1(1, 0, 2, nc.vector.tensor_copy)
+        round_w1(1, 2, 1, nc.vector.tensor_copy)
+        round_w1(1, 3, 1, nc.scalar.copy)
+        for t in range(EARLY):
             for a in range(PASSES):
                 infer_pass(a, 1, t, t)
             infer_copy(1, t, t)
-        for t in range(4):
+
+        for t in range(TILES):
             goal_pass(0, 0, t, 4 + t)
         quantise_w1(H, 2 * P, w1_g[1, 0])
-        order_w3()
         quantise_w1(H + 2 * P, 2 * P, w1_g[1, 1])
-        w3_s = keep.tile([P, H], U8, name="w3_s", align_bytes=64)
-        nc.vector.tensor_copy(w3_s[:].bitcast(I32).rearrange("p (t b e) -> p t b e", t=4, e=2),
-                              w3_scale_rows[:].bitcast(I32).rearrange("p (b t e) -> p t b e", t=4, e=2))
-        for t in range(4):
+        order_w3_words()
+        order_w3_scales()
+        for t in range(TILES):
             goal_pass(1, 0, t, 4 + t)
-        for t in range(4):
+        for t in range(TILES):
             maximum(0, t, 4 + t)
-        length(0, 0, 2)
-        length(0, 1, 3)
-        length(1, 0, 0)
-        length(1, 1, 1)
+        length(0, 2)
+        length(1, 0)
         penalise(0, QUART)
-        for t in range(2, 4):
+        for t in range(EARLY, TILES):
             for a in range(PASSES):
                 infer_pass(a, 1, t, 2 + t)
             infer_copy(1, t, 2 + t)
         penalise(QUART, QUART)
         for m in range(3):
             round_w4(m)
-        quantise(0, QUART)
-        for t in range(4):
-            bank = (6, 7, 2, 3)[t]
+
+        quantise_h(0, QUART)
+        between = {0: lambda: quantise_h(QUART, QUART), 1: quantise_w4}
+        for t, bank in enumerate((6, 7, 2, 3)):
             for a in range(PASSES):
                 goal_pass(a, 1, t, bank)
             maximum(1, t, bank)
-            if t == 0:
-                quantise(QUART, QUART)
-            if t == 1:
-                quantise_w4()
-        length(2, 0, 0)
-        length(2, 1, 1)
+            if t in between:
+                between[t]()
+        length(2, 0)
         scores(0, QUART, 4)
-        length(3, 0, 6)
-        length(3, 1, 7)
+        length(3, 6)
         penalise(2 * QUART, QUART)
         scores(QUART, QUART, 2)
+
         penalise(3 * QUART, P)
-        quantise(2 * QUART, QUART)
+        quantise_h(2 * QUART, QUART)
         scores(2 * QUART, QUART, 0)
         penalise(3 * QUART + P, P)
-        quantise(3 * QUART, P)
+        quantise_h(3 * QUART, P)
         scores(3 * QUART, P, 4)
-        quantise(3 * QUART + P, P)
+        quantise_h(3 * QUART + P, P)
         last_scores(3 * QUART + P, 5)

@@ -21,24 +21,22 @@ PASSES = 2
 TILES = 4
 HALF = 512
 QUART = 256
-EARLY = 2
 
 LAP = 64
 W1A_AT = 0
 ROWS_AT = W1A_AT + 8192 - LAP
 W1B_AT = ROWS_AT + T - LAP
 W3ROWS_AT = ROWS_AT + 512
-BEST0_AT = W3ROWS_AT + LAP - 8192
-LATE_INF_AT = W1B_AT + LAP
-W3_AT = LATE_INF_AT + 8192
-LAM_AT = W3_AT + 4096
+W3_AT = W1B_AT + 8192
+PICKED_AT = W3_AT + 4096 - LAP
+LAM_AT = PICKED_AT + LAP
 BO_AT = LAM_AT + 128
 W4_AT = BO_AT + 64
-PICKED_AT = LAM_AT - 256
-TAB1_AT = W4_AT + 6144
-EARLY_INF_AT = TAB1_AT + 8192
-W4G_AT = EARLY_INF_AT + 5120
-W3C_AT = EARLY_INF_AT + 8192
+W2C_AT = W4_AT + 6144
+W2S_AT = W2C_AT + 4096
+INFER0_AT = W2S_AT + 1024
+W4G_AT = INFER0_AT + 5120
+BEST1_AT = INFER0_AT + 8192 - LAP
 
 
 def tile_list_clause_evaluator_kernel(
@@ -56,55 +54,56 @@ def tile_list_clause_evaluator_kernel(
 
         tab_scale_rows = reuse.tile([P, T], U8, name="tab_scale_rows", offset=ROWS_AT, align_bytes=64)
         nc.vector.memset(tab_scale_rows[:].bitcast(I32), 0)
-        w2_scale_rows = keep.tile([P, PASSES * H], U8, name="w2_scale_rows", align_bytes=64)
-        nc.vector.memset(w2_scale_rows[:].bitcast(I32), 0)
-        v_s = keep.tile([P, PASSES * S], U8, name="v_s", align_bytes=64)
-        nc.vector.memset(v_s[:].bitcast(I32), 0)
+        v_s = [keep.tile([P, PASSES * HALF], U8, name="v_s%d" % hf, align_bytes=64) for hf in range(2)]
+        w2_s = reuse.tile([P, PASSES * H], U8, name="w2_s", offset=W2S_AT, align_bytes=64)
+        nc.vector.memset(w2_s[:].bitcast(I32), 0)
+        for hf in range(2):
+            nc.vector.memset(v_s[hf][:].bitcast(I32), 0)
 
         w2_raw = keep.tile([P, PASSES, H // 2], I32, name="w2_raw", align_bytes=64)
         nc.sync.dma_start(w2_raw[:], w2_words.bitcast(I32).rearrange("a p c -> p a c"))
         nc.sync.dma_start(tab_scale_rows[0:P:4, :].bitcast(I32), tab_scales.bitcast(I32).rearrange("a q c -> q a c"))
-        tab = [keep.tile([P, T], I32, name="tab0", align_bytes=64),
-               reuse.tile([P, T], I32, name="tab1", offset=TAB1_AT, align_bytes=64)]
-
-        def load_table(a):
-            nc.sync.dma_start(tab[a][:], tab_words[a].rearrange("p t i -> p (t i)").bitcast(I32))
-
-        load_table(0)
+        w2_scale_rows = keep.tile([P, PASSES * H], U8, name="w2_scale_rows", align_bytes=64)
         for d in range(4):
             nc.sync.dma_start(
                 w2_scale_rows[32 * d:32 * d + 4, :].bitcast(I32).rearrange("p (a c) -> p a c", a=PASSES),
                 w2_scales.bitcast(I32)[:, 4 * d:4 * d + 4, :].rearrange("a s c -> s a c"))
-        load_table(1)
+        tab = [keep.tile([P, T], I32, name="tab%d" % a, align_bytes=64) for a in range(PASSES)]
+        for a in range(PASSES):
+            nc.sync.dma_start(tab[a][:], tab_words[a].rearrange("p t i -> p (t i)").bitcast(I32))
 
-        picked = reuse.tile([P, S], U8, name="picked", offset=PICKED_AT, align_bytes=64)
-        nc.vector.tensor_copy(picked[:, 0:S], tab_scale_rows[:].indirect(offsets[:]))
-        w3_scale_rows = reuse.tile([P, H], U8, name="w3_scale_rows", offset=W3ROWS_AT, align_bytes=64)
-        nc.vector.memset(w3_scale_rows[:].bitcast(I32), 0)
-        for d in (0, 2, 1, 3):
-            nc.sync.dma_start(
-                v_s[32 * d:32 * d + 4, :].bitcast(I32).rearrange("p (a c) -> p a c", a=PASSES),
-                picked[32 * d:32 * d + 32:4, 0:S].bitcast(I32))
+        w2_c = reuse.tile([P, PASSES * H // 2], I32, name="w2_c", offset=W2C_AT, align_bytes=64)
+        nc.scalar.copy(
+            w2_c[:].bitcast(U32).rearrange("p (a t b e) -> p a t b e", a=PASSES, t=TILES, e=4),
+            w2_raw[:].bitcast(U32).rearrange("p a (b t e) -> p a t b e", t=TILES, e=4))
+        for d in range(4):
+            nc.scalar.copy(
+                w2_s[32 * d:32 * d + 4, :].bitcast(U32).rearrange("p (a t b e) -> p a t b e", a=PASSES, t=TILES, e=2),
+                w2_scale_rows[32 * d:32 * d + 4, :].bitcast(U32).rearrange(
+                    "p (a b t e) -> p a t b e", a=PASSES, t=TILES, e=2))
+
+        picked = [keep.tile([P, HALF], U8, name="picked0", align_bytes=64),
+                  reuse.tile([P, HALF], U8, name="picked1", offset=PICKED_AT, align_bytes=64)]
+        for hf in range(2):
+            nc.vector.tensor_copy(picked[hf][:], tab_scale_rows[:].indirect(offsets[:, 32 * hf:32 * (hf + 1)]))
+            for d in (0, 2, 1, 3):
+                nc.scalar.dma_start(
+                    v_s[hf][32 * d:32 * d + 4, :].bitcast(I32).rearrange("p (a c) -> p a c", a=PASSES),
+                    picked[hf][32 * d:32 * d + 32:4, :].bitcast(I32))
 
         w1_raw = [reuse.tile([P, 4 * H], F32, name="w1_raw%d" % a, offset=at, align_bytes=64)
                   for a, at in enumerate((W1A_AT, W1B_AT))]
-
-        def load_w1(a):
+        for a in range(PASSES):
             nc.sync.dma_start(w1_raw[a][:], w1[512 * a:512 * (a + 1), :].rearrange("(p i) c -> p (i c)", i=4))
 
-        load_w1(0)
+        w3_scale_rows = reuse.tile([P, H], U8, name="w3_scale_rows", offset=W3ROWS_AT, align_bytes=64)
+        nc.vector.memset(w3_scale_rows[:].bitcast(I32), 0)
         for d in range(4):
             nc.sync.dma_start(w3_scale_rows[32 * d + 8:32 * d + 16, :].bitcast(I32),
                               w3_scales.bitcast(I32)[:, 4 * d:4 * d + 4, :])
-        load_w1(1)
-
         w3_raw = reuse.tile([P, PASSES, H], I32, name="w3_raw", offset=W3_AT, align_bytes=64)
         nc.sync.dma_start(
             w3_raw[:], w3_words.rearrange("a p c i -> a p (c i)").bitcast(I32).rearrange("a p c -> p a c"))
-        w2_s = keep.tile([P, PASSES * H], U8, name="w2_s", align_bytes=64)
-        nc.scalar.copy(
-            w2_s[:].bitcast(U32).rearrange("p (a t b e) -> p a t b e", a=PASSES, t=TILES, e=2),
-            w2_scale_rows[:].bitcast(U32).rearrange("p (a b t e) -> p a t b e", a=PASSES, t=TILES, e=2))
         lam_t = [reuse.tile([P, 1], F32, name="lam%d" % t, offset=LAM_AT + 32 * t) for t in range(TILES)]
         bo_t = reuse.tile([P, 3], F32, name="bo_t", offset=BO_AT)
         w4_raw = reuse.tile([P, TILES * N], F32, name="w4_raw", offset=W4_AT, align_bytes=64)
@@ -115,10 +114,6 @@ def tile_list_clause_evaluator_kernel(
                 nc.sync.dma_start(w4_raw[:, t * N:(t + 1) * N], w4.rearrange("(b t j) n -> t b j n", t=TILES, j=8)[t])
             nc.sync.dma_start(bo_t[:], bo.rearrange("(m p) -> p m", p=P))
 
-        w2_c = keep.tile([P, PASSES * H // 2], I32, name="w2_c", align_bytes=64)
-        nc.scalar.copy(
-            w2_c[:].bitcast(U32).rearrange("p (a t b e) -> p a t b e", a=PASSES, t=TILES, e=4),
-            w2_raw[:].bitcast(U32).rearrange("p a (b t e) -> p a t b e", t=TILES, e=4))
         v_c = {}
         for a in range(PASSES):
             for hf in range(2):
@@ -130,61 +125,73 @@ def tile_list_clause_evaluator_kernel(
             hf, ch = c0 // HALF, c0 % HALF
             nc.tensor.matmul_mx(
                 acc, lhsT=codes, lhsT_scale=scales, rhs=v_c[a, hf][:, ch:ch + n].bitcast(FP8X4),
-                rhs_scale=v_s[:, a * S + c0:a * S + c0 + n], start=(a == 0), stop=(a == PASSES - 1))
+                rhs_scale=v_s[hf][:, a * HALF + ch:a * HALF + ch + n], start=(a == 0), stop=(a == PASSES - 1))
 
-        infer = {(hf, t): reuse.tile([P, HALF], F32, name="infer%d_%d" % (hf, t), offset=at + 2048 * t, align_bytes=64)
-                 for hf, at in enumerate((EARLY_INF_AT, LATE_INF_AT)) for t in range(TILES)}
-
-        def infer_pass(a, hf, t, bank):
-            c = a * H + t * P
-            one_pass(banks[bank][:], w2_c[:, c // 2:(c + P) // 2].bitcast(FP4X4), w2_s[:, c:c + P], a, hf * HALF, HALF)
-
-        def infer_copy(hf, t, bank):
-            nc.scalar.copy(infer[hf, t][:], banks[bank][:])
+        infer = [reuse.tile([P, TILES, HALF], F32, name="infer0", offset=INFER0_AT, align_bytes=64),
+                 keep.tile([P, TILES, HALF], F32, name="infer1", align_bytes=64)]
+        for hf in range(2):
+            for a in range(PASSES):
+                for t in range(TILES):
+                    c = a * H + t * P
+                    one_pass(banks[4 * hf + t][:], w2_c[:, c // 2:(c + P) // 2].bitcast(FP4X4), w2_s[:, c:c + P],
+                             a, hf * HALF, HALF)
+            for t in range(TILES):
+                nc.scalar.copy(infer[hf][:, t, :], banks[4 * hf + t][:])
 
         w1_c = keep.tile([P, PASSES * H], U32, name="w1_c", align_bytes=64)
         w1_s = keep.tile([P, PASSES * H], U8, name="w1_s", align_bytes=64)
-        w1_g0 = keep.tile([P, 4 * H], BF16, name="w1_g0", align_bytes=64)
-        w1_g10 = keep.tile([P, 2 * H], BF16, name="w1_g10", align_bytes=64)
-        w1_g11 = reuse.tile([P, 2 * H], BF16, name="w1_g11", offset=W3C_AT, align_bytes=64)
-        w1_g = {(0, 0): w1_g0[:, 0:2 * H], (0, 1): w1_g0[:, 2 * H:], (1, 0): w1_g10[:], (1, 1): w1_g11[:]}
+        w1_g = [keep.tile([P, 4 * H], BF16, name="w1_g%d" % a, align_bytes=64) for a in range(PASSES)]
 
-        def round_w1(a, t0, count, copy):
-            copy(w1_g[a, t0 // 2].rearrange("p (t b j i) -> p t b j i", t=2, j=8, i=4)[:, t0 % 2:t0 % 2 + count],
-                 w1_raw[a][:].rearrange("p (i b t j) -> p t b j i", i=4, t=TILES, j=8)[:, t0:t0 + count])
+        def round_w1(a, t):
+            nc.vector.tensor_copy(
+                w1_g[a][:, t * H:(t + 1) * H].rearrange("p (b u e i) -> p b u i e", u=2, e=4, i=4),
+                w1_raw[a][:].rearrange("p (i b t u e) -> p t b u i e", i=4, t=TILES, u=2, e=4)[:, t])
 
-        def quantise_w1(c, n, rounded):
-            nc.vector.quantize_mx(w1_c[:, c:c + n].bitcast(FP8X4), w1_s[:, c:c + n], rounded)
+        def quantise_w1(a, t0, count):
+            c, n = a * H + t0 * P, count * P
+            nc.vector.quantize_mx(w1_c[:, c:c + n].bitcast(FP8X4), w1_s[:, c:c + n],
+                                  w1_g[a][:, t0 * H:(t0 + count) * H])
 
-        def goal_pass(a, hf, t, bank):
+        def goal_pass(acc, a, t, c0, n):
             c = a * H + t * P
-            one_pass(banks[bank][:], w1_c[:, c:c + P].bitcast(FP8X4), w1_s[:, c:c + P], a, hf * HALF, HALF)
+            one_pass(acc, w1_c[:, c:c + P].bitcast(FP8X4), w1_s[:, c:c + P], a, c0, n)
 
-        best = [reuse.tile([P, TILES, HALF], F32, name="best0", offset=BEST0_AT, align_bytes=64),
-                keep.tile([P, TILES, HALF], F32, name="best1", align_bytes=64)]
-
-        def maximum(hf, t, bank):
-            nc.vector.tensor_tensor(best[hf][:, t, :], banks[bank][:], infer[hf, t][:], ALU.max)
-
-        w3_c = reuse.tile([P, PASSES * H], I32, name="w3_c", offset=W3C_AT, align_bytes=64)
-        weighted = [keep.tile([P, TILES, QUART], F32, name="weighted%d" % qt, align_bytes=64) for qt in range(4)]
+        best = [keep.tile([P, TILES, HALF], F32, name="best0", align_bytes=64),
+                reuse.tile([P, TILES, HALF], F32, name="best1", offset=BEST1_AT, align_bytes=64)]
+        w3_c = reuse.tile([P, PASSES * H], I32, name="w3_c", offset=W2C_AT, align_bytes=64)
+        w3_s = reuse.tile([P, H], U8, name="w3_s", offset=W2S_AT, align_bytes=64)
+        weighted = [reuse.tile([P, TILES, QUART], F32, name="weighted2", offset=W4_AT + 2048, align_bytes=64) if qt == 2
+                    else keep.tile([P, TILES, QUART], F32, name="weighted%d" % qt, align_bytes=64) for qt in range(4)]
         w4_g = reuse.tile([P, TILES * N], BF16, name="w4_g", offset=W4G_AT, align_bytes=64)
         w4_c = keep.tile([P, N], U32, name="w4_c", align_bytes=64)
         w4_s = keep.tile([P, N], U8, name="w4_s", align_bytes=64)
         h_g = keep.tile([P, TILES * S], BF16, name="h_g", align_bytes=64)
         h_c = keep.tile([P, S], U32, name="h_c", align_bytes=64)
         h_s = keep.tile([P, S], U8, name="h_s", align_bytes=64)
-        w3_s = keep.tile([P, H], U8, name="w3_s", align_bytes=64)
 
-        def order_w3_words():
-            nc.vector.tensor_copy(
-                w3_c[:].rearrange("p (a t b j) -> p a t b j", a=PASSES, t=TILES, j=8),
-                w3_raw[:].rearrange("p a (b t j) -> p a t b j", t=TILES, j=8))
+        def order_w3_words(pair):
+            nc.scalar.copy(
+                w3_c[:].bitcast(U32).rearrange("p (a t b j) -> p a t b j", a=PASSES, t=TILES, j=8)[:, :, 2 * pair:2 * pair + 2],
+                w3_raw[:].bitcast(U32).rearrange("p a (b t j) -> p a t b j", t=TILES, j=8)[:, :, 2 * pair:2 * pair + 2])
 
         def order_w3_scales():
-            nc.vector.tensor_copy(
-                w3_s[:].bitcast(I32).rearrange("p (t b e) -> p t b e", t=TILES, e=2),
-                w3_scale_rows[:].bitcast(I32).rearrange("p (b t e) -> p t b e", t=TILES, e=2))
+            nc.scalar.copy(
+                w3_s[:].bitcast(U32).rearrange("p (t b e) -> p t b e", t=TILES, e=2),
+                w3_scale_rows[:].bitcast(U32).rearrange("p (b t e) -> p t b e", t=TILES, e=2))
+
+        def goal_quarter(qt, first_bank):
+            for t in range(TILES):
+                acc = banks[first_bank + t // 2][:, (t % 2) * QUART:(t % 2 + 1) * QUART]
+                for a in range(PASSES):
+                    goal_pass(acc, a, t, qt * QUART, QUART)
+
+        def maximum_quarter(qt, first_bank):
+            hf, ch = qt // 2, (qt % 2) * QUART
+            for pair in range(2):
+                nc.vector.tensor_tensor(
+                    best[hf][:, 2 * pair:2 * pair + 2, ch:ch + QUART],
+                    banks[first_bank + pair][:].rearrange("p (t c) -> p t c", t=2),
+                    infer[hf][:, 2 * pair:2 * pair + 2, ch:ch + QUART], ALU.max)
 
         def length(qt, first_bank):
             for pair in range(2):
@@ -203,8 +210,7 @@ def tile_list_clause_evaluator_kernel(
                            w4_raw[:].rearrange("p (t c e) -> p c t e", e=4, t=TILES)[:, 32 * m:32 * (m + 1)])
 
         def quantise_w4():
-            for c0, c1 in ((0, 256), (256, N)):
-                nc.vector.quantize_mx(w4_c[:, c0:c1].bitcast(FP8X4), w4_s[:, c0:c1], w4_g[:, 4 * c0:4 * c1])
+            nc.vector.quantize_mx(w4_c[:].bitcast(FP8X4), w4_s[:], w4_g[:])
 
         def penalise(c0, n):
             hf, ch, qt, cq = c0 // HALF, c0 % HALF, c0 // QUART, c0 % QUART
@@ -242,62 +248,46 @@ def tile_list_clause_evaluator_kernel(
                 bo_t[:].unsqueeze(2).broadcast_to([P, 3, P]), ALU.add)
             nc.sync.dma_start(out_rows[:, :, c0:c0 + P], res[:])
 
-        for a in range(PASSES):
-            for t in range(TILES):
-                infer_pass(a, 0, t, t)
         for t in range(TILES):
-            infer_copy(0, t, t)
-        round_w1(0, 0, 2, nc.vector.tensor_copy)
-        round_w1(0, 2, 2, nc.vector.tensor_copy)
-        quantise_w1(0, H, w1_g0[:])
-        round_w1(1, 0, 2, nc.vector.tensor_copy)
-        round_w1(1, 2, 1, nc.vector.tensor_copy)
-        round_w1(1, 3, 1, nc.scalar.copy)
-        for t in range(EARLY):
-            for a in range(PASSES):
-                infer_pass(a, 1, t, t)
-            infer_copy(1, t, t)
-
+            round_w1(0, t)
+        quantise_w1(0, 0, TILES)
         for t in range(TILES):
-            goal_pass(0, 0, t, 4 + t)
-        quantise_w1(H, 2 * P, w1_g[1, 0])
-        quantise_w1(H + 2 * P, 2 * P, w1_g[1, 1])
-        order_w3_words()
+            goal_pass(banks[t][:], 0, t, 0, HALF)
+        for t in range(3):
+            round_w1(1, t)
+        quantise_w1(1, 0, 2)
+        round_w1(1, 3)
+        quantise_w1(1, 2, 2)
+        order_w3_words(0)
         order_w3_scales()
+        order_w3_words(1)
         for t in range(TILES):
-            goal_pass(1, 0, t, 4 + t)
+            goal_pass(banks[t][:], 1, t, 0, HALF)
         for t in range(TILES):
-            maximum(0, t, 4 + t)
-        length(0, 2)
-        length(1, 0)
+            nc.vector.tensor_tensor(best[0][:, t, :], banks[t][:], infer[0][:, t, :], ALU.max)
+        length(0, 4)
+        length(1, 6)
         penalise(0, QUART)
-        for t in range(EARLY, TILES):
-            for a in range(PASSES):
-                infer_pass(a, 1, t, 2 + t)
-            infer_copy(1, t, 2 + t)
         penalise(QUART, QUART)
         for m in range(3):
             round_w4(m)
-
-        quantise_h(0, QUART)
-        between = {0: lambda: quantise_h(QUART, QUART), 1: quantise_w4}
-        for t, bank in enumerate((6, 7, 2, 3)):
-            for a in range(PASSES):
-                goal_pass(a, 1, t, bank)
-            maximum(1, t, bank)
-            if t in between:
-                between[t]()
+        goal_quarter(2, 4)
         length(2, 0)
-        scores(0, QUART, 4)
-        length(3, 6)
+        goal_quarter(3, 6)
+        quantise_h(0, QUART)
+        quantise_w4()
+        quantise_h(QUART, QUART)
+        scores(0, QUART, 2)
+        scores(QUART, QUART, 0)
+        maximum_quarter(2, 4)
+        length(3, 4)
         penalise(2 * QUART, QUART)
-        scores(QUART, QUART, 2)
-
-        penalise(3 * QUART, P)
+        maximum_quarter(3, 6)
         quantise_h(2 * QUART, QUART)
-        scores(2 * QUART, QUART, 0)
+        scores(2 * QUART, QUART, 2)
+        penalise(3 * QUART, P)
         penalise(3 * QUART + P, P)
         quantise_h(3 * QUART, P)
-        scores(3 * QUART, P, 4)
+        scores(3 * QUART, P, 6)
         quantise_h(3 * QUART + P, P)
-        last_scores(3 * QUART + P, 5)
+        last_scores(3 * QUART + P, 7)

@@ -1,6 +1,7 @@
 from contextlib import ExitStack
 
 import concourse.mybir as mybir
+from concourse.masks import make_identity
 
 K, T, S, H, N = 1024, 2048, 1024, 512, 384
 FLOPS = 2 * K * H * S * 3 + 2 * H * N * S
@@ -21,16 +22,17 @@ PASSES = 2
 TILES = 4
 HALF = 512
 QUART = 256
+WARM = 3
 
 LAP = 64
 W1A_AT = 0
 ROWS_AT = W1A_AT + 8192 - LAP
 W1B_AT = ROWS_AT + T - LAP
 W3ROWS_AT = ROWS_AT + 512
+IDLE_AT = W3ROWS_AT + 512
 W3_AT = W1B_AT + 8192
 PICKED_AT = W3_AT + 4096 - LAP
-LAM_AT = PICKED_AT + LAP
-BO_AT = LAM_AT + 128
+BO_AT = PICKED_AT + LAP
 W4_AT = BO_AT + 64
 W2C_AT = W4_AT + 6144
 W2S_AT = W2C_AT + 4096
@@ -54,42 +56,57 @@ def tile_list_clause_evaluator_kernel(
 
         tab_scale_rows = reuse.tile([P, T], U8, name="tab_scale_rows", offset=ROWS_AT, align_bytes=64)
         nc.vector.memset(tab_scale_rows[:].bitcast(I32), 0)
-        v_s = [keep.tile([P, PASSES * HALF], U8, name="v_s%d" % hf, align_bytes=64) for hf in range(2)]
+        v_s = keep.tile([P, PASSES * S], U8, name="v_s", align_bytes=64)
         w2_s = reuse.tile([P, PASSES * H], U8, name="w2_s", offset=W2S_AT, align_bytes=64)
-        nc.vector.memset(w2_s[:].bitcast(I32), 0)
-        for hf in range(2):
-            nc.vector.memset(v_s[hf][:].bitcast(I32), 0)
+        w2_scale_rows = keep.tile([P, PASSES * H], U8, name="w2_scale_rows", align_bytes=64)
+        nc.vector.memset(w2_scale_rows[:].bitcast(I32), 0)
+        lam_rows = keep.tile([P, P], F32, name="lam_rows", align_bytes=64)
+        nc.vector.memset(lam_rows[:], 0.0)
+        identity = keep.tile([P, P], F32, name="identity", align_bytes=64)
+        nc.vector.memset(identity[:], 0.0)
+        make_identity(nc, identity[:], nomemset=True)
+        nc.vector.memset(v_s[:].bitcast(I32), 0)
+        idle_g = keep.tile([P, 4 * P], BF16, name="idle_g", align_bytes=64)
+        nc.vector.memset(idle_g[:].bitcast(I32), 0)
+        idle_c = keep.tile([P, P], U32, name="idle_c", align_bytes=64)
+        idle_s = keep.tile([P, P], U8, name="idle_s", align_bytes=64)
+        nc.vector.memset(idle_s[:].bitcast(I32), 0)
+        nc.vector.quantize_mx(idle_c[:].bitcast(FP8X4), idle_s[:], idle_g[:])
 
         w2_raw = keep.tile([P, PASSES, H // 2], I32, name="w2_raw", align_bytes=64)
         nc.sync.dma_start(w2_raw[:], w2_words.bitcast(I32).rearrange("a p c -> p a c"))
         nc.sync.dma_start(tab_scale_rows[0:P:4, :].bitcast(I32), tab_scales.bitcast(I32).rearrange("a q c -> q a c"))
-        w2_scale_rows = keep.tile([P, PASSES * H], U8, name="w2_scale_rows", align_bytes=64)
-        for d in range(4):
+        tab = [keep.tile([P, T], I32, name="tab%d" % a, align_bytes=64) for a in range(PASSES)]
+
+        def load_table(a):
+            nc.sync.dma_start(tab[a][:], tab_words[a].rearrange("p t i -> p (t i)").bitcast(I32))
+
+        load_table(0)
+        for d in (0, 2, 1, 3):
             nc.sync.dma_start(
                 w2_scale_rows[32 * d:32 * d + 4, :].bitcast(I32).rearrange("p (a c) -> p a c", a=PASSES),
                 w2_scales.bitcast(I32)[:, 4 * d:4 * d + 4, :].rearrange("a s c -> s a c"))
-        tab = [keep.tile([P, T], I32, name="tab%d" % a, align_bytes=64) for a in range(PASSES)]
-        for a in range(PASSES):
-            nc.sync.dma_start(tab[a][:], tab_words[a].rearrange("p t i -> p (t i)").bitcast(I32))
+        nc.sync.dma_start(lam_rows[0:TILES, :].rearrange("t (b j) -> t b j", j=8),
+                          lam.rearrange("(b t j) -> t b j", t=TILES, j=8))
+        load_table(1)
+        nc.tensor.transpose(banks[7][:, 0:P], lam_rows[:], identity[:])
+        lam_t = keep.tile([P, TILES], F32, name="lam_t")
+        nc.scalar.copy(lam_t[:], banks[7][:, 0:TILES])
 
         w2_c = reuse.tile([P, PASSES * H // 2], I32, name="w2_c", offset=W2C_AT, align_bytes=64)
         nc.scalar.copy(
             w2_c[:].bitcast(U32).rearrange("p (a t b e) -> p a t b e", a=PASSES, t=TILES, e=4),
             w2_raw[:].bitcast(U32).rearrange("p a (b t e) -> p a t b e", t=TILES, e=4))
-        for d in range(4):
-            nc.scalar.copy(
-                w2_s[32 * d:32 * d + 4, :].bitcast(U32).rearrange("p (a t b e) -> p a t b e", a=PASSES, t=TILES, e=2),
-                w2_scale_rows[32 * d:32 * d + 4, :].bitcast(U32).rearrange(
-                    "p (a b t e) -> p a t b e", a=PASSES, t=TILES, e=2))
+        nc.scalar.copy(
+            w2_s[:].bitcast(U32).rearrange("p (a t b e) -> p a t b e", a=PASSES, t=TILES, e=2),
+            w2_scale_rows[:].bitcast(U32).rearrange("p (a b t e) -> p a t b e", a=PASSES, t=TILES, e=2))
 
-        picked = [keep.tile([P, HALF], U8, name="picked0", align_bytes=64),
-                  reuse.tile([P, HALF], U8, name="picked1", offset=PICKED_AT, align_bytes=64)]
-        for hf in range(2):
-            nc.vector.tensor_copy(picked[hf][:], tab_scale_rows[:].indirect(offsets[:, 32 * hf:32 * (hf + 1)]))
-            for d in (0, 2, 1, 3):
-                nc.scalar.dma_start(
-                    v_s[hf][32 * d:32 * d + 4, :].bitcast(I32).rearrange("p (a c) -> p a c", a=PASSES),
-                    picked[hf][32 * d:32 * d + 32:4, :].bitcast(I32))
+        picked = reuse.tile([P, S], U8, name="picked", offset=PICKED_AT, align_bytes=64)
+        nc.vector.tensor_copy(picked[:], tab_scale_rows[:].indirect(offsets[:]))
+        for d in (0, 2, 1, 3):
+            nc.sync.dma_start(
+                v_s[32 * d:32 * d + 4, :].bitcast(I32).rearrange("p (a c) -> p a c", a=PASSES),
+                picked[32 * d:32 * d + 32:4, :].bitcast(I32))
 
         w1_raw = [reuse.tile([P, 4 * H], F32, name="w1_raw%d" % a, offset=at, align_bytes=64)
                   for a, at in enumerate((W1A_AT, W1B_AT))]
@@ -98,18 +115,21 @@ def tile_list_clause_evaluator_kernel(
 
         w3_scale_rows = reuse.tile([P, H], U8, name="w3_scale_rows", offset=W3ROWS_AT, align_bytes=64)
         nc.vector.memset(w3_scale_rows[:].bitcast(I32), 0)
+        idle_plane = reuse.tile([P, HALF], U8, name="idle_plane", offset=IDLE_AT, align_bytes=64)
+        nc.scalar.copy(idle_plane[:].bitcast(U32).rearrange("p (r c) -> p r c", r=4),
+                       idle_s[:].bitcast(U32).unsqueeze(1).broadcast_to([P, 4, P // 4]))
+        for i in range(WARM):
+            nc.tensor.matmul_mx(banks[6][:], lhsT=idle_c[:].bitcast(FP8X4), lhsT_scale=idle_s[:],
+                                rhs=w2_raw[:, 0, :].bitcast(FP4X4), rhs_scale=idle_plane[:], start=True, stop=True)
         for d in range(4):
             nc.sync.dma_start(w3_scale_rows[32 * d + 8:32 * d + 16, :].bitcast(I32),
                               w3_scales.bitcast(I32)[:, 4 * d:4 * d + 4, :])
         w3_raw = reuse.tile([P, PASSES, H], I32, name="w3_raw", offset=W3_AT, align_bytes=64)
         nc.sync.dma_start(
             w3_raw[:], w3_words.rearrange("a p c i -> a p (c i)").bitcast(I32).rearrange("a p c -> p a c"))
-        lam_t = [reuse.tile([P, 1], F32, name="lam%d" % t, offset=LAM_AT + 32 * t) for t in range(TILES)]
         bo_t = reuse.tile([P, 3], F32, name="bo_t", offset=BO_AT)
         w4_raw = reuse.tile([P, TILES * N], F32, name="w4_raw", offset=W4_AT, align_bytes=64)
         with nc.allow_non_contiguous_dma(reason="one value a partition"):
-            for t in range(TILES):
-                nc.sync.dma_start(lam_t[t][:], lam.rearrange("(b t j) -> t b j", t=TILES, j=8)[t])
             for t in range(TILES):
                 nc.sync.dma_start(w4_raw[:, t * N:(t + 1) * N], w4.rearrange("(b t j) n -> t b j n", t=TILES, j=8)[t])
             nc.sync.dma_start(bo_t[:], bo.rearrange("(m p) -> p m", p=P))
@@ -125,7 +145,7 @@ def tile_list_clause_evaluator_kernel(
             hf, ch = c0 // HALF, c0 % HALF
             nc.tensor.matmul_mx(
                 acc, lhsT=codes, lhsT_scale=scales, rhs=v_c[a, hf][:, ch:ch + n].bitcast(FP8X4),
-                rhs_scale=v_s[hf][:, a * HALF + ch:a * HALF + ch + n], start=(a == 0), stop=(a == PASSES - 1))
+                rhs_scale=v_s[:, a * S + c0:a * S + c0 + n], start=(a == 0), stop=(a == PASSES - 1))
 
         infer = [reuse.tile([P, TILES, HALF], F32, name="infer0", offset=INFER0_AT, align_bytes=64),
                  keep.tile([P, TILES, HALF], F32, name="infer1", align_bytes=64)]
@@ -135,7 +155,7 @@ def tile_list_clause_evaluator_kernel(
                     c = a * H + t * P
                     one_pass(banks[4 * hf + t][:], w2_c[:, c // 2:(c + P) // 2].bitcast(FP4X4), w2_s[:, c:c + P],
                              a, hf * HALF, HALF)
-            for t in range(TILES):
+            for t in range(TILES if hf == 0 else 2):
                 nc.scalar.copy(infer[hf][:, t, :], banks[4 * hf + t][:])
 
         w1_c = keep.tile([P, PASSES * H], U32, name="w1_c", align_bytes=64)
@@ -203,7 +223,7 @@ def tile_list_clause_evaluator_kernel(
                         one_pass(accs[t], w3_c[:, c:c + P].bitcast(FP8X4), w3_s[8 + 4 * a:P, t * P:(t + 1) * P],
                                  a, qt * QUART, QUART)
                 for t in tiles:
-                    nc.scalar.activation(weighted[qt][:, t, :], accs[t], ACT.Copy, scale=lam_t[t][:])
+                    nc.scalar.activation(weighted[qt][:, t, :], accs[t], ACT.Copy, scale=lam_t[:, t:t + 1])
 
         def round_w4(m):
             nc.scalar.copy(w4_g[:].rearrange("p (c e t) -> p c t e", e=4, t=TILES)[:, 32 * m:32 * (m + 1)],
@@ -261,6 +281,8 @@ def tile_list_clause_evaluator_kernel(
         order_w3_words(0)
         order_w3_scales()
         order_w3_words(1)
+        for t in range(2, TILES):
+            nc.scalar.copy(infer[1][:, t, :], banks[4 + t][:])
         for t in range(TILES):
             goal_pass(banks[t][:], 1, t, 0, HALF)
         for t in range(TILES):

@@ -28,17 +28,15 @@ LAP = 64
 W1A_AT = 0
 ROWS_AT = W1A_AT + 8192 - LAP
 W1B_AT = ROWS_AT + T - LAP
-W3ROWS_AT = ROWS_AT + 512
-IDLE_AT = W3ROWS_AT + 512
-W3_AT = W1B_AT + 8192
-PICKED_AT = W3_AT + 4096 - LAP
-BO_AT = PICKED_AT + LAP
+IDLE_AT = ROWS_AT + 1024
+BO_AT = W1A_AT
 W4_AT = BO_AT + 64
-W2C_AT = W4_AT + 6144
-W2S_AT = W2C_AT + 4096
-INFER0_AT = W2S_AT + 1024
-W4G_AT = INFER0_AT + 5120
-BEST1_AT = INFER0_AT + 8192 - LAP
+W3_AT = W1B_AT + 8192
+W3ROWS_AT = W3_AT + 4096
+PICKED_AT = W3ROWS_AT - LAP
+EARLY_AT = PICKED_AT + S
+LATE1_AT = EARLY_AT + 8192
+WEIGHTED0_AT = LATE1_AT + 4096 - LAP
 
 
 def tile_list_clause_evaluator_kernel(
@@ -57,7 +55,7 @@ def tile_list_clause_evaluator_kernel(
         tab_scale_rows = reuse.tile([P, T], U8, name="tab_scale_rows", offset=ROWS_AT, align_bytes=64)
         nc.vector.memset(tab_scale_rows[:].bitcast(I32), 0)
         v_s = keep.tile([P, PASSES * S], U8, name="v_s", align_bytes=64)
-        w2_s = reuse.tile([P, PASSES * H], U8, name="w2_s", offset=W2S_AT, align_bytes=64)
+        w2_s = keep.tile([P, PASSES * H], U8, name="w2_s", align_bytes=64)
         w2_scale_rows = keep.tile([P, PASSES * H], U8, name="w2_scale_rows", align_bytes=64)
         nc.vector.memset(w2_scale_rows[:].bitcast(I32), 0)
         lam_rows = keep.tile([P, P], F32, name="lam_rows", align_bytes=64)
@@ -66,6 +64,8 @@ def tile_list_clause_evaluator_kernel(
         nc.vector.memset(identity[:], 0.0)
         make_identity(nc, identity[:], nomemset=True)
         nc.vector.memset(v_s[:].bitcast(I32), 0)
+        zeros = keep.tile([P, P], U32, name="zeros", align_bytes=64)
+        nc.vector.memset(zeros[:], 0)
         idle_g = keep.tile([P, 4 * P], BF16, name="idle_g", align_bytes=64)
         nc.vector.memset(idle_g[:].bitcast(I32), 0)
         idle_c = keep.tile([P, P], U32, name="idle_c", align_bytes=64)
@@ -93,7 +93,7 @@ def tile_list_clause_evaluator_kernel(
         lam_t = keep.tile([P, TILES], F32, name="lam_t")
         nc.scalar.copy(lam_t[:], banks[7][:, 0:TILES])
 
-        w2_c = reuse.tile([P, PASSES * H // 2], I32, name="w2_c", offset=W2C_AT, align_bytes=64)
+        w2_c = keep.tile([P, PASSES * H // 2], I32, name="w2_c", align_bytes=64)
         nc.scalar.copy(
             w2_c[:].bitcast(U32).rearrange("p (a t b e) -> p a t b e", a=PASSES, t=TILES, e=4),
             w2_raw[:].bitcast(U32).rearrange("p a (b t e) -> p a t b e", t=TILES, e=4))
@@ -113,20 +113,20 @@ def tile_list_clause_evaluator_kernel(
         for a in range(PASSES):
             nc.sync.dma_start(w1_raw[a][:], w1[512 * a:512 * (a + 1), :].rearrange("(p i) c -> p (i c)", i=4))
 
-        w3_scale_rows = reuse.tile([P, H], U8, name="w3_scale_rows", offset=W3ROWS_AT, align_bytes=64)
-        nc.vector.memset(w3_scale_rows[:].bitcast(I32), 0)
         idle_plane = reuse.tile([P, HALF], U8, name="idle_plane", offset=IDLE_AT, align_bytes=64)
         nc.scalar.copy(idle_plane[:].bitcast(U32).rearrange("p (r c) -> p r c", r=4),
                        idle_s[:].bitcast(U32).unsqueeze(1).broadcast_to([P, 4, P // 4]))
         for i in range(WARM):
             nc.tensor.matmul_mx(banks[6][:], lhsT=idle_c[:].bitcast(FP8X4), lhsT_scale=idle_s[:],
                                 rhs=w2_raw[:, 0, :].bitcast(FP4X4), rhs_scale=idle_plane[:], start=True, stop=True)
-        for d in range(4):
-            nc.sync.dma_start(w3_scale_rows[32 * d + 8:32 * d + 16, :].bitcast(I32),
-                              w3_scales.bitcast(I32)[:, 4 * d:4 * d + 4, :])
         w3_raw = reuse.tile([P, PASSES, H], I32, name="w3_raw", offset=W3_AT, align_bytes=64)
         nc.sync.dma_start(
             w3_raw[:], w3_words.rearrange("a p c i -> a p (c i)").bitcast(I32).rearrange("a p c -> p a c"))
+        w3_scale_rows = reuse.tile([P, H], U8, name="w3_scale_rows", offset=W3ROWS_AT, align_bytes=64)
+        nc.scalar.copy(w3_scale_rows[:].bitcast(U32), zeros[:])
+        for d in range(4):
+            nc.sync.dma_start(w3_scale_rows[32 * d + 8:32 * d + 16, :].bitcast(I32),
+                              w3_scales.bitcast(I32)[:, 4 * d:4 * d + 4, :])
         bo_t = reuse.tile([P, 3], F32, name="bo_t", offset=BO_AT)
         w4_raw = reuse.tile([P, TILES * N], F32, name="w4_raw", offset=W4_AT, align_bytes=64)
         with nc.allow_non_contiguous_dma(reason="one value a partition"):
@@ -141,22 +141,36 @@ def tile_list_clause_evaluator_kernel(
                 nc.vector.tensor_copy(
                     v_c[a, hf][:], tab[a][:].bitcast(U32).indirect(offsets[:, 32 * hf:32 * (hf + 1)]))
 
-        def one_pass(acc, codes, scales, a, c0, n):
+        def one_pass(acc, codes, scales, a, c0, n, opens=True, closes=True):
             hf, ch = c0 // HALF, c0 % HALF
             nc.tensor.matmul_mx(
                 acc, lhsT=codes, lhsT_scale=scales, rhs=v_c[a, hf][:, ch:ch + n].bitcast(FP8X4),
-                rhs_scale=v_s[:, a * S + c0:a * S + c0 + n], start=(a == 0), stop=(a == PASSES - 1))
+                rhs_scale=v_s[:, a * S + c0:a * S + c0 + n],
+                start=(a == 0 and opens), stop=(a == PASSES - 1 and closes))
 
-        infer = [reuse.tile([P, TILES, HALF], F32, name="infer0", offset=INFER0_AT, align_bytes=64),
-                 keep.tile([P, TILES, HALF], F32, name="infer1", align_bytes=64)]
-        for hf in range(2):
+        early = reuse.tile([P, TILES, HALF], F32, name="early", offset=EARLY_AT, align_bytes=64)
+        late = [keep.tile([P, 2, HALF], F32, name="late0", align_bytes=64),
+                reuse.tile([P, 2, HALF], F32, name="late1", offset=LATE1_AT, align_bytes=64)]
+
+        def infer_rows(hf, pair):
+            return early[:, 2 * pair:2 * pair + 2, :] if hf == 0 else late[pair][:]
+
+        def infer_passes(hf, tiles, first_bank):
             for a in range(PASSES):
-                for t in range(TILES):
+                for i, t in enumerate(tiles):
                     c = a * H + t * P
-                    one_pass(banks[4 * hf + t][:], w2_c[:, c // 2:(c + P) // 2].bitcast(FP4X4), w2_s[:, c:c + P],
+                    one_pass(banks[first_bank + i][:], w2_c[:, c // 2:(c + P) // 2].bitcast(FP4X4), w2_s[:, c:c + P],
                              a, hf * HALF, HALF)
-            for t in range(TILES if hf == 0 else 2):
-                nc.scalar.copy(infer[hf][:, t, :], banks[4 * hf + t][:])
+
+        def infer_copy(hf, t, bank):
+            nc.scalar.copy(infer_rows(hf, t // 2)[:, t % 2, :], banks[bank][:])
+
+        infer_passes(0, range(TILES), 0)
+        for t in range(TILES):
+            infer_copy(0, t, t)
+        infer_passes(1, (0, 1), 4)
+        for t in range(2):
+            infer_copy(1, t, 4 + t)
 
         w1_c = keep.tile([P, PASSES * H], U32, name="w1_c", align_bytes=64)
         w1_s = keep.tile([P, PASSES * H], U8, name="w1_s", align_bytes=64)
@@ -172,17 +186,20 @@ def tile_list_clause_evaluator_kernel(
             nc.vector.quantize_mx(w1_c[:, c:c + n].bitcast(FP8X4), w1_s[:, c:c + n],
                                   w1_g[a][:, t0 * H:(t0 + count) * H])
 
-        def goal_pass(acc, a, t, c0, n):
+        def goal_pass(a, t, qt, pair_banks):
             c = a * H + t * P
-            one_pass(acc, w1_c[:, c:c + P].bitcast(FP8X4), w1_s[:, c:c + P], a, c0, n)
+            one_pass(banks[pair_banks[t // 2]][:, (t % 2) * QUART:(t % 2 + 1) * QUART],
+                     w1_c[:, c:c + P].bitcast(FP8X4), w1_s[:, c:c + P], a, qt * QUART, QUART,
+                     opens=(t % 2 == 0), closes=(t % 2 == 1))
 
         best = [keep.tile([P, TILES, HALF], F32, name="best0", align_bytes=64),
-                reuse.tile([P, TILES, HALF], F32, name="best1", offset=BEST1_AT, align_bytes=64)]
-        w3_c = reuse.tile([P, PASSES * H], I32, name="w3_c", offset=W2C_AT, align_bytes=64)
-        w3_s = reuse.tile([P, H], U8, name="w3_s", offset=W2S_AT, align_bytes=64)
-        weighted = [reuse.tile([P, TILES, QUART], F32, name="weighted2", offset=W4_AT + 2048, align_bytes=64) if qt == 2
-                    else keep.tile([P, TILES, QUART], F32, name="weighted%d" % qt, align_bytes=64) for qt in range(4)]
-        w4_g = reuse.tile([P, TILES * N], BF16, name="w4_g", offset=W4G_AT, align_bytes=64)
+                keep.tile([P, TILES, HALF], F32, name="best1", align_bytes=64)]
+        w3_c = keep.tile([P, PASSES * H], I32, name="w3_c", align_bytes=64)
+        w3_s = keep.tile([P, H], U8, name="w3_s", align_bytes=64)
+        weighted = [reuse.tile([P, TILES, QUART], F32, name="weighted0", offset=WEIGHTED0_AT, align_bytes=64)]
+        weighted += [keep.tile([P, TILES, QUART], F32, name="weighted%d" % qt, align_bytes=64) for qt in range(1, 4)]
+        w4_g = [reuse.tile([P, TILES * 2 * P], BF16, name="w4_g0", offset=EARLY_AT, align_bytes=64),
+                reuse.tile([P, TILES * P], BF16, name="w4_g1", offset=WEIGHTED0_AT + 1024, align_bytes=64)]
         w4_c = keep.tile([P, N], U32, name="w4_c", align_bytes=64)
         w4_s = keep.tile([P, N], U8, name="w4_s", align_bytes=64)
         h_g = keep.tile([P, TILES * S], BF16, name="h_g", align_bytes=64)
@@ -199,24 +216,26 @@ def tile_list_clause_evaluator_kernel(
                 w3_s[:].bitcast(U32).rearrange("p (t b e) -> p t b e", t=TILES, e=2),
                 w3_scale_rows[:].bitcast(U32).rearrange("p (b t e) -> p t b e", t=TILES, e=2))
 
-        def goal_quarter(qt, first_bank):
-            for t in range(TILES):
-                acc = banks[first_bank + t // 2][:, (t % 2) * QUART:(t % 2 + 1) * QUART]
-                for a in range(PASSES):
-                    goal_pass(acc, a, t, qt * QUART, QUART)
-
-        def maximum_quarter(qt, first_bank):
-            hf, ch = qt // 2, (qt % 2) * QUART
+        def goal_quarter(qt, pair_banks):
             for pair in range(2):
-                nc.vector.tensor_tensor(
-                    best[hf][:, 2 * pair:2 * pair + 2, ch:ch + QUART],
-                    banks[first_bank + pair][:].rearrange("p (t c) -> p t c", t=2),
-                    infer[hf][:, 2 * pair:2 * pair + 2, ch:ch + QUART], ALU.max)
+                for a in range(PASSES):
+                    for t in (2 * pair, 2 * pair + 1):
+                        goal_pass(a, t, qt, pair_banks)
 
-        def length(qt, first_bank):
+        def maximum(qt, pair, bank):
+            hf, ch = qt // 2, (qt % 2) * QUART
+            nc.vector.tensor_tensor(
+                best[hf][:, 2 * pair:2 * pair + 2, ch:ch + QUART], banks[bank][:].rearrange("p (t c) -> p t c", t=2),
+                infer_rows(hf, pair)[:, :, ch:ch + QUART], ALU.max)
+
+        def maximum_quarter(qt, pair_banks):
+            for pair in range(2):
+                maximum(qt, pair, pair_banks[pair])
+
+        def length(qt, pair_banks):
             for pair in range(2):
                 tiles = (2 * pair, 2 * pair + 1)
-                accs = {t: banks[first_bank + pair][:, (t % 2) * QUART:(t % 2 + 1) * QUART] for t in tiles}
+                accs = {t: banks[pair_banks[pair]][:, (t % 2) * QUART:(t % 2 + 1) * QUART] for t in tiles}
                 for t in tiles:
                     for a in range(PASSES):
                         c = a * H + t * P
@@ -225,12 +244,16 @@ def tile_list_clause_evaluator_kernel(
                 for t in tiles:
                     nc.scalar.activation(weighted[qt][:, t, :], accs[t], ACT.Copy, scale=lam_t[:, t:t + 1])
 
-        def round_w4(m):
-            nc.scalar.copy(w4_g[:].rearrange("p (c e t) -> p c t e", e=4, t=TILES)[:, 32 * m:32 * (m + 1)],
-                           w4_raw[:].rearrange("p (t c e) -> p c t e", e=4, t=TILES)[:, 32 * m:32 * (m + 1)])
+        w4_cols = ((0, 2 * P), (2 * P, N))
 
-        def quantise_w4():
-            nc.vector.quantize_mx(w4_c[:].bitcast(FP8X4), w4_s[:], w4_g[:])
+        def round_w4(part, copy):
+            c0, c1 = w4_cols[part]
+            copy(w4_g[part][:].rearrange("p (c e t) -> p c t e", e=4, t=TILES),
+                 w4_raw[:].rearrange("p (t c e) -> p c t e", e=4, t=TILES)[:, c0 // 4:c1 // 4])
+
+        def quantise_w4(part):
+            c0, c1 = w4_cols[part]
+            nc.vector.quantize_mx(w4_c[:, c0:c1].bitcast(FP8X4), w4_s[:, c0:c1], w4_g[part][:])
 
         def penalise(c0, n):
             hf, ch, qt, cq = c0 // HALF, c0 % HALF, c0 // QUART, c0 % QUART
@@ -244,72 +267,84 @@ def tile_list_clause_evaluator_kernel(
 
         out_rows = out.rearrange("(m p) j -> p m j", p=P)
 
-        def score_products(c0, n, first_bank):
+        def score_products(c0, n, score_banks):
             per_bank = HALF // n
-            accs = [banks[first_bank + m // per_bank][:, (m % per_bank) * n:(m % per_bank + 1) * n] for m in range(3)]
+            accs = [banks[score_banks[m // per_bank]][:, (m % per_bank) * n:(m % per_bank + 1) * n] for m in range(3)]
             for m in range(3):
                 nc.tensor.matmul_mx(
                     accs[m], lhsT=w4_c[:, m * P:(m + 1) * P].bitcast(FP8X4), lhsT_scale=w4_s[:, m * P:(m + 1) * P],
                     rhs=h_c[:, c0:c0 + n].bitcast(FP8X4), rhs_scale=h_s[:, c0:c0 + n], start=True, stop=True)
             return accs
 
-        def scores(c0, n, first_bank):
+        def scores(c0, n, score_banks):
             res = keep.tile([P, 3, n], F32, name="res%d" % c0, align_bytes=64)
-            accs = score_products(c0, n, first_bank)
+            accs = score_products(c0, n, score_banks)
             for m in range(3):
                 nc.scalar.activation(res[:, m, :], accs[m], ACT.Identity, bias=bo_t[:, m:m + 1])
             nc.sync.dma_start(out_rows[:, :, c0:c0 + n], res[:])
 
         def last_scores(c0, bank):
             res = keep.tile([P, 3, P], F32, name="res%d" % c0, align_bytes=64)
-            score_products(c0, P, bank)
+            score_products(c0, P, (bank,))
             nc.vector.tensor_tensor(
                 res[:], banks[bank][:, 0:3 * P].rearrange("p (m c) -> p m c", m=3),
                 bo_t[:].unsqueeze(2).broadcast_to([P, 3, P]), ALU.add)
             nc.sync.dma_start(out_rows[:, :, c0:c0 + P], res[:])
 
+        def prepare_w1(a):
+            round_w1(a, 0)
+            for t in range(1, TILES):
+                round_w1(a, t)
+                quantise_w1(a, t - 1, 1)
+            quantise_w1(a, TILES - 1, 1)
+
+        first_goal = ((6, 7), (0, 1))
         for t in range(TILES):
             round_w1(0, t)
-        quantise_w1(0, 0, TILES)
-        for t in range(TILES):
-            goal_pass(banks[t][:], 0, t, 0, HALF)
-        for t in range(3):
-            round_w1(1, t)
-        quantise_w1(1, 0, 2)
-        round_w1(1, 3)
-        quantise_w1(1, 2, 2)
+        quantise_w1(0, 0, 2)
+        quantise_w1(0, 2, 2)
+        for qt in range(2):
+            for t in range(TILES):
+                goal_pass(0, t, qt, first_goal[qt])
+        prepare_w1(1)
         order_w3_words(0)
         order_w3_scales()
         order_w3_words(1)
-        for t in range(2, TILES):
-            nc.scalar.copy(infer[1][:, t, :], banks[4 + t][:])
-        for t in range(TILES):
-            goal_pass(banks[t][:], 1, t, 0, HALF)
-        for t in range(TILES):
-            nc.vector.tensor_tensor(best[0][:, t, :], banks[t][:], infer[0][:, t, :], ALU.max)
-        length(0, 4)
-        length(1, 6)
+        for pair in range(2):
+            for qt in range(2):
+                for t in (2 * pair, 2 * pair + 1):
+                    goal_pass(1, t, qt, first_goal[qt])
+        for pair in range(2):
+            for qt in range(2):
+                maximum(qt, pair, first_goal[qt][pair])
+        round_w4(0, nc.vector.tensor_copy)
+        infer_passes(1, (2,), 2)
+        length(0, (3, 4))
+        length(1, (5, 6))
+        infer_passes(1, (3,), 3)
         penalise(0, QUART)
+        quantise_w4(0)
+        round_w4(1, nc.scalar.copy)
+        infer_copy(1, 2, 2)
+        infer_copy(1, 3, 3)
         penalise(QUART, QUART)
-        for m in range(3):
-            round_w4(m)
-        goal_quarter(2, 4)
-        length(2, 0)
-        goal_quarter(3, 6)
+        goal_quarter(2, (4, 5))
+        length(2, (0, 1))
         quantise_h(0, QUART)
-        quantise_w4()
+        quantise_w4(1)
+        scores(0, QUART, (7, 2))
+        goal_quarter(3, (6, 3))
+        maximum_quarter(2, (4, 5))
         quantise_h(QUART, QUART)
-        scores(0, QUART, 2)
-        scores(QUART, QUART, 0)
-        maximum_quarter(2, 4)
-        length(3, 4)
+        scores(QUART, QUART, (0, 1))
+        length(3, (4, 5))
         penalise(2 * QUART, QUART)
-        maximum_quarter(3, 6)
+        maximum_quarter(3, (6, 3))
         quantise_h(2 * QUART, QUART)
-        scores(2 * QUART, QUART, 2)
+        scores(2 * QUART, QUART, (7, 2))
         penalise(3 * QUART, P)
         penalise(3 * QUART + P, P)
         quantise_h(3 * QUART, P)
-        scores(3 * QUART, P, 6)
+        scores(3 * QUART, P, (6,))
         quantise_h(3 * QUART + P, P)
-        last_scores(3 * QUART + P, 7)
+        last_scores(3 * QUART + P, 3)

@@ -28,13 +28,13 @@ LAP = 64
 W1A_AT = 0
 ROWS_AT = W1A_AT + 8192 - LAP
 W1B_AT = ROWS_AT + T - LAP
+W3ROWS_AT = ROWS_AT + 512
 IDLE_AT = ROWS_AT + 1024
-BO_AT = W1A_AT
-W4_AT = BO_AT + 64
 W3_AT = W1B_AT + 8192
-W3ROWS_AT = W3_AT + 4096
-PICKED_AT = W3ROWS_AT - LAP
-EARLY_AT = PICKED_AT + S
+PICKED_AT = W3_AT + 4096 - LAP
+BO_AT = PICKED_AT + LAP
+W4_AT = BO_AT + 64
+EARLY_AT = W4_AT + 6144
 LATE1_AT = EARLY_AT + 8192
 WEIGHTED0_AT = LATE1_AT + 4096 - LAP
 
@@ -119,14 +119,14 @@ def tile_list_clause_evaluator_kernel(
         for i in range(WARM):
             nc.tensor.matmul_mx(banks[6][:], lhsT=idle_c[:].bitcast(FP8X4), lhsT_scale=idle_s[:],
                                 rhs=w2_raw[:, 0, :].bitcast(FP4X4), rhs_scale=idle_plane[:], start=True, stop=True)
-        w3_raw = reuse.tile([P, PASSES, H], I32, name="w3_raw", offset=W3_AT, align_bytes=64)
-        nc.sync.dma_start(
-            w3_raw[:], w3_words.rearrange("a p c i -> a p (c i)").bitcast(I32).rearrange("a p c -> p a c"))
         w3_scale_rows = reuse.tile([P, H], U8, name="w3_scale_rows", offset=W3ROWS_AT, align_bytes=64)
         nc.scalar.copy(w3_scale_rows[:].bitcast(U32), zeros[:])
         for d in range(4):
             nc.sync.dma_start(w3_scale_rows[32 * d + 8:32 * d + 16, :].bitcast(I32),
                               w3_scales.bitcast(I32)[:, 4 * d:4 * d + 4, :])
+        w3_raw = reuse.tile([P, PASSES, H], I32, name="w3_raw", offset=W3_AT, align_bytes=64)
+        nc.sync.dma_start(
+            w3_raw[:], w3_words.rearrange("a p c i -> a p (c i)").bitcast(I32).rearrange("a p c -> p a c"))
         bo_t = reuse.tile([P, 3], F32, name="bo_t", offset=BO_AT)
         w4_raw = reuse.tile([P, TILES * N], F32, name="w4_raw", offset=W4_AT, align_bytes=64)
         with nc.allow_non_contiguous_dma(reason="one value a partition"):
@@ -171,6 +171,7 @@ def tile_list_clause_evaluator_kernel(
         infer_passes(1, (0, 1), 4)
         for t in range(2):
             infer_copy(1, t, 4 + t)
+        infer_passes(1, (2,), 2)
 
         w1_c = keep.tile([P, PASSES * H], U32, name="w1_c", align_bytes=64)
         w1_s = keep.tile([P, PASSES * H], U8, name="w1_s", align_bytes=64)
@@ -318,7 +319,6 @@ def tile_list_clause_evaluator_kernel(
             for qt in range(2):
                 maximum(qt, pair, first_goal[qt][pair])
         round_w4(0, nc.vector.tensor_copy)
-        infer_passes(1, (2,), 2)
         length(0, (3, 4))
         length(1, (5, 6))
         infer_passes(1, (3,), 3)

@@ -28,8 +28,9 @@ LAP = 64
 W1A_AT = 0
 ROWS_AT = W1A_AT + 8192 - LAP
 W1B_AT = ROWS_AT + T - LAP
-W3ROWS_AT = ROWS_AT + 512
-IDLE_AT = ROWS_AT + 1024
+W3ROWS_AT = ROWS_AT + LAP
+IDLE_AT = W3ROWS_AT + 512
+LAMROWS_AT = IDLE_AT + 512
 W3_AT = W1B_AT + 8192
 PICKED_AT = W3_AT + 4096 - LAP
 BO_AT = PICKED_AT + LAP
@@ -58,8 +59,6 @@ def tile_list_clause_evaluator_kernel(
         w2_s = keep.tile([P, PASSES * H], U8, name="w2_s", align_bytes=64)
         w2_scale_rows = keep.tile([P, PASSES * H], U8, name="w2_scale_rows", align_bytes=64)
         nc.vector.memset(w2_scale_rows[:].bitcast(I32), 0)
-        lam_rows = keep.tile([P, P], F32, name="lam_rows", align_bytes=64)
-        nc.vector.memset(lam_rows[:], 0.0)
         identity = keep.tile([P, P], F32, name="identity", align_bytes=64)
         nc.vector.memset(identity[:], 0.0)
         make_identity(nc, identity[:], nomemset=True)
@@ -82,16 +81,11 @@ def tile_list_clause_evaluator_kernel(
             nc.sync.dma_start(tab[a][:], tab_words[a].rearrange("p t i -> p (t i)").bitcast(I32))
 
         load_table(0)
-        for d in (0, 2, 1, 3):
+        for s in range(4):
             nc.sync.dma_start(
-                w2_scale_rows[32 * d:32 * d + 4, :].bitcast(I32).rearrange("p (a c) -> p a c", a=PASSES),
-                w2_scales.bitcast(I32)[:, 4 * d:4 * d + 4, :].rearrange("a s c -> s a c"))
-        nc.sync.dma_start(lam_rows[0:TILES, :].rearrange("t (b j) -> t b j", j=8),
-                          lam.rearrange("(b t j) -> t b j", t=TILES, j=8))
+                w2_scale_rows[s:P:32, :].bitcast(I32).rearrange("p (a c) -> p a c", a=PASSES),
+                w2_scales.bitcast(I32)[:, s:16:4, :].rearrange("a d c -> d a c"))
         load_table(1)
-        nc.tensor.transpose(banks[7][:, 0:P], lam_rows[:], identity[:])
-        lam_t = keep.tile([P, TILES], F32, name="lam_t")
-        nc.scalar.copy(lam_t[:], banks[7][:, 0:TILES])
 
         w2_c = keep.tile([P, PASSES * H // 2], I32, name="w2_c", align_bytes=64)
         nc.scalar.copy(
@@ -119,6 +113,10 @@ def tile_list_clause_evaluator_kernel(
         for i in range(WARM):
             nc.tensor.matmul_mx(banks[6][:], lhsT=idle_c[:].bitcast(FP8X4), lhsT_scale=idle_s[:],
                                 rhs=w2_raw[:, 0, :].bitcast(FP4X4), rhs_scale=idle_plane[:], start=True, stop=True)
+        lam_rows = reuse.tile([P, P], F32, name="lam_rows", offset=LAMROWS_AT, align_bytes=64)
+        nc.scalar.copy(lam_rows[:], zeros[:].bitcast(F32))
+        nc.sync.dma_start(lam_rows[0:TILES, :].rearrange("t (b j) -> t b j", j=8),
+                          lam.rearrange("(b t j) -> t b j", t=TILES, j=8))
         w3_scale_rows = reuse.tile([P, H], U8, name="w3_scale_rows", offset=W3ROWS_AT, align_bytes=64)
         nc.scalar.copy(w3_scale_rows[:].bitcast(U32), zeros[:])
         for d in range(4):
@@ -177,8 +175,8 @@ def tile_list_clause_evaluator_kernel(
         w1_s = keep.tile([P, PASSES * H], U8, name="w1_s", align_bytes=64)
         w1_g = [keep.tile([P, 4 * H], BF16, name="w1_g%d" % a, align_bytes=64) for a in range(PASSES)]
 
-        def round_w1(a, t):
-            nc.vector.tensor_copy(
+        def round_w1(a, t, copy=nc.vector.tensor_copy):
+            copy(
                 w1_g[a][:, t * H:(t + 1) * H].rearrange("p (b u e i) -> p b u i e", u=2, e=4, i=4),
                 w1_raw[a][:].rearrange("p (i b t u e) -> p t b u i e", i=4, t=TILES, u=2, e=4)[:, t])
 
@@ -292,13 +290,6 @@ def tile_list_clause_evaluator_kernel(
                 bo_t[:].unsqueeze(2).broadcast_to([P, 3, P]), ALU.add)
             nc.sync.dma_start(out_rows[:, :, c0:c0 + P], res[:])
 
-        def prepare_w1(a):
-            round_w1(a, 0)
-            for t in range(1, TILES):
-                round_w1(a, t)
-                quantise_w1(a, t - 1, 1)
-            quantise_w1(a, TILES - 1, 1)
-
         first_goal = ((6, 7), (0, 1))
         for t in range(TILES):
             round_w1(0, t)
@@ -307,17 +298,29 @@ def tile_list_clause_evaluator_kernel(
         for qt in range(2):
             for t in range(TILES):
                 goal_pass(0, t, qt, first_goal[qt])
-        prepare_w1(1)
+        nc.tensor.transpose(banks[3][:, 0:P], lam_rows[:], identity[:])
+        lam_t = keep.tile([P, TILES], F32, name="lam_t")
+        nc.scalar.copy(lam_t[:], banks[3][:, 0:TILES])
+        round_w1(1, 3, nc.scalar.copy)
+        round_w1(1, 0)
+        for t in range(1, 3):
+            round_w1(1, t)
+            quantise_w1(1, t - 1, 1)
+        quantise_w1(1, 2, 1)
         order_w3_words(0)
         order_w3_scales()
         order_w3_words(1)
-        for pair in range(2):
-            for qt in range(2):
-                for t in (2 * pair, 2 * pair + 1):
-                    goal_pass(1, t, qt, first_goal[qt])
-        for pair in range(2):
-            for qt in range(2):
-                maximum(qt, pair, first_goal[qt][pair])
+        for qt in range(2):
+            for t in (0, 1):
+                goal_pass(1, t, qt, first_goal[qt])
+        maximum(0, 0, first_goal[0][0])
+        quantise_w1(1, 3, 1)
+        for qt in range(2):
+            for t in (2, 3):
+                goal_pass(1, t, qt, first_goal[qt])
+        maximum(1, 0, first_goal[1][0])
+        for qt in range(2):
+            maximum(qt, 1, first_goal[qt][1])
         round_w4(0, nc.vector.tensor_copy)
         length(0, (3, 4))
         length(1, (5, 6))

@@ -22,7 +22,7 @@ PASSES = 2
 TILES = 4
 HALF = 512
 QUART = 256
-WARM = 3
+WARM = (2, 3)
 
 LAP = 64
 W1A_AT = 0
@@ -107,12 +107,14 @@ def tile_list_clause_evaluator_kernel(
         for a in range(PASSES):
             nc.sync.dma_start(w1_raw[a][:], w1[512 * a:512 * (a + 1), :].rearrange("(p i) c -> p (i c)", i=4))
 
-        idle_plane = reuse.tile([P, HALF], U8, name="idle_plane", offset=IDLE_AT, align_bytes=64)
-        nc.scalar.copy(idle_plane[:].bitcast(U32).rearrange("p (r c) -> p r c", r=4),
-                       idle_s[:].bitcast(U32).unsqueeze(1).broadcast_to([P, 4, P // 4]))
-        for i in range(WARM):
-            nc.tensor.matmul_mx(banks[6][:], lhsT=idle_c[:].bitcast(FP8X4), lhsT_scale=idle_s[:],
-                                rhs=w2_raw[:, 0, :].bitcast(FP4X4), rhs_scale=idle_plane[:], start=True, stop=True)
+        idle_planes = [keep.tile([P, HALF], U8, name="idle_plane0", align_bytes=64),
+                       reuse.tile([P, HALF], U8, name="idle_plane1", offset=IDLE_AT, align_bytes=64)]
+        for plane, count in zip(idle_planes, WARM):
+            nc.scalar.copy(plane[:].bitcast(U32).rearrange("p (r c) -> p r c", r=4),
+                           idle_s[:].bitcast(U32).unsqueeze(1).broadcast_to([P, 4, P // 4]))
+            for i in range(count):
+                nc.tensor.matmul_mx(banks[6][:], lhsT=idle_c[:].bitcast(FP8X4), lhsT_scale=idle_s[:],
+                                    rhs=w2_c[:, 0:HALF // 2].bitcast(FP4X4), rhs_scale=plane[:], start=True, stop=True)
         lam_rows = reuse.tile([P, P], F32, name="lam_rows", offset=LAMROWS_AT, align_bytes=64)
         nc.scalar.copy(lam_rows[:], zeros[:].bitcast(F32))
         nc.sync.dma_start(lam_rows[0:TILES, :].rearrange("t (b j) -> t b j", j=8),

@@ -27,17 +27,19 @@ WARM = (2, 3)
 LAP = 64
 W1A_AT = 0
 ROWS_AT = W1A_AT + 8192 - LAP
-W1B_AT = ROWS_AT + T - LAP
-W3ROWS_AT = ROWS_AT + LAP
-IDLE_AT = W3ROWS_AT + 512
-LAMROWS_AT = IDLE_AT + 512
-W3_AT = W1B_AT + 8192
+IDLE_AT = ROWS_AT + LAP
+W1B_AT = ROWS_AT + T
+PICKED0_AT = W1B_AT + 8192 - LAP
+W3ROWS_AT = PICKED0_AT + LAP
+LAMROWS_AT = W3ROWS_AT + 512
+W3_AT = LAMROWS_AT + 512 + LAP
 PICKED_AT = W3_AT + 4096 - LAP
 BO_AT = PICKED_AT + LAP
 W4_AT = BO_AT + 64
 EARLY_AT = W4_AT + 6144
 LATE1_AT = EARLY_AT + 8192
 WEIGHTED0_AT = LATE1_AT + 4096 - LAP
+W2A_AT = WEIGHTED0_AT + 4096
 
 
 def tile_list_clause_evaluator_kernel(
@@ -55,14 +57,15 @@ def tile_list_clause_evaluator_kernel(
 
         tab_scale_rows = reuse.tile([P, T], U8, name="tab_scale_rows", offset=ROWS_AT, align_bytes=64)
         nc.vector.memset(tab_scale_rows[:].bitcast(I32), 0)
-        v_s = keep.tile([P, PASSES * S], U8, name="v_s", align_bytes=64)
+        v_s = [keep.tile([P, PASSES * HALF], U8, name="v_s%d" % hf, align_bytes=64) for hf in range(2)]
         w2_s = keep.tile([P, PASSES * H], U8, name="w2_s", align_bytes=64)
         w2_scale_rows = keep.tile([P, PASSES * H], U8, name="w2_scale_rows", align_bytes=64)
         nc.vector.memset(w2_scale_rows[:].bitcast(I32), 0)
         identity = keep.tile([P, P], F32, name="identity", align_bytes=64)
         nc.vector.memset(identity[:], 0.0)
         make_identity(nc, identity[:], nomemset=True)
-        nc.vector.memset(v_s[:].bitcast(I32), 0)
+        for hf in range(2):
+            nc.vector.memset(v_s[hf][:].bitcast(I32), 0)
         zeros = keep.tile([P, P], U32, name="zeros", align_bytes=64)
         nc.vector.memset(zeros[:], 0)
         idle_g = keep.tile([P, 4 * P], BF16, name="idle_g", align_bytes=64)
@@ -87,25 +90,33 @@ def tile_list_clause_evaluator_kernel(
                 w2_scales.bitcast(I32)[:, s:16:4, :].rearrange("a d c -> d a c"))
         load_table(1)
 
-        w2_c = keep.tile([P, PASSES * H // 2], I32, name="w2_c", align_bytes=64)
-        nc.scalar.copy(
-            w2_c[:].bitcast(U32).rearrange("p (a t b e) -> p a t b e", a=PASSES, t=TILES, e=4),
-            w2_raw[:].bitcast(U32).rearrange("p a (b t e) -> p a t b e", t=TILES, e=4))
+        w2_first = reuse.tile([P, P], I32, name="w2_first", offset=W2A_AT, align_bytes=64)
+        w2_rest = keep.tile([P, 3 * P], I32, name="w2_rest", align_bytes=64)
+        for ordered, t0, t1 in ((w2_first, 0, 1), (w2_rest, 1, TILES)):
+            nc.scalar.copy(
+                ordered[:].bitcast(U32).rearrange("p (t a b e) -> p t a b e", a=PASSES, t=t1 - t0, e=4),
+                w2_raw[:].bitcast(U32).rearrange("p a (b t e) -> p t a b e", t=TILES, e=4)[:, t0:t1])
+
+        def w2_words_of(a, t):
+            w = (2 * max(t - 1, 0) + a) * P // 2
+            return (w2_rest if t else w2_first)[:, w:w + P // 2].bitcast(FP4X4)
         nc.scalar.copy(
             w2_s[:].bitcast(U32).rearrange("p (a t b e) -> p a t b e", a=PASSES, t=TILES, e=2),
             w2_scale_rows[:].bitcast(U32).rearrange("p (a b t e) -> p a t b e", a=PASSES, t=TILES, e=2))
 
-        picked = reuse.tile([P, S], U8, name="picked", offset=PICKED_AT, align_bytes=64)
-        nc.vector.tensor_copy(picked[:], tab_scale_rows[:].indirect(offsets[:]))
-        for d in (0, 2, 1, 3):
-            nc.sync.dma_start(
-                v_s[32 * d:32 * d + 4, :].bitcast(I32).rearrange("p (a c) -> p a c", a=PASSES),
-                picked[32 * d:32 * d + 32:4, :].bitcast(I32))
+        picked = [reuse.tile([P, W3_AT - PICKED0_AT], U8, name="picked0", offset=PICKED0_AT, align_bytes=64),
+                  reuse.tile([P, HALF], U8, name="picked1", offset=PICKED_AT, align_bytes=64)]
+        for hf in range(2):
+            nc.vector.tensor_copy(picked[hf][:, 0:HALF], tab_scale_rows[:].indirect(offsets[:, 32 * hf:32 * (hf + 1)]))
 
         w1_raw = [reuse.tile([P, 4 * H], F32, name="w1_raw%d" % a, offset=at, align_bytes=64)
                   for a, at in enumerate((W1A_AT, W1B_AT))]
-        for a in range(PASSES):
-            nc.sync.dma_start(w1_raw[a][:], w1[512 * a:512 * (a + 1), :].rearrange("(p i) c -> p (i c)", i=4))
+        for i in range(2):
+            for d in (0, 2, 1, 3):
+                nc.sync.dma_start(
+                    v_s[i][32 * d:32 * d + 4, :].bitcast(I32).rearrange("p (a c) -> p a c", a=PASSES),
+                    picked[i][32 * d:32 * d + 32:4, 0:HALF].bitcast(I32))
+            nc.sync.dma_start(w1_raw[i][:], w1[512 * i:512 * (i + 1), :].rearrange("(p i) c -> p (i c)", i=4))
 
         idle_planes = [keep.tile([P, HALF], U8, name="idle_plane0", align_bytes=64),
                        reuse.tile([P, HALF], U8, name="idle_plane1", offset=IDLE_AT, align_bytes=64)]
@@ -114,7 +125,7 @@ def tile_list_clause_evaluator_kernel(
                            idle_s[:].bitcast(U32).unsqueeze(1).broadcast_to([P, 4, P // 4]))
             for i in range(count):
                 nc.tensor.matmul_mx(banks[6][:], lhsT=idle_c[:].bitcast(FP8X4), lhsT_scale=idle_s[:],
-                                    rhs=w2_c[:, 0:HALF // 2].bitcast(FP4X4), rhs_scale=plane[:], start=True, stop=True)
+                                    rhs=w2_rest[:, 0:HALF // 2].bitcast(FP4X4), rhs_scale=plane[:], start=True, stop=True)
         lam_rows = reuse.tile([P, P], F32, name="lam_rows", offset=LAMROWS_AT, align_bytes=64)
         nc.scalar.copy(lam_rows[:], zeros[:].bitcast(F32))
         nc.sync.dma_start(lam_rows[0:TILES, :].rearrange("t (b j) -> t b j", j=8),
@@ -145,7 +156,7 @@ def tile_list_clause_evaluator_kernel(
             hf, ch = c0 // HALF, c0 % HALF
             nc.tensor.matmul_mx(
                 acc, lhsT=codes, lhsT_scale=scales, rhs=v_c[a, hf][:, ch:ch + n].bitcast(FP8X4),
-                rhs_scale=v_s[:, a * S + c0:a * S + c0 + n],
+                rhs_scale=v_s[hf][:, a * HALF + ch:a * HALF + ch + n],
                 start=(a == 0 and opens), stop=(a == PASSES - 1 and closes))
 
         early = reuse.tile([P, TILES, HALF], F32, name="early", offset=EARLY_AT, align_bytes=64)
@@ -159,8 +170,7 @@ def tile_list_clause_evaluator_kernel(
             for a in range(PASSES):
                 for i, t in enumerate(tiles):
                     c = a * H + t * P
-                    one_pass(banks[first_bank + i][:], w2_c[:, c // 2:(c + P) // 2].bitcast(FP4X4), w2_s[:, c:c + P],
-                             a, hf * HALF, HALF)
+                    one_pass(banks[first_bank + i][:], w2_words_of(a, t), w2_s[:, c:c + P], a, hf * HALF, HALF)
 
         def infer_copy(hf, t, bank):
             nc.scalar.copy(infer_rows(hf, t // 2)[:, t % 2, :], banks[bank][:])
@@ -168,13 +178,15 @@ def tile_list_clause_evaluator_kernel(
         infer_passes(0, range(TILES), 0)
         for t in range(TILES):
             infer_copy(0, t, t)
-        infer_passes(1, (0, 1), 4)
+        for t in range(2):
+            infer_passes(1, (t,), 4 + t)
         for t in range(2):
             infer_copy(1, t, 4 + t)
         infer_passes(1, (2,), 2)
 
         w1_c = keep.tile([P, PASSES * H], U32, name="w1_c", align_bytes=64)
-        w1_s = keep.tile([P, PASSES * H], U8, name="w1_s", align_bytes=64)
+        w1_s = [reuse.tile([P, H], U8, name="w1_s0", offset=W2A_AT, align_bytes=64),
+                keep.tile([P, H], U8, name="w1_s1", align_bytes=64)]
         w1_g = [keep.tile([P, 4 * H], BF16, name="w1_g%d" % a, align_bytes=64) for a in range(PASSES)]
 
         def round_w1(a, t, copy=nc.vector.tensor_copy):
@@ -184,13 +196,13 @@ def tile_list_clause_evaluator_kernel(
 
         def quantise_w1(a, t0, count):
             c, n = a * H + t0 * P, count * P
-            nc.vector.quantize_mx(w1_c[:, c:c + n].bitcast(FP8X4), w1_s[:, c:c + n],
+            nc.vector.quantize_mx(w1_c[:, c:c + n].bitcast(FP8X4), w1_s[a][:, t0 * P:t0 * P + n],
                                   w1_g[a][:, t0 * H:(t0 + count) * H])
 
         def goal_pass(a, t, qt, pair_banks):
             c = a * H + t * P
             one_pass(banks[pair_banks[t // 2]][:, (t % 2) * QUART:(t % 2 + 1) * QUART],
-                     w1_c[:, c:c + P].bitcast(FP8X4), w1_s[:, c:c + P], a, qt * QUART, QUART,
+                     w1_c[:, c:c + P].bitcast(FP8X4), w1_s[a][:, t * P:(t + 1) * P], a, qt * QUART, QUART,
                      opens=(t % 2 == 0), closes=(t % 2 == 1))
 
         best = [keep.tile([P, TILES, HALF], F32, name="best0", align_bytes=64),

@@ -149,8 +149,11 @@ def tile_list_clause_evaluator_kernel(
         for a in range(PASSES):
             for hf in range(2):
                 v_c[a, hf] = keep.tile([P, HALF], U32, name="v%d_%d" % (a, hf), align_bytes=64)
-                nc.vector.tensor_copy(
-                    v_c[a, hf][:], tab[a][:].bitcast(U32).indirect(offsets[:, 32 * hf:32 * (hf + 1)]))
+                step = QUART if (a, hf) == (1, 0) else HALF
+                for c in range(0, HALF, step):
+                    j = (hf * HALF + c) // 16
+                    nc.vector.tensor_copy(
+                        v_c[a, hf][:, c:c + step], tab[a][:].bitcast(U32).indirect(offsets[:, j:j + step // 16]))
 
         def one_pass(acc, codes, scales, a, c0, n, opens=True, closes=True):
             hf, ch = c0 // HALF, c0 % HALF
@@ -175,11 +178,17 @@ def tile_list_clause_evaluator_kernel(
         def infer_copy(hf, t, bank):
             nc.scalar.copy(infer_rows(hf, t // 2)[:, t % 2, :], banks[bank][:])
 
-        infer_passes(0, range(TILES), 0)
-        for t in range(TILES):
-            infer_copy(0, t, t)
-        for t in range(2):
-            infer_passes(1, (t,), 4 + t)
+        for a in range(PASSES):
+            for qt in range(2):
+                for t in range(TILES):
+                    c = a * H + t * P
+                    one_pass(banks[2 * qt + t // 2][:, (t % 2) * QUART:(t % 2 + 1) * QUART], w2_words_of(a, t),
+                             w2_s[:, c:c + P], a, qt * QUART, QUART, opens=(t % 2 == 0), closes=(t % 2 == 1))
+        for qt in range(2):
+            for pair in range(2):
+                nc.scalar.copy(early[:, 2 * pair:2 * pair + 2, qt * QUART:(qt + 1) * QUART],
+                               banks[2 * qt + pair][:].rearrange("p (t c) -> p t c", t=2))
+        infer_passes(1, (0, 1), 4)
         for t in range(2):
             infer_copy(1, t, 4 + t)
         infer_passes(1, (2,), 2)
@@ -256,6 +265,31 @@ def tile_list_clause_evaluator_kernel(
                                  a, qt * QUART, QUART)
                 for t in tiles:
                     nc.scalar.activation(weighted[qt][:, t, :], accs[t], ACT.Copy, scale=lam_t[:, t:t + 1])
+
+        def eighth_passes(codes, scales, c0, bank):
+            for a in range(PASSES):
+                for t in range(TILES):
+                    c = a * H + t * P
+                    one_pass(banks[bank][:, t * P:(t + 1) * P], codes[:, c:c + P].bitcast(FP8X4), scales(a, t),
+                             a, c0, P, opens=(t == 0), closes=(t == TILES - 1))
+
+        def goal_eighth(c0, bank):
+            eighth_passes(w1_c, lambda a, t: w1_s[a][:, t * P:(t + 1) * P], c0, bank)
+
+        def length_eighth(c0, bank):
+            eighth_passes(w3_c, lambda a, t: w3_s[8 + 4 * a:P, t * P:(t + 1) * P], c0, bank)
+            cq = c0 % QUART
+            for t in range(TILES):
+                nc.scalar.activation(weighted[3][:, t, cq:cq + P], banks[bank][:, t * P:(t + 1) * P], ACT.Copy,
+                                     scale=lam_t[:, t:t + 1])
+
+        def maximum_eighth(c0, bank):
+            ch = c0 % HALF
+            for pair in range(2):
+                nc.vector.tensor_tensor(
+                    best[1][:, 2 * pair:2 * pair + 2, ch:ch + P],
+                    banks[bank][:, pair * QUART:(pair + 1) * QUART].rearrange("p (t c) -> p t c", t=2),
+                    late[pair][:, :, ch:ch + P], ALU.max)
 
         w4_cols = ((0, 2 * P), (2 * P, N))
 
@@ -350,18 +384,21 @@ def tile_list_clause_evaluator_kernel(
         quantise_h(0, QUART)
         quantise_w4(1)
         scores(0, QUART, (7, 2))
-        goal_quarter(3, (6, 3))
+        goal_eighth(3 * QUART, 6)
+        goal_eighth(3 * QUART + P, 3)
         maximum_quarter(2, (4, 5))
         quantise_h(QUART, QUART)
         scores(QUART, QUART, (0, 1))
-        length(3, (4, 5))
+        length_eighth(3 * QUART, 4)
+        length_eighth(3 * QUART + P, 5)
         penalise(2 * QUART, QUART)
-        maximum_quarter(3, (6, 3))
+        maximum_eighth(3 * QUART, 6)
         quantise_h(2 * QUART, QUART)
         scores(2 * QUART, QUART, (7, 2))
         penalise(3 * QUART, P)
-        penalise(3 * QUART + P, P)
+        maximum_eighth(3 * QUART + P, 3)
         quantise_h(3 * QUART, P)
         scores(3 * QUART, P, (6,))
+        penalise(3 * QUART + P, P)
         quantise_h(3 * QUART + P, P)
         last_scores(3 * QUART + P, 3)

@@ -37,8 +37,7 @@ PICKED_AT = W3_AT + 4096 - LAP
 BO_AT = PICKED_AT + LAP
 W4_AT = BO_AT + 64
 EARLY_AT = W4_AT + 6144
-LATE1_AT = EARLY_AT + 8192
-WEIGHTED0_AT = LATE1_AT + 4096 - LAP
+WEIGHTED0_AT = EARLY_AT + 8192
 W2A_AT = WEIGHTED0_AT + 4096
 
 
@@ -163,11 +162,10 @@ def tile_list_clause_evaluator_kernel(
                 start=(a == 0 and opens), stop=(a == PASSES - 1 and closes))
 
         early = reuse.tile([P, TILES, HALF], F32, name="early", offset=EARLY_AT, align_bytes=64)
-        late = [keep.tile([P, 2, HALF], F32, name="late0", align_bytes=64),
-                reuse.tile([P, 2, HALF], F32, name="late1", offset=LATE1_AT, align_bytes=64)]
+        late = keep.tile([P, TILES, HALF], F32, name="late", align_bytes=64)
 
         def infer_rows(hf, pair):
-            return early[:, 2 * pair:2 * pair + 2, :] if hf == 0 else late[pair][:]
+            return (early, late)[hf][:, 2 * pair:2 * pair + 2, :]
 
         def infer_passes(hf, tiles, first_bank):
             for a in range(PASSES):
@@ -191,7 +189,6 @@ def tile_list_clause_evaluator_kernel(
         infer_passes(1, (0, 1), 4)
         for t in range(2):
             infer_copy(1, t, 4 + t)
-        infer_passes(1, (2,), 2)
 
         w1_c = keep.tile([P, PASSES * H], U32, name="w1_c", align_bytes=64)
         w1_s = [reuse.tile([P, H], U8, name="w1_s0", offset=W2A_AT, align_bytes=64),
@@ -285,11 +282,9 @@ def tile_list_clause_evaluator_kernel(
 
         def maximum_eighth(c0, bank):
             ch = c0 % HALF
-            for pair in range(2):
-                nc.vector.tensor_tensor(
-                    best[1][:, 2 * pair:2 * pair + 2, ch:ch + P],
-                    banks[bank][:, pair * QUART:(pair + 1) * QUART].rearrange("p (t c) -> p t c", t=2),
-                    late[pair][:, :, ch:ch + P], ALU.max)
+            nc.vector.tensor_tensor(
+                best[1][:, :, ch:ch + P], banks[bank][:].rearrange("p (t c) -> p t c", t=TILES),
+                late[:, :, ch:ch + P], ALU.max)
 
         w4_cols = ((0, 2 * P), (2 * P, N))
 
@@ -328,7 +323,10 @@ def tile_list_clause_evaluator_kernel(
             accs = score_products(c0, n, score_banks)
             for m in range(3):
                 nc.scalar.activation(res[:, m, :], accs[m], ACT.Identity, bias=bo_t[:, m:m + 1])
-            nc.sync.dma_start(out_rows[:, :, c0:c0 + n], res[:])
+                if c0 >= HALF:
+                    nc.sync.dma_start(out_rows[:, m, c0:c0 + n], res[:, m, :])
+            if c0 < HALF:
+                nc.sync.dma_start(out_rows[:, :, c0:c0 + n], res[:])
 
         def last_scores(c0, bank):
             res = keep.tile([P, 3, P], F32, name="res%d" % c0, align_bytes=64)
@@ -372,33 +370,33 @@ def tile_list_clause_evaluator_kernel(
         round_w4(0, nc.vector.tensor_copy)
         length(0, (3, 4))
         length(1, (5, 6))
-        infer_passes(1, (3,), 3)
+        infer_passes(1, (2, 3), 3)
         penalise(0, QUART)
         quantise_w4(0)
         round_w4(1, nc.scalar.copy)
-        infer_copy(1, 2, 2)
-        infer_copy(1, 3, 3)
+        infer_copy(1, 2, 3)
+        infer_copy(1, 3, 4)
         penalise(QUART, QUART)
-        goal_quarter(2, (4, 5))
+        goal_quarter(2, (5, 6))
         length(2, (0, 1))
         quantise_h(0, QUART)
         quantise_w4(1)
         scores(0, QUART, (7, 2))
-        goal_eighth(3 * QUART, 6)
-        goal_eighth(3 * QUART + P, 3)
-        maximum_quarter(2, (4, 5))
+        goal_eighth(3 * QUART, 3)
+        goal_eighth(3 * QUART + P, 4)
+        maximum_quarter(2, (5, 6))
         quantise_h(QUART, QUART)
         scores(QUART, QUART, (0, 1))
-        length_eighth(3 * QUART, 4)
-        length_eighth(3 * QUART + P, 5)
+        length_eighth(3 * QUART, 5)
+        length_eighth(3 * QUART + P, 6)
         penalise(2 * QUART, QUART)
-        maximum_eighth(3 * QUART, 6)
+        maximum_eighth(3 * QUART, 3)
         quantise_h(2 * QUART, QUART)
         scores(2 * QUART, QUART, (7, 2))
         penalise(3 * QUART, P)
-        maximum_eighth(3 * QUART + P, 3)
+        maximum_eighth(3 * QUART + P, 4)
         quantise_h(3 * QUART, P)
-        scores(3 * QUART, P, (6,))
+        scores(3 * QUART, P, (3,))
         penalise(3 * QUART + P, P)
         quantise_h(3 * QUART + P, P)
-        last_scores(3 * QUART + P, 3)
+        last_scores(3 * QUART + P, 4)

@@ -309,13 +309,16 @@ def tile_list_clause_evaluator_kernel(
 
         out_rows = out.rearrange("(m p) j -> p m j", p=P)
 
+        def score_product(acc, m, c0, n):
+            nc.tensor.matmul_mx(
+                acc, lhsT=w4_c[:, m * P:(m + 1) * P].bitcast(FP8X4), lhsT_scale=w4_s[:, m * P:(m + 1) * P],
+                rhs=h_c[:, c0:c0 + n].bitcast(FP8X4), rhs_scale=h_s[:, c0:c0 + n], start=True, stop=True)
+
         def score_products(c0, n, score_banks):
             per_bank = HALF // n
             accs = [banks[score_banks[m // per_bank]][:, (m % per_bank) * n:(m % per_bank + 1) * n] for m in range(3)]
             for m in range(3):
-                nc.tensor.matmul_mx(
-                    accs[m], lhsT=w4_c[:, m * P:(m + 1) * P].bitcast(FP8X4), lhsT_scale=w4_s[:, m * P:(m + 1) * P],
-                    rhs=h_c[:, c0:c0 + n].bitcast(FP8X4), rhs_scale=h_s[:, c0:c0 + n], start=True, stop=True)
+                score_product(accs[m], m, c0, n)
             return accs
 
         def scores(c0, n, score_banks):
@@ -328,13 +331,18 @@ def tile_list_clause_evaluator_kernel(
             if c0 < HALF:
                 nc.sync.dma_start(out_rows[:, :, c0:c0 + n], res[:])
 
-        def last_scores(c0, bank):
-            res = keep.tile([P, 3, P], F32, name="res%d" % c0, align_bytes=64)
-            score_products(c0, P, (bank,))
+        def last_scores(c0, pair_bank, single_bank):
+            pair = keep.tile([P, 2, P], F32, name="last_pair", align_bytes=64)
+            single = keep.tile([P, P], F32, name="last_single", align_bytes=64)
+            for m in range(2):
+                score_product(banks[pair_bank][:, m * P:(m + 1) * P], m, c0, P)
+            score_product(banks[single_bank][:, 0:P], 2, c0, P)
             nc.vector.tensor_tensor(
-                res[:], banks[bank][:, 0:3 * P].rearrange("p (m c) -> p m c", m=3),
-                bo_t[:].unsqueeze(2).broadcast_to([P, 3, P]), ALU.add)
-            nc.sync.dma_start(out_rows[:, :, c0:c0 + P], res[:])
+                pair[:], banks[pair_bank][:, 0:2 * P].rearrange("p (m c) -> p m c", m=2),
+                bo_t[:, 0:2].unsqueeze(2).broadcast_to([P, 2, P]), ALU.add)
+            nc.scalar.activation(single[:], banks[single_bank][:, 0:P], ACT.Identity, bias=bo_t[:, 2:3])
+            nc.sync.dma_start(out_rows[:, 2, c0:c0 + P], single[:])
+            nc.sync.dma_start(out_rows[:, 0:2, c0:c0 + P], pair[:])
 
         first_goal = ((6, 7), (0, 1))
         for t in range(TILES):
@@ -383,20 +391,20 @@ def tile_list_clause_evaluator_kernel(
         quantise_w4(1)
         scores(0, QUART, (7, 2))
         goal_eighth(3 * QUART, 3)
-        goal_eighth(3 * QUART + P, 4)
         maximum_quarter(2, (5, 6))
         quantise_h(QUART, QUART)
-        scores(QUART, QUART, (0, 1))
         length_eighth(3 * QUART, 5)
+        scores(QUART, QUART, (0, 1))
         length_eighth(3 * QUART + P, 6)
+        goal_eighth(3 * QUART + P, 5)
         penalise(2 * QUART, QUART)
         maximum_eighth(3 * QUART, 3)
         quantise_h(2 * QUART, QUART)
         scores(2 * QUART, QUART, (7, 2))
         penalise(3 * QUART, P)
-        maximum_eighth(3 * QUART + P, 4)
+        maximum_eighth(3 * QUART + P, 5)
         quantise_h(3 * QUART, P)
         scores(3 * QUART, P, (3,))
         penalise(3 * QUART + P, P)
         quantise_h(3 * QUART + P, P)
-        last_scores(3 * QUART + P, 4)
+        last_scores(3 * QUART + P, 4, 0)

from contextlib import ExitStack

import concourse.mybir as mybir
from concourse.masks import make_identity

K, T, S, H, N = 1024, 2048, 1024, 512, 384
FLOPS = 2 * K * H * S * 3 + 2 * H * N * S

F32 = mybir.dt.float32
BF16 = mybir.dt.bfloat16
I32 = mybir.dt.int32
U32 = mybir.dt.uint32
U16 = mybir.dt.uint16
U8 = mybir.dt.uint8
FP8X4 = mybir.dt.float8_e4m3fn_x4
FP4X4 = mybir.dt.float4_e2m1fn_x4
ALU = mybir.AluOpType
ACT = mybir.ActivationFunctionType

P = 128
PASSES = 2
TILES = 4
HALF = 512
QUART = 256
WARM = (2, 3)

LAP = 64
W1A_AT = 0
ROWS_AT = W1A_AT + 8192 - LAP
IDLE_AT = ROWS_AT + LAP
W1B_AT = ROWS_AT + T
PICKED0_AT = W1B_AT + 8192 - LAP
W3ROWS_AT = PICKED0_AT + LAP
LAMROWS_AT = W3ROWS_AT + 512
W3_AT = LAMROWS_AT + 512 + LAP
PICKED_AT = W3_AT + 4096 - LAP
BO_AT = PICKED_AT + LAP
W4_AT = BO_AT + 64
EARLY_AT = W4_AT + 6144
WEIGHTED0_AT = EARLY_AT + 8192
W2A_AT = WEIGHTED0_AT + 4096


def tile_list_clause_evaluator_kernel(
    tc, tab_words, tab_scales, offs, w1, w2_words, w2_scales, w3_words, w3_scales, lam, w4, bo, out
):
    nc = tc.nc
    with ExitStack() as ctx:
        keep = ctx.enter_context(tc.tile_pool(name="keep", bufs=1))
        reuse = ctx.enter_context(tc.tile_pool(name="reuse", bufs=1))
        psum = ctx.enter_context(tc.psum_pool(name="psum", bufs=1))
        banks = [psum.tile([P, HALF], F32, name="bank%d" % i) for i in range(8)]

        offsets = keep.tile([P, S // 16], U16, name="offsets")
        nc.sync.dma_start(offsets[:], offs)

        tab_scale_rows = reuse.tile([P, T], U8, name="tab_scale_rows", offset=ROWS_AT, align_bytes=64)
        nc.vector.memset(tab_scale_rows[:].bitcast(I32), 0)
        v_s = [keep.tile([P, PASSES * HALF], U8, name="v_s%d" % hf, align_bytes=64) for hf in range(2)]
        w2_s = keep.tile([P, PASSES * H], U8, name="w2_s", align_bytes=64)
        w2_scale_rows = keep.tile([P, PASSES * H], U8, name="w2_scale_rows", align_bytes=64)
        nc.vector.memset(w2_scale_rows[:].bitcast(I32), 0)
        identity = keep.tile([P, P], F32, name="identity", align_bytes=64)
        nc.vector.memset(identity[:], 0.0)
        make_identity(nc, identity[:], nomemset=True)
        for hf in range(2):
            nc.vector.memset(v_s[hf][:].bitcast(I32), 0)
        zeros = keep.tile([P, P], U32, name="zeros", align_bytes=64)
        nc.vector.memset(zeros[:], 0)
        idle_g = keep.tile([P, 4 * P], BF16, name="idle_g", align_bytes=64)
        nc.vector.memset(idle_g[:].bitcast(I32), 0)
        idle_c = keep.tile([P, P], U32, name="idle_c", align_bytes=64)
        idle_s = keep.tile([P, P], U8, name="idle_s", align_bytes=64)
        nc.vector.memset(idle_s[:].bitcast(I32), 0)
        nc.vector.quantize_mx(idle_c[:].bitcast(FP8X4), idle_s[:], idle_g[:])

        w2_raw = keep.tile([P, PASSES, H // 2], I32, name="w2_raw", align_bytes=64)
        nc.sync.dma_start(w2_raw[:], w2_words.bitcast(I32).rearrange("a p c -> p a c"))
        nc.sync.dma_start(tab_scale_rows[0:P:4, :].bitcast(I32), tab_scales.bitcast(I32).rearrange("a q c -> q a c"))
        tab = [keep.tile([P, T], I32, name="tab%d" % a, align_bytes=64) for a in range(PASSES)]

        def load_table(a):
            nc.sync.dma_start(tab[a][:], tab_words[a].rearrange("p t i -> p (t i)").bitcast(I32))

        load_table(0)
        for s in range(4):
            nc.sync.dma_start(
                w2_scale_rows[s:P:32, :].bitcast(I32).rearrange("p (a c) -> p a c", a=PASSES),
                w2_scales.bitcast(I32)[:, s:16:4, :].rearrange("a d c -> d a c"))
        load_table(1)

        w2_first = reuse.tile([P, P], I32, name="w2_first", offset=W2A_AT, align_bytes=64)
        w2_rest = keep.tile([P, 3 * P], I32, name="w2_rest", align_bytes=64)
        for ordered, t0, t1 in ((w2_first, 0, 1), (w2_rest, 1, TILES)):
            nc.scalar.copy(
                ordered[:].bitcast(U32).rearrange("p (t a b e) -> p t a b e", a=PASSES, t=t1 - t0, e=4),
                w2_raw[:].bitcast(U32).rearrange("p a (b t e) -> p t a b e", t=TILES, e=4)[:, t0:t1])

        def w2_words_of(a, t):
            w = (2 * max(t - 1, 0) + a) * P // 2
            return (w2_rest if t else w2_first)[:, w:w + P // 2].bitcast(FP4X4)
        nc.scalar.copy(
            w2_s[:].bitcast(U32).rearrange("p (a t b e) -> p a t b e", a=PASSES, t=TILES, e=2),
            w2_scale_rows[:].bitcast(U32).rearrange("p (a b t e) -> p a t b e", a=PASSES, t=TILES, e=2))

        picked = [reuse.tile([P, W3_AT - PICKED0_AT], U8, name="picked0", offset=PICKED0_AT, align_bytes=64),
                  reuse.tile([P, HALF], U8, name="picked1", offset=PICKED_AT, align_bytes=64)]
        for hf in range(2):
            nc.vector.tensor_copy(picked[hf][:, 0:HALF], tab_scale_rows[:].indirect(offsets[:, 32 * hf:32 * (hf + 1)]))

        w1_raw = [reuse.tile([P, 4 * H], F32, name="w1_raw%d" % a, offset=at, align_bytes=64)
                  for a, at in enumerate((W1A_AT, W1B_AT))]
        for i in range(2):
            for d in (0, 2, 1, 3):
                nc.sync.dma_start(
                    v_s[i][32 * d:32 * d + 4, :].bitcast(I32).rearrange("p (a c) -> p a c", a=PASSES),
                    picked[i][32 * d:32 * d + 32:4, 0:HALF].bitcast(I32))
            nc.sync.dma_start(w1_raw[i][:], w1[512 * i:512 * (i + 1), :].rearrange("(p i) c -> p (i c)", i=4))

        idle_planes = [keep.tile([P, HALF], U8, name="idle_plane0", align_bytes=64),
                       reuse.tile([P, HALF], U8, name="idle_plane1", offset=IDLE_AT, align_bytes=64)]
        for plane, count in zip(idle_planes, WARM):
            nc.scalar.copy(plane[:].bitcast(U32).rearrange("p (r c) -> p r c", r=4),
                           idle_s[:].bitcast(U32).unsqueeze(1).broadcast_to([P, 4, P // 4]))
            for i in range(count):
                nc.tensor.matmul_mx(banks[6][:], lhsT=idle_c[:].bitcast(FP8X4), lhsT_scale=idle_s[:],
                                    rhs=w2_rest[:, 0:HALF // 2].bitcast(FP4X4), rhs_scale=plane[:], start=True, stop=True)
        lam_rows = reuse.tile([P, P], F32, name="lam_rows", offset=LAMROWS_AT, align_bytes=64)
        nc.scalar.copy(lam_rows[:], zeros[:].bitcast(F32))
        nc.sync.dma_start(lam_rows[0:TILES, :].rearrange("t (b j) -> t b j", j=8),
                          lam.rearrange("(b t j) -> t b j", t=TILES, j=8))
        w3_scale_rows = reuse.tile([P, H], U8, name="w3_scale_rows", offset=W3ROWS_AT, align_bytes=64)
        nc.scalar.copy(w3_scale_rows[:].bitcast(U32), zeros[:])
        for d in range(4):
            nc.sync.dma_start(w3_scale_rows[32 * d + 8:32 * d + 16, :].bitcast(I32),
                              w3_scales.bitcast(I32)[:, 4 * d:4 * d + 4, :])
        w3_raw = reuse.tile([P, PASSES, H], I32, name="w3_raw", offset=W3_AT, align_bytes=64)
        nc.sync.dma_start(
            w3_raw[:], w3_words.rearrange("a p c i -> a p (c i)").bitcast(I32).rearrange("a p c -> p a c"))
        bo_t = reuse.tile([P, 3], F32, name="bo_t", offset=BO_AT)
        w4_raw = reuse.tile([P, TILES * N], F32, name="w4_raw", offset=W4_AT, align_bytes=64)
        with nc.allow_non_contiguous_dma(reason="one value a partition"):
            for t in range(TILES):
                nc.sync.dma_start(w4_raw[:, t * N:(t + 1) * N], w4.rearrange("(b t j) n -> t b j n", t=TILES, j=8)[t])
            nc.sync.dma_start(bo_t[:], bo.rearrange("(m p) -> p m", p=P))

        v_c = {}
        for a in range(PASSES):
            for hf in range(2):
                v_c[a, hf] = keep.tile([P, HALF], U32, name="v%d_%d" % (a, hf), align_bytes=64)
                step = QUART if (a, hf) == (1, 0) else HALF
                for c in range(0, HALF, step):
                    j = (hf * HALF + c) // 16
                    nc.vector.tensor_copy(
                        v_c[a, hf][:, c:c + step], tab[a][:].bitcast(U32).indirect(offsets[:, j:j + step // 16]))

        def one_pass(acc, codes, scales, a, c0, n, opens=True, closes=True):
            hf, ch = c0 // HALF, c0 % HALF
            nc.tensor.matmul_mx(
                acc, lhsT=codes, lhsT_scale=scales, rhs=v_c[a, hf][:, ch:ch + n].bitcast(FP8X4),
                rhs_scale=v_s[hf][:, a * HALF + ch:a * HALF + ch + n],
                start=(a == 0 and opens), stop=(a == PASSES - 1 and closes))

        early = reuse.tile([P, TILES, HALF], F32, name="early", offset=EARLY_AT, align_bytes=64)
        late = keep.tile([P, TILES, HALF], F32, name="late", align_bytes=64)

        def infer_rows(hf, pair):
            return (early, late)[hf][:, 2 * pair:2 * pair + 2, :]

        def infer_passes(hf, tiles, first_bank):
            for a in range(PASSES):
                for i, t in enumerate(tiles):
                    c = a * H + t * P
                    one_pass(banks[first_bank + i][:], w2_words_of(a, t), w2_s[:, c:c + P], a, hf * HALF, HALF)

        def infer_copy(hf, t, bank):
            nc.scalar.copy(infer_rows(hf, t // 2)[:, t % 2, :], banks[bank][:])

        for a in range(PASSES):
            for qt in range(2):
                for t in range(TILES):
                    c = a * H + t * P
                    one_pass(banks[2 * qt + t // 2][:, (t % 2) * QUART:(t % 2 + 1) * QUART], w2_words_of(a, t),
                             w2_s[:, c:c + P], a, qt * QUART, QUART, opens=(t % 2 == 0), closes=(t % 2 == 1))
        for qt in range(2):
            for pair in range(2):
                nc.scalar.copy(early[:, 2 * pair:2 * pair + 2, qt * QUART:(qt + 1) * QUART],
                               banks[2 * qt + pair][:].rearrange("p (t c) -> p t c", t=2))
        infer_passes(1, (0, 1), 4)
        for t in range(2):
            infer_copy(1, t, 4 + t)

        w1_c = keep.tile([P, PASSES * H], U32, name="w1_c", align_bytes=64)
        w1_s = [reuse.tile([P, H], U8, name="w1_s0", offset=W2A_AT, align_bytes=64),
                keep.tile([P, H], U8, name="w1_s1", align_bytes=64)]
        w1_g = [keep.tile([P, 4 * H], BF16, name="w1_g%d" % a, align_bytes=64) for a in range(PASSES)]

        def round_w1(a, t, copy=nc.vector.tensor_copy):
            copy(
                w1_g[a][:, t * H:(t + 1) * H].rearrange("p (b u e i) -> p b u i e", u=2, e=4, i=4),
                w1_raw[a][:].rearrange("p (i b t u e) -> p t b u i e", i=4, t=TILES, u=2, e=4)[:, t])

        def quantise_w1(a, t0, count):
            c, n = a * H + t0 * P, count * P
            nc.vector.quantize_mx(w1_c[:, c:c + n].bitcast(FP8X4), w1_s[a][:, t0 * P:t0 * P + n],
                                  w1_g[a][:, t0 * H:(t0 + count) * H])

        def goal_pass(a, t, qt, pair_banks):
            c = a * H + t * P
            one_pass(banks[pair_banks[t // 2]][:, (t % 2) * QUART:(t % 2 + 1) * QUART],
                     w1_c[:, c:c + P].bitcast(FP8X4), w1_s[a][:, t * P:(t + 1) * P], a, qt * QUART, QUART,
                     opens=(t % 2 == 0), closes=(t % 2 == 1))

        best = [keep.tile([P, TILES, HALF], F32, name="best0", align_bytes=64),
                keep.tile([P, TILES, HALF], F32, name="best1", align_bytes=64)]
        w3_c = keep.tile([P, PASSES * H], I32, name="w3_c", align_bytes=64)
        w3_s = keep.tile([P, H], U8, name="w3_s", align_bytes=64)
        weighted = [reuse.tile([P, TILES, QUART], F32, name="weighted0", offset=WEIGHTED0_AT, align_bytes=64)]
        weighted += [keep.tile([P, TILES, QUART], F32, name="weighted%d" % qt, align_bytes=64) for qt in range(1, 4)]
        w4_g = [reuse.tile([P, TILES * 2 * P], BF16, name="w4_g0", offset=EARLY_AT, align_bytes=64),
                reuse.tile([P, TILES * P], BF16, name="w4_g1", offset=WEIGHTED0_AT + 1024, align_bytes=64)]
        w4_c = keep.tile([P, N], U32, name="w4_c", align_bytes=64)
        w4_s = keep.tile([P, N], U8, name="w4_s", align_bytes=64)
        h_g = keep.tile([P, TILES * S], BF16, name="h_g", align_bytes=64)
        h_c = keep.tile([P, S], U32, name="h_c", align_bytes=64)
        h_s = keep.tile([P, S], U8, name="h_s", align_bytes=64)

        def order_w3_words(pair):
            nc.scalar.copy(
                w3_c[:].bitcast(U32).rearrange("p (a t b j) -> p a t b j", a=PASSES, t=TILES, j=8)[:, :, 2 * pair:2 * pair + 2],
                w3_raw[:].bitcast(U32).rearrange("p a (b t j) -> p a t b j", t=TILES, j=8)[:, :, 2 * pair:2 * pair + 2])

        def order_w3_scales():
            nc.scalar.copy(
                w3_s[:].bitcast(U32).rearrange("p (t b e) -> p t b e", t=TILES, e=2),
                w3_scale_rows[:].bitcast(U32).rearrange("p (b t e) -> p t b e", t=TILES, e=2))

        def goal_quarter(qt, pair_banks):
            for pair in range(2):
                for a in range(PASSES):
                    for t in (2 * pair, 2 * pair + 1):
                        goal_pass(a, t, qt, pair_banks)

        def maximum(qt, pair, bank):
            hf, ch = qt // 2, (qt % 2) * QUART
            nc.vector.tensor_tensor(
                best[hf][:, 2 * pair:2 * pair + 2, ch:ch + QUART], banks[bank][:].rearrange("p (t c) -> p t c", t=2),
                infer_rows(hf, pair)[:, :, ch:ch + QUART], ALU.max)

        def maximum_quarter(qt, pair_banks):
            for pair in range(2):
                maximum(qt, pair, pair_banks[pair])

        def length(qt, pair_banks):
            for pair in range(2):
                tiles = (2 * pair, 2 * pair + 1)
                accs = {t: banks[pair_banks[pair]][:, (t % 2) * QUART:(t % 2 + 1) * QUART] for t in tiles}
                for t in tiles:
                    for a in range(PASSES):
                        c = a * H + t * P
                        one_pass(accs[t], w3_c[:, c:c + P].bitcast(FP8X4), w3_s[8 + 4 * a:P, t * P:(t + 1) * P],
                                 a, qt * QUART, QUART)
                for t in tiles:
                    nc.scalar.activation(weighted[qt][:, t, :], accs[t], ACT.Copy, scale=lam_t[:, t:t + 1])

        def eighth_passes(codes, scales, c0, bank):
            for a in range(PASSES):
                for t in range(TILES):
                    c = a * H + t * P
                    one_pass(banks[bank][:, t * P:(t + 1) * P], codes[:, c:c + P].bitcast(FP8X4), scales(a, t),
                             a, c0, P, opens=(t == 0), closes=(t == TILES - 1))

        def goal_eighth(c0, bank):
            eighth_passes(w1_c, lambda a, t: w1_s[a][:, t * P:(t + 1) * P], c0, bank)

        def length_eighth(c0, bank):
            eighth_passes(w3_c, lambda a, t: w3_s[8 + 4 * a:P, t * P:(t + 1) * P], c0, bank)
            cq = c0 % QUART
            for t in range(TILES):
                nc.scalar.activation(weighted[3][:, t, cq:cq + P], banks[bank][:, t * P:(t + 1) * P], ACT.Copy,
                                     scale=lam_t[:, t:t + 1])

        def maximum_eighth(c0, bank):
            ch = c0 % HALF
            nc.vector.tensor_tensor(
                best[1][:, :, ch:ch + P], banks[bank][:].rearrange("p (t c) -> p t c", t=TILES),
                late[:, :, ch:ch + P], ALU.max)

        w4_cols = ((0, 2 * P), (2 * P, N))

        def round_w4(part, copy):
            c0, c1 = w4_cols[part]
            copy(w4_g[part][:].rearrange("p (c e t) -> p c t e", e=4, t=TILES),
                 w4_raw[:].rearrange("p (t c e) -> p c t e", e=4, t=TILES)[:, c0 // 4:c1 // 4])

        def quantise_w4(part):
            c0, c1 = w4_cols[part]
            nc.vector.quantize_mx(w4_c[:, c0:c1].bitcast(FP8X4), w4_s[:, c0:c1], w4_g[part][:])

        def penalise(c0, n):
            hf, ch, qt, cq = c0 // HALF, c0 % HALF, c0 // QUART, c0 % QUART
            nc.vector.tensor_tensor(
                h_g[:, 4 * c0:4 * (c0 + n)].rearrange("p (c e t) -> p c t e", e=4, t=TILES),
                best[hf][:, :, ch:ch + n].rearrange("p t (c e) -> p c t e", e=4),
                weighted[qt][:, :, cq:cq + n].rearrange("p t (c e) -> p c t e", e=4), ALU.subtract)

        def quantise_h(c0, n):
            nc.vector.quantize_mx(h_c[:, c0:c0 + n].bitcast(FP8X4), h_s[:, c0:c0 + n], h_g[:, 4 * c0:4 * (c0 + n)])

        out_rows = out.rearrange("(m p) j -> p m j", p=P)

        def score_product(acc, m, c0, n):
            nc.tensor.matmul_mx(
                acc, lhsT=w4_c[:, m * P:(m + 1) * P].bitcast(FP8X4), lhsT_scale=w4_s[:, m * P:(m + 1) * P],
                rhs=h_c[:, c0:c0 + n].bitcast(FP8X4), rhs_scale=h_s[:, c0:c0 + n], start=True, stop=True)

        def score_products(c0, n, score_banks):
            per_bank = HALF // n
            accs = [banks[score_banks[m // per_bank]][:, (m % per_bank) * n:(m % per_bank + 1) * n] for m in range(3)]
            for m in range(3):
                score_product(accs[m], m, c0, n)
            return accs

        def scores(c0, n, score_banks):
            res = keep.tile([P, 3, n], F32, name="res%d" % c0, align_bytes=64)
            accs = score_products(c0, n, score_banks)
            for m in range(3):
                nc.scalar.activation(res[:, m, :], accs[m], ACT.Identity, bias=bo_t[:, m:m + 1])
                if c0 >= HALF:
                    nc.sync.dma_start(out_rows[:, m, c0:c0 + n], res[:, m, :])
            if c0 < HALF:
                nc.sync.dma_start(out_rows[:, :, c0:c0 + n], res[:])

        def last_scores(c0, pair_bank, single_bank):
            pair = keep.tile([P, 2, P], F32, name="last_pair", align_bytes=64)
            single = keep.tile([P, P], F32, name="last_single", align_bytes=64)
            for m in range(2):
                score_product(banks[pair_bank][:, m * P:(m + 1) * P], m, c0, P)
            score_product(banks[single_bank][:, 0:P], 2, c0, P)
            nc.vector.tensor_tensor(
                pair[:], banks[pair_bank][:, 0:2 * P].rearrange("p (m c) -> p m c", m=2),
                bo_t[:, 0:2].unsqueeze(2).broadcast_to([P, 2, P]), ALU.add)
            nc.scalar.activation(single[:], banks[single_bank][:, 0:P], ACT.Identity, bias=bo_t[:, 2:3])
            nc.sync.dma_start(out_rows[:, 2, c0:c0 + P], single[:])
            nc.sync.dma_start(out_rows[:, 0:2, c0:c0 + P], pair[:])

        first_goal = ((6, 7), (0, 1))
        for t in range(TILES):
            round_w1(0, t)
        quantise_w1(0, 0, 2)
        quantise_w1(0, 2, 2)
        for qt in range(2):
            for t in range(TILES):
                goal_pass(0, t, qt, first_goal[qt])
        nc.tensor.transpose(banks[3][:, 0:P], lam_rows[:], identity[:])
        lam_t = keep.tile([P, TILES], F32, name="lam_t")
        nc.scalar.copy(lam_t[:], banks[3][:, 0:TILES])
        round_w1(1, 3, nc.scalar.copy)
        round_w1(1, 0)
        for t in range(1, 3):
            round_w1(1, t)
            quantise_w1(1, t - 1, 1)
        quantise_w1(1, 2, 1)
        order_w3_words(0)
        order_w3_scales()
        order_w3_words(1)
        for qt in range(2):
            for t in (0, 1):
                goal_pass(1, t, qt, first_goal[qt])
        maximum(0, 0, first_goal[0][0])
        quantise_w1(1, 3, 1)
        for qt in range(2):
            for t in (2, 3):
                goal_pass(1, t, qt, first_goal[qt])
        maximum(1, 0, first_goal[1][0])
        for qt in range(2):
            maximum(qt, 1, first_goal[qt][1])
        round_w4(0, nc.vector.tensor_copy)
        length(0, (3, 4))
        length(1, (5, 6))
        infer_passes(1, (2, 3), 3)
        penalise(0, QUART)
        quantise_w4(0)
        round_w4(1, nc.scalar.copy)
        infer_copy(1, 2, 3)
        infer_copy(1, 3, 4)
        penalise(QUART, QUART)
        goal_quarter(2, (5, 6))
        length(2, (0, 1))
        quantise_h(0, QUART)
        quantise_w4(1)
        scores(0, QUART, (7, 2))
        goal_eighth(3 * QUART, 3)
        maximum_quarter(2, (5, 6))
        quantise_h(QUART, QUART)
        length_eighth(3 * QUART, 5)
        scores(QUART, QUART, (0, 1))
        length_eighth(3 * QUART + P, 6)
        goal_eighth(3 * QUART + P, 5)
        penalise(2 * QUART, QUART)
        maximum_eighth(3 * QUART, 3)
        quantise_h(2 * QUART, QUART)
        scores(2 * QUART, QUART, (7, 2))
        penalise(3 * QUART, P)
        maximum_eighth(3 * QUART + P, 5)
        quantise_h(3 * QUART, P)
        scores(3 * QUART, P, (3,))
        penalise(3 * QUART + P, P)
        quantise_h(3 * QUART + P, P)
        last_scores(3 * QUART + P, 4, 0)
